import numpy as np, ml_dtypes
CORES = [40,64,80,88,96,104,120,144]
N = 8
import mx_ref
BF = ml_dtypes.bfloat16
def gentries(a):
    return np.ascontiguousarray(a.reshape(8, 16, -1).transpose(0, 2, 1)).reshape(8, -1)
def gtable(e):
    e = np.asarray(e); return np.ascontiguousarray(e.reshape(8, -1, 16).transpose(0, 2, 1)).reshape(128, -1).astype(np.int32)
def gcols(t, e):
    v = np.concatenate([t.reshape(8, 16, -1, 4), np.zeros((8, 16, 1, 4), BF)], axis=2)
    return np.ascontiguousarray(np.stack([v[g][:, e[g]] for g in range(8)])).reshape(128, -1)
def gpick(z, e):
    return np.concatenate([z[16 * g:16 * g + 16][:, e[g]] for g in range(8)])
def tile(rs):
    return np.stack(rs, axis=2).reshape(128, -1).astype(BF)
def pick(q, e):
    c = np.concatenate([q[0].reshape(128, -1, 4), np.zeros((128, 1, 4), np.uint8)], axis=1); s = np.concatenate([q[1], np.ones((16, 1), np.uint8)], axis=1)
    return (np.ascontiguousarray(c[:, e].reshape(128, -1)), np.ascontiguousarray(s[:, e]))
def join(*qs):
    return (np.concatenate([q[0] for q in qs], axis=1), np.concatenate([q[1] for q in qs], axis=1))
def put(q, e, v):
    c, s = q[0].reshape(128, -1, 4).copy(), q[1].copy(); c[:, e] = v[0].reshape(128, -1, 4); s[:, e] = v[1]
    return (c.reshape(128, -1), s)
def pk(c, s):
    return (np.ascontiguousarray(c), mx_ref.live(s))
def emit(q):
    return q[0], q[1]
def packed(v, rng):
    q = [mx_ref.quantize(np.ascontiguousarray(v[r])) for r in range(N)]
    return np.stack([a for a, b in q]), np.stack([mx_ref.plane(b, rng) for a, b in q])
def values_of_codes():
    e, c = np.zeros((128, 128, 4), np.float32), np.zeros((128, 2, 4), np.uint8)
    e[np.arange(128), np.arange(128), 0] = 1
    c[:127, :, 0] = np.arange(256).reshape(2, 128).T[:127]
    return mx_ref.matmul(mx_ref.quantize(e.reshape(128, 512).astype(BF)), (c.reshape(128, 8), np.full((16, 2), 127, np.uint8))).T.reshape(-1).astype(np.float64)
CODE_VALUE, SCALE_VALUE = values_of_codes(), 2.0 ** (np.arange(256) - 127.0)
def decode(q):
    return (CODE_VALUE[q[0]].reshape(16, 8, -1, 4) * SCALE_VALUE[q[1]][:, None, :, None] + 0.0).reshape(128, -1).astype(np.float32)
def f(rng, *shape):
    return mx_ref.flush((rng.standard_normal(shape, dtype=np.float32) * np.exp2(rng.integers(-2, 3, shape[:-1] + (1,)))).astype(BF))
def wide(rng, *shape, cols=0):
    v = rng.standard_normal(shape, dtype=np.float32) * np.exp2(rng.integers(-12, 13, shape)).astype(np.float32)
    if cols: v *= np.repeat(np.exp2(rng.integers(-cols, cols + 1, shape[:-2] + (1, shape[-1] // 4))) * (rng.random(shape[:-2] + (1, shape[-1] // 4)) > 0.0625), 4, axis=-1).astype(np.float32)
    return mx_ref.flush(v.astype(BF))
C = 288
STEP = [4, 1, 2]
def numbers_of(rng):
    return {"x": np.array(f(rng, N, 128, 4 * C)), "u": np.array(f(rng, N, 128, 512)), "v": np.array(f(rng, N, 128, 512))}
def drawn(rng):
    e = np.tile(np.arange(C), (N, 8, 1))
    p, k, s, m = rng.permuted(e, axis=2), rng.permuted(e, axis=2), rng.permuted(e, axis=2), np.zeros_like(e)
    np.put_along_axis(m, s[:, :, ::2], s[:, :, 1::2], 2)
    np.put_along_axis(m, s[:, :, 1::2], s[:, :, ::2], 2)
    return p, k, m
def stored(p, k, m):
    return {"pg": np.stack([gtable(p[r]) for r in range(N)]), "kg": np.stack([gtable(k[r]) for r in range(N)]), "mg": np.stack([gtable(m[r]) for r in range(N)])}
def layers(rng):
    return np.array(f(rng, N, 128, 2048)).reshape(N, 8, 16, 4, 8, 16, 4)
def weights(rng, w):
    c, s = packed(np.ascontiguousarray(w).reshape(N, 128, 2048), rng)
    return {"wc": c, "ws": s}
def setup_inputs(rng):
    return {**numbers_of(rng), **stored(*drawn(rng)), **weights(rng, layers(rng))}
def setup_inputs_ties(rng):
    d = numbers_of(rng)
    o = rng.permutation(N)
    s = rng.integers(-1, 2, (N, 2, 8, C))
    s[o[0]] = 0
    s[o[1]] = 1
    s[o[2], 0] = np.where(np.arange(C) % 2 == 1, 1, rng.integers(-1, 1, (8, C)))
    x = d["x"].astype(np.float32).reshape(N, 8, 16, C, 4)
    u = d["u"].astype(np.float32).reshape(N, 128, 128, 4)
    for i in range(2):
        x[:, :, i] = 0
        x[:, :, i, :, 0] = s[:, i]
        u[:, :, i::16] = 0
        for h in range(0, 128, 16): u[:, h + i, h + i, 0] = 1
    p, k, m = drawn(rng)
    p[o[2]] = k[o[2]] = np.arange(C)
    m[o[2]] = np.arange(C) ^ 1
    w = layers(rng)
    w[:, :, :, :, :, :8] = 0
    return {"x": x.reshape(N, 128, 4 * C).astype(BF), "u": u.reshape(N, 128, 512).astype(BF), "v": d["v"], **stored(p, k, m), **weights(rng, w)}
def setup_inputs_near(rng):
    d = numbers_of(rng)
    o = rng.permutation(N)
    k = np.where(o % 2 == 0, 2.0 ** -30, 1.0)
    x = np.zeros((N, 8, 16, C, 4))
    s = rng.integers(-1, 2, (N, 2, 8, C)) * k[:, None, None, None]
    for i in range(2):
        x[:, :, 2 * i, :, 0] = 1.125 * s[:, i]
        x[:, :, 2 * i + 1, :, 0] = -1.25 * s[:, i]
    x[:, :, 9, :, 0] = rng.choice([-1.0, 1.0], (N, 8, C)) * 2.0 ** -17
    x[:, :, 10:] = rng.choice([-1.0, 1.0], (N, 8, 6, C, 4)) * (1 + 0.125 * rng.integers(0, 8, (N, 8, 6, C, 4))) * np.exp2(-12.0 - rng.integers(0, 4, (N, 8, 6, C, 4)))
    u = d["u"].astype(np.float32).reshape(N, 128, 128, 4)
    u[:, :, ::16] = 0
    u[:, :, 1::16] = 0
    w = layers(rng)
    w[:, :, :8] = 0
    w[:, :, :, :, :, :10] = 0
    for r in range(N):
        for g in rng.permutation(8)[:4]: x[r, g, 0, rng.integers(C), 0] = 2.0 ** 30 * rng.choice([-1.0, 1.0])
        if o[r] == 0:
            x[r, :, :8] = 0
            x[r, :, 0, :, 0] = 2.0 ** -30
        for g in range(8):
            h = 16 * g
            if o[r] == 0:
                u[r, h + 4, h, 0] = 2.0 ** -30
                u[r, h + 4, h + 1, 0] = -2.0 ** -30
                w[r, g, 8, 0, g, 4, 0] = 2.0 ** -8
                w[r, g, 9, 0, g, 4, 0] = 2.0 ** -22
            else:
                for i in range(2):
                    u[r, h + 2 * i, h + i, 0] = 1.125 * k[r]
                    u[r, h + 2 * i + 1, h + i, 0] = k[r]
    return {"x": x.astype(np.float32).reshape(N, 128, 4 * C).astype(BF), "u": u.reshape(N, 128, 512).astype(BF), "v": d["v"], **stored(*drawn(rng)), **weights(rng, w)}
def setup_inputs_odd(rng):
    d = numbers_of(rng)
    x = (1.0 + (2 * rng.integers(0, 64, (N, 16, 8, C, 4)) + 1) * 2.0 ** -7) * np.exp2(-rng.integers(0, 7, (N, 16, 8, C, 4)).astype(np.float64)) * rng.choice([-1.0, 1.0], (N, 16, 8, C, 4))
    x[:, ::2, 0, :, 0] = 1.96875 * 2.0 ** 8 * rng.choice([-1.0, 1.0], (8, 1))
    x[:, 1::2, 0, :, 0] = 1.96875 * 2.0 ** 8 * rng.choice([-1.0, 1.0], (N, 8, C))
    u = d["u"].astype(np.float32).reshape(N, 16, 8, 128, 4)
    u[:, :, 0, ::16] = 0
    u[:, :, :, 1::16] = 0
    h = rng.permutation(8) % 4
    for g in range(8):
        x[:, 2 * g, 1, :, 0] = (8 + rng.integers(0, 2, (N, C))) * 2.0 ** (int(h[g]) - 9)
        x[:, 2 * g, 2, :, 0] = -2.0 ** (int(h[g]) - 6)
        u[:, 2 * g, 1:3, 16 * g + 1, 0] = 1
    w = layers(rng)
    for i in (0, 8):
        w[:, :, i] = 0
        w[:, :, :, :, :, i] = 0
    w[:, :, :, 0, :, 1:3] = 0
    for g in range(8): w[:, g, 0, 0, g, 0, 0] = -0.5
    p, k, m = drawn(rng)
    t = int(rng.integers(N))
    p[t] = m[t] = np.arange(C)
    k[t] = rng.permutation(C)
    return {"x": x.astype(np.float32).reshape(N, 128, 4 * C).astype(BF), "u": u.reshape(N, 128, 512).astype(BF), "v": d["v"], **stored(p, k, m), **weights(rng, w)}
def setup_inputs_ends(rng):
    d = numbers_of(rng)
    o, ep, ek, em = [rng.permutation(N) % 4 for i in range(4)]
    s = rng.choice([-1.0, 1.0], (N, 128, C, 4))
    s[o == 0] = -1
    s[o == 1] = rng.choice([-1.0, 1.0], (N, 1, C, 1))[o == 1]
    x = s * (0.90 + 0.02 * rng.random((N, 128, C, 4))) * 2.0 ** 30
    tiny = (1 + 0.125 * rng.integers(0, 8, (N, 128, C, 4))) * 2.0 ** -30
    x[o == 3] = (s * tiny)[o == 3]
    x[:, 8:16] = tiny[:, 8:16]
    u = d["u"].astype(np.float32).reshape(N, 128, 128, 4)
    for r in range(N):
        h = rng.permutation(8)
        size = 2.0 ** -30 if o[r] == 3 else 2.0 ** 30
        u[r, :, ::16] = ((h % 2 * 2 - 1) * size)[None, :, None]
        u[r, :, 1::16] = ((h // 2 % 2 * 2 - 1) * size)[None, :, None]
    v = rng.choice([-1.0, 1.0], (N, 128, 512)) * np.where(o % 2 == 0, 2.0 ** 30, 2.0 ** -30)[:, None, None]
    p, k, m = drawn(rng)
    line = np.arange(C)
    p[ep == 0] = line
    p[ep == 1] = (line + 1) % C
    p[ep == 2] = C - 1 - line
    k[ek == 0] = line
    k[ek == 1] = C - 1 - line
    k[ek == 2] = (line + C - 1) % C
    m[em == 0] = line
    m[em == 1] = C - 1 - line
    m[em == 2] = line ^ 1
    w = np.zeros((N, 128, 4, 128, 4), np.float32)
    i = np.arange(128)
    for b in range(4): w[:, i, b, i, b] = np.where((i >= 8) & (i < 16), np.where(o == 3, 2.0 ** 8, 2.0 ** -8)[:, None], -0.25)
    return {"x": x.astype(np.float32).reshape(N, 128, 4 * C).astype(BF), "u": u.reshape(N, 128, 512).astype(BF), "v": v.astype(np.float32).astype(BF), **stored(p, k, m), **weights(rng, w.astype(BF))}
def setup_inputs_spread(rng):
    d = setup_inputs(rng)
    d["x"] = wide(rng, N, 128, 4 * C, cols=6)
    return d
def check_inputs(d):
    b = []
    for k in ("x", "u", "v"):
        a = np.abs(d[k].astype(np.float32))
        if not (np.isfinite(a).all() and ((a == 0) | (a >= 2.0 ** -30) & (a <= 2.0 ** 30)).all()): b.append("a value of " + k)
    none, least, most = [emit(mx_ref.quantize(np.full((128, 16), k, np.float32).astype(BF)))[1][0, 0] for k in (0.0, 2.0 ** -8, 2.0 ** 8)]
    top = emit(mx_ref.quantize(np.full((128, 16), 1.9921875, np.float32).astype(BF)))[0][0, 0] & 0x7F
    line = np.arange(C)
    for r in range(N):
        for k in ("pg", "kg"):
            if not (np.sort(gentries(d[k][r]), axis=1) == line).all(): b.append(k + ": no permutation")
        m = gentries(d["mg"][r])
        if not ((m >= 0) & (m < C)).all(): b.append("an entry of mg")
        elif not (np.take_along_axis(m, m, 1) == line).all(): b.append("mg: a mate's mate")
        if ((d["wc"][r] == 0x7F) | (d["wc"][r] == 0xFF)).any(): b.append("wc: a code that is no number")
        if ((d["wc"][r] & 0x7F) > top).any(): b.append("wc: a code that quantize_mx does not give")
        s = mx_ref.live(d["ws"][r])
        if ((s != none) & ((s < least) | (s > most))).any(): b.append("ws: a scale out of range")
    return b
def reference(x, u, v, pg, kg, mg, wc, ws):
    qu = [mx_ref.quantize(u[r]) for r in range(N)]
    lay = [pk(wc[r], ws[r]) for r in range(N)]
    p, k, m = [[gentries(a[r]).astype(np.int64) for r in range(N)] for a in (pg, kg, mg)]
    now = [x[r] for r in range(N)]
    for step in STEP:
        own, land, mosaic = [], [], []
        for r in range(N):
            q = mx_ref.quantize(now[r])
            s = mx_ref.matmul(qu[r], q)
            first = (s[::16] > 0).astype(np.int64)
            e = first + 2 * (s[1::16] > 0).astype(np.int64)
            at = np.zeros((8, C), np.int64)
            for g in range(8):
                power = np.ones(C, np.int64) if g == 0 else e[g - 1][at[g - 1]]
                a = k[r][g]
                for i in range(3): a = np.where(i < power, p[r][g][a], a)
                at[g] = a
            bit = np.take_along_axis(first, at, 1)
            p[r] = np.where(bit != np.take_along_axis(bit, m[r], 1), np.take_along_axis(p[r], m[r], 1), p[r])
            land.append(at)
            own.append(decode(q))
            mosaic.append(mx_ref.quantize(gcols(own[r].astype(BF), at)))
        made = []
        for r in range(N):
            h = [mx_ref.matmul(pick(lay[r], np.arange(128 * b, 128 * b + 128)), mosaic[r ^ step]) * np.float32(0.03125) for b in range(4)]
            made.append(tile([own[r][:, b::4] + gpick(h[b], land[r]) for b in range(4)]))
        now = made
    y, pl = np.zeros((N, 128, C), np.float32), np.zeros((N, 8, 2 * C), np.float32)
    oc, osc = np.zeros((N, 128, 4 * C), np.uint8), np.zeros((N, 16, C), np.uint8)
    for r in range(N):
        q = mx_ref.quantize(now[r])
        y[r] = mx_ref.matmul(mx_ref.quantize(v[r]), q)
        pl[r] = np.concatenate([land[r], p[r]], axis=1)
        oc[r], osc[r] = emit(q)
    return {"y": y, "pl": pl, "oc": oc, "osc": osc}

@@ -1,0 +1,501 @@
+from concourse.bass import DstId, RemoteDMATransfer
+from concourse.mybir import dt, AluOpType, ActivationFunctionType
+
+N = 8
+C = 288
+STEP = [4, 1, 2]
+HALF = C // 2
+ENT = 10
+BLK = 4 * ENT
+BIAS = 144.0
+
+SCRATCH = {
+    "zt": ("sbuf", [128, 4 * C], "bfloat16"), "zq": ("sbuf", [128, C], "float8_e4m3fn_x4"), "zp": ("sbuf", [128, C], "uint8"),
+    "xt": ("sbuf", [128, 4 * C], "bfloat16"), "ut": ("sbuf", [128, 512], "bfloat16"), "vt": ("sbuf", [128, 512], "bfloat16"),
+    "pI": ("sbuf", [128, 18], "int32"), "kI": ("sbuf", [128, 18], "int32"), "mI": ("sbuf", [128, 18], "int32"),
+    "wq": ("sbuf", [128, 512], "float8_e4m3fn_x4"), "wp": ("sbuf", [128, 512], "uint8"),
+    "uq": ("sbuf", [128, 128], "float8_e4m3fn_x4"), "up": ("sbuf", [128, 128], "uint8"),
+    "u3q": ("sbuf", [128, 384], "float8_e4m3fn_x4"), "u3p": ("sbuf", [128, 384], "uint8"),
+    "vq": ("sbuf", [128, 128], "float8_e4m3fn_x4"), "vp": ("sbuf", [128, 128], "uint8"),
+    "ones": ("sbuf", [128, 516], "bfloat16"), "e0": ("sbuf", [128, 516], "bfloat16"),
+    "eq": ("sbuf", [128, 512], "float8_e4m3fn_x4"), "ep": ("sbuf", [128, 512], "uint8"),
+    "ior": ("sbuf", [128, C], "bfloat16"), "idr": ("sbuf", [128, C], "bfloat16"),
+    "pid": ("sbuf", [128, 8], "int32"), "cst": ("sbuf", [128, 32], "float32"),
+    "ulf": ("sbuf", [128, 24], "float32"), "ull": ("sbuf", [128, 24], "uint16"),
+    "m42": ("sbuf", [128, 42], "float32"), "cg": ("sbuf", [128, BLK], "bfloat16"),
+    "pls": ("sbuf", [128, 18], "uint16"), "mls": ("sbuf", [128, 18], "uint16"), "k20": ("sbuf", [128, 20], "uint16"),
+    "kf": ("sbuf", [128, 18], "float32"), "ke": ("sbuf", [128, 20], "float32"), "ko": ("sbuf", [128, 20], "float32"),
+    "tl1": ("sbuf", [128, 20], "uint16"), "tl2": ("sbuf", [128, 20], "uint16"),
+    "xm": ("sbuf", [128, 42], "float32"), "lf": ("sbuf", [128, 20], "float32"),
+    "cP": ("sbuf", [128, 42], "float32"), "cQ": ("sbuf", [128, 42], "float32"), "cR": ("sbuf", [128, 42], "float32"), "cU": ("sbuf", [128, 42], "float32"),
+    "tab": ("sbuf", [128, 8 * BLK], "float32"), "tb6": ("sbuf", [128, 48], "float32"), "tb7": ("sbuf", [128, 48], "float32"), "tf": ("sbuf", [128, 88], "float32"),
+    "w1": ("sbuf", [128, C], "bfloat16"), "w2": ("sbuf", [128, C], "bfloat16"), "wg": ("sbuf", [128, C], "bfloat16"),
+    "s5": ("sbuf", [128, BLK], "float32"), "s5b": ("sbuf", [128, 48], "float32"), "s6": ("sbuf", [128, 88], "float32"),
+    "pm": ("sbuf", [128, 18], "float32"), "l32": ("sbuf", [128, 18], "float32"),
+    "be": ("sbuf", [128, C], "bfloat16"), "be2": ("sbuf", [128, C], "bfloat16"),
+    "ne2": ("sbuf", [128, 2 * C], "bfloat16"), "pd": ("sbuf", [128, 2 * C], "float32"),
+    "m2": ("sbuf", [128, 18], "uint16"), "k20p": ("sbuf", [128, 20], "uint16"),
+    "yo": ("sbuf", [128, C], "float32"), "lo": ("sbuf", [128, C], "float32"), "po": ("sbuf", [128, C], "float32"),
+}
+for _i in range(2):
+    SCRATCH["gg%d" % _i] = ("sbuf", [128, 208], "bfloat16")
+    SCRATCH["gt%d" % _i] = ("sbuf", [128, 352], "bfloat16")
+    SCRATCH["sc%d" % _i] = ("sbuf", [128, BLK], "float32")
+    SCRATCH["of%d" % _i] = ("sbuf", [128, ENT], "uint16")
+for _i in range(4):
+    SCRATCH["tr%d" % _i] = ("sbuf", [128, 368], "bfloat16")
+    SCRATCH["tt%d" % _i] = ("sbuf", [128, 672], "bfloat16")
+    SCRATCH["pr%d" % _i] = ("sbuf", [128, 2 * C], "bfloat16")
+    SCRATCH["q%d" % _i] = ("sbuf", [128, C], "float8_e4m3fn_x4")
+    SCRATCH["qp%d" % _i] = ("sbuf", [128, C], "uint8")
+    SCRATCH["fo%d" % _i] = ("sbuf", [128, C], "bfloat16")
+    SCRATCH["fp%d" % _i] = ("sbuf", [128, C], "bfloat16")
+    SCRATCH["hb%d" % _i] = ("sbuf", [128, C], "float32")
+for _i in range(8):
+    SCRATCH["ps%d" % _i] = ("psum", [128, 512], "float32")
+for _i in range(3):
+    SCRATCH["xn%d" % _i] = ("sbuf", [128, 4 * C], "bfloat16")
+    SCRATCH["aq%d" % _i] = ("sbuf", [128, C], "float8_e4m3fn_x4")
+    SCRATCH["ap%d" % _i] = ("sbuf", [128, C], "uint8")
+    SCRATCH["ll%d" % _i] = ("sbuf", [128, 18], "uint16")
+    SCRATCH["al%d" % _i] = ("sbuf", [128, 18], "uint16")
+
+SEMAPHORES = ["sv", "sa", "st", "sg", "left",
+              "lx", "lu", "lv", "lp", "lk", "lm", "lw", "lws", "out"]
+for _i in range(3):
+    SEMAPHORES += ["rc%d" % _i, "rs%d" % _i, "rL%d" % _i, "aq_%d" % _i, "aL_%d" % _i, "dt%d" % _i]
+
+
+def relays(core, partner, topo):
+    may = [c for c in topo.cores_of(core) if c != core and topo.may_write(c, partner)]
+    same = [c for c in may if topo.die(c) == topo.die(core)]
+    other = [c for c in may if topo.die(c) != topo.die(core)]
+    return [same[0], other[0]], same[0]
+
+
+def bits(es):
+    return sum(1 << e for e in es)
+
+
+def relay_program(g, core, T, topo):
+    home = [c for c in topo.cores_of(core) if T.rank_of(c) is not None]
+    if not home:
+        return
+    home = home[0]
+    left = 0
+    for r in range(3):
+        partner = T.cores[T.rank_of(home) ^ STEP[r]]
+        data, lst = relays(home, partner, topo)
+        rid, pid = topo.addr(partner, core) if core in data or core == lst else (0, 0)
+        es = topo.engines(core, partner)
+        if core in data:
+            k = data.index(core)
+            n_in = len(topo.engines(home, core)) // 2
+            a, b = k * HALF, (k + 1) * HALF
+            g.wait_ge(T.sem["rc%d" % r], n_in)
+            g.remote_dma(T["aq%d" % r][:, a:b].bitcast(dt.uint8), T["aq%d" % r][:, a:b].bitcast(dt.uint8), T.sem["aq_%d" % r], T.sem.left, pid, rid, bits(es))
+            g.wait_ge(T.sem["rs%d" % r], n_in)
+            g.remote_dma(T["ap%d" % r][:, a:b], T["ap%d" % r][:, a:b], T.sem["aq_%d" % r], T.sem.left, pid, rid, bits(es))
+            left += 2 * len(es)
+        if core == lst:
+            g.wait_ge(T.sem["rL%d" % r], len(topo.engines(home, core)))
+            g.remote_dma(T["al%d" % r][:], T["al%d" % r][:], T.sem["aL_%d" % r], T.sem.left, pid, rid, bits(es))
+            left += len(es)
+    if left:
+        g.wait_ge(T.sem.left, left)
+
+
+def rank_program(g, core, T, topo):
+    rank = T.rank_of(core)
+    if rank is None:
+        return relay_program(g, core, T, topo)
+    A = AluOpType
+    F = ActivationFunctionType
+    queue = {"v": g.vector, "a": g.scalar, "t": g.tensor, "g": g, "s": g.sync}
+    own = {"v": "sv", "a": "sa", "t": "st", "g": "sg"}
+    known = {e: {} for e in queue}
+    count, snap, wr, rd = {}, {}, {}, {}
+
+    def need(e, deps):
+        deps = [d for d in set(deps) if known[e].get(d[0], 0) < d[1]]
+        deps.sort(key=lambda d: -sum(snap.get(d, {}).values()))
+        for d in deps:
+            if known[e].get(d[0], 0) >= d[1]:
+                continue
+            queue[e].wait_ge(T.sem[d[0]], d[1])
+            for s, n in list(snap.get(d, {}).items()) + [d]:
+                known[e][s] = max(known[e].get(s, 0), n)
+
+    def before(e, reads, writes):
+        deps = []
+        for k in reads:
+            deps += wr.get(k, [])
+        for k in writes:
+            deps += wr.get(k, []) + rd.get(k, [])
+        need(e, deps)
+
+    def after(reads, writes, d):
+        for k in reads:
+            rd[k] = [x for x in rd.get(k, []) if x[0] != d[0]] + [d]
+        for k in writes:
+            wr[k] = [d]
+            rd[k] = []
+
+    def op(e, reads, writes, call):
+        before(e, reads, writes)
+        s = own[e]
+        count[s] = count.get(s, 0) + 1
+        call().then_inc(T.sem[s], 1)
+        d = (s, count[s])
+        snap[d] = dict(known[e])
+        snap[d][s] = count[s]
+        after(reads, writes, d)
+
+    def dma(e, sem, total, reads, writes, out, in_):
+        before(e, reads, writes)
+        queue[e].dma_start(out, in_).then_inc(T.sem[sem], 16)
+        count[sem] = 16 * total
+        d = (sem, 16 * total)
+        m = snap.setdefault(d, {})
+        for s, n in known[e].items():
+            m[s] = max(m.get(s, 0), n)
+        for k in reads:
+            rd[k] = [x for x in rd.get(k, []) if x != d] + [d]
+        for k in writes:
+            wr[k] = [x for x in wr.get(k, []) if x == d] or [d]
+            rd[k] = []
+
+    def ts(reads, writes, out, in0, s1, op0, s2=None, op1=None):
+        if op1 is None:
+            op("v", reads, writes, lambda: g.vector.tensor_scalar(out, in0, s1, None, op0))
+        else:
+            op("v", reads, writes, lambda: g.vector.tensor_scalar(out, in0, s1, s2, op0, op1))
+
+    def tt(reads, writes, out, in0, in1, o):
+        op("v", reads, writes, lambda: g.vector.tensor_tensor(out, in0, in1, o))
+
+    def cp(reads, writes, out, in_):
+        op("v", reads, writes, lambda: g.vector.tensor_copy(out, in_))
+
+    def act(reads, writes, out, in_, f=F.Copy, **kw):
+        op("a", reads, writes, lambda: g.scalar.activation(out, in_, f, **kw))
+
+    def mm(reads, bank, lhs, lhsp, rhs, rhsp):
+        op("t", reads, ["ps%d" % bank], lambda: g.tensor.matmul_mx(T["ps%d" % bank][:, 0:C], lhs, lhsp, rhs, rhsp, True, True))
+
+    def quant(reads, writes, q, p, t):
+        op("v", reads, writes, lambda: g.vector.quantize_mx(q, p, t))
+
+    def fill(key, ap, c):
+        op("v", [], [key], lambda: g.vector.memset(ap, c))
+
+    dma("s", "lp", 1, [], ["pI"], T.pI[:], T.pg[:])
+    dma("a", "lk", 1, [], ["kI"], T.kI[:], T.kg[:])
+    dma("s", "lx", 1, [], ["xt"], T.xt[:], T.x[:])
+    dma("a", "lu", 1, [], ["ut"], T.ut[:], T.u[:])
+    dma("a", "lm", 1, [], ["mI"], T.mI[:], T.mg[:])
+    dma("s", "lw", 1, [], ["wq"], T.wq[:].bitcast(dt.uint8), T.wc[:])
+    dma("s", "lws", 1, [], ["wp"], T.wp[:], T.ws[:])
+    dma("a", "lv", 1, [], ["vt"], T.vt[:], T.v[:])
+
+    op("g", [], ["pid0"], lambda: g.iota(T.pid[:, 0:1], [[0, 1]], 0, 1))
+    op("g", [], ["ior"], lambda: g.iota(T.ior[:], [[1, C]], -144, 0, allow_small_or_imprecise_dtypes=True))
+    op("g", [], ["ulf"], lambda: g.iota(T.ulf[:, 0:16], [[64, 2], [32, 4], [0, 2]], -96, 0, allow_small_or_imprecise_dtypes=True))
+    op("g", [], ["ulf2"], lambda: g.iota(T.ulf[:, 16:24], [[16, 8]], 0, 0, allow_small_or_imprecise_dtypes=True))
+    fill("ones", T.ones[:], 1.0)
+    op("g", ["ones"], ["e0"], lambda: g.affine_select(T.e0[:], T.ones[:], [[1, 516]], A.is_equal, 0.0, -3, -4))
+    S, I = T.cst, T.pid
+    cc = lambda j: S[:, j:j + 1]
+
+    def plain(key, out, n, c):
+        act(["ones"], [key], out, T.ones[:, 0:n], scale=c)
+
+    fill("ke", T.ke[:], 0.0)
+    fill("ko", T.ko[:], 0.0)
+    plain("pr0", T.pr0[:, 0:2 * C:2], C, 0.0)
+    for i in (1, 2, 3, 0):
+        plain("tr%da" % i, T["tr%d" % i][:, 16:32], 16, 0.0)
+        plain("tr%db" % i, T["tr%d" % i][:, 352:368], 16, 0.0)
+    ts(["pid0"], ["pid1"], I[:, 1:2], I[:, 0:1], 3, A.bitwise_and)
+    ts(["pid0"], ["pid2"], I[:, 2:3], I[:, 0:1], 2, A.logical_shift_right, 3, A.bitwise_and)
+    ts(["pid0"], ["pid3"], I[:, 3:4], I[:, 0:1], 4, A.logical_shift_right, 1, A.bitwise_and)
+    ts(["pid0"], ["pid4"], I[:, 4:5], I[:, 0:1], 5, A.logical_shift_right)
+    ts(["pid3"], ["c3"], cc(3), I[:, 3:4], 0.0, A.is_equal)
+    cp(["pid3"], ["c4"], cc(4), I[:, 3:4])
+    ts(["ior"], ["idr"], T.idr[:], T.ior[:], 0.25, A.mult)
+    cp(["pid1"], ["c0"], cc(0), I[:, 1:2])
+    ts(["pid2"], ["c1"], cc(1), I[:, 2:3], 2.0, A.is_equal)
+    ts(["c0", "c1"], ["c7"], cc(7), cc(0), 16.0, A.mult, cc(1), A.add)
+    ts(["ulf", "c7"], ["ull"], T.ull[:, 0:16], T.ulf[:, 0:16], cc(7), A.add, 0.0, A.max)
+    cp(["ulf2"], ["ull2"], T.ull[:, 16:24], T.ulf[:, 16:24])
+
+    cp(["kI"], ["kf"], T.kf[:], T.kI[:])
+    cp(["pI"], ["pls"], T.pls[:], T.pI[:])
+    ts(["pI"], ["tl1"], T.tl1[:, 0:18], T.pI[:], 2.0, A.mult, 1.0, A.add)
+    cp(["idr", "pls", "pr0"], ["pr0"], T.pr0[:, 1:2 * C:2], T.idr[:].indirect(T.pls[:]))
+    for h in range(2):
+        for y in range(2):
+            c0 = 10 * (1 - h) + y
+            n = len(range(c0, 18 if h == 0 else 10, 2))
+            m0 = 2 * h + y
+            act(["kf", "c3", "ke"], ["ke%d" % m0], T.ke[:, m0:m0 + 4 * n - 3:4], T.kf[:, c0:c0 + 2 * n - 1:2], scale=cc(3))
+    act(["kf", "c4", "ko"], ["ko1"], T.ko[:, 1:20:2], T.kf[:, 0:10], scale=cc(4))
+    act(["kf", "c4", "ko"], ["ko0"], T.ko[:, 0:15:2], T.kf[:, 10:18], scale=cc(4))
+    tt(["ke0", "ke1", "ke2", "ke3", "ko0", "ko1"], ["ke"], T.ke[:], T.ke[:], T.ko[:], A.add)
+    ts(["ke"], ["k20"], T.k20[:], T.ke[:], 2.0, A.mult, 1.0, A.add)
+    cp(["ke"], ["k20p"], T.k20p[:], T.ke[:])
+    cp(["pr0", "tl1"], ["pr1"], T.pr1[:, 0:C], T.pr0[:].indirect(T.tl1[:, 0:18]))
+    act(["pr0", "k20"], ["tr1"], T.tr1[:, 32:352], T.pr0[:].indirect(T.k20[:]))
+    act(["pr1", "k20p"], ["tr2"], T.tr2[:, 32:352], T.pr1[:, 0:C].indirect(T.k20p[:]))
+    act(["idr", "k20p"], ["tr0"], T.tr0[:, 32:352], T.idr[:].indirect(T.k20p[:]))
+    plain("tab", T.tab[:], 8 * BLK, 0.0)
+    act(["c3", "ones"], ["m42"], T.m42[:, 0:42:2], T.ones[:, 0:21], scale=cc(3))
+    act(["c4", "ones"], ["m42b"], T.m42[:, 1:42:2], T.ones[:, 0:21], scale=cc(4))
+    act(["pr0"], ["pd1"], T.pd[:, 1:2 * C:2], T.pr0[:, 1:2 * C:2])
+    plain("cg0", T.cg[:, 0:BLK:4], ENT, 0.0)
+    plain("cg1", T.cg[:, 1:BLK:4], ENT, 1.0)
+    plain("cg2", T.cg[:, 2:BLK:4], ENT, -1.0)
+    plain("cg3", T.cg[:, 3:BLK:4], ENT, 1.0)
+    plain("c14", cc(14), 1, -1e-29)
+    plain("tb6", T.tb6[:], 48, 0.0)
+    plain("tb7", T.tb7[:], 48, 0.0)
+    for i in range(2):
+        plain("gg%da" % i, T["gg%d" % i][:, 16:32], 16, 0.0)
+        plain("gg%db" % i, T["gg%d" % i][:, 192:208], 16, 0.0)
+    plain("ne0", T.ne2[:, 0:2 * C:2], C, 0.0)
+
+    def turn(n):
+        k, t = "tr%d" % n, "tt%d" % n
+        op("v", [k], [t + "a"], lambda: g.vector.transpose(T[t][:, 0:320], T[k][:, 32:352]))
+        op("v", [k, k + "a", k + "b"], [t + "b"], lambda: g.vector.transpose(T[t][:, 320:672], T[k][:, 16:368]))
+
+    def ent(n):
+        return T["tt%d" % n][:, 0:672:16]
+
+    def aslist(n, name):
+        t = "tt%d" % n
+        tt([t + "a", t + "b", "m42", "m42b"], ["xm"], T.xm[:], ent(n), T.m42[:], A.mult)
+        tt(["xm"], ["lf"], T.lf[:], T.xm[:, 0:20], T.xm[:, 21:41], A.add)
+        ts(["lf"], [name], T[name][:], T.lf[:], 8.0, A.mult, 2 * BIAS + 1, A.add)
+
+    def rows(n, key, lst, e="v"):
+        (cp if e == "v" else act)([key, lst], ["tr%d" % n], T["tr%d" % n][:, 32:352], T[key][:].indirect(T[lst][:]))
+
+    COMB = [("cR", "cU", A.subtract), ("cP", "cQ", A.subtract), ("cR", "cU", A.add), ("cP", "cQ", A.add)]
+
+    def powers(r):
+        p = "pr%d" % r
+        rows(1, p, "k20")
+        turn(1)
+        aslist(1, "tl1")
+        rows(2, p, "tl1")
+        turn(2)
+        aslist(2, "tl2")
+        middle()
+
+    def middle():
+        ks = ["tt1a", "tt1b", "tt2a", "tt2b"]
+        tt(ks, ["cQ"], T.cQ[:], ent(1), ent(2), A.add)
+        tt(ks, ["cU"], T.cU[:], ent(1), ent(2), A.subtract)
+
+    def tables(r):
+        turn(3)
+        ks = ["tt0a", "tt0b", "tt3a", "tt3b"]
+        tt(ks, ["cP"], T.cP[:], ent(0), ent(3), A.add)
+        tt(ks, ["cR"], T.cR[:], ent(3), ent(0), A.subtract)
+        for h in range(2):
+            for k in range(4):
+                x, y, o = COMB[k]
+                c0 = 6 * BLK + BLK * h + k
+                tt([x, y], ["tab"] if h == k == 0 else ["tab%d" % (4 * h + k)], T.tab[:, c0:c0 + BLK - 3:4], T[x][:, h:20:2], T[y][:, h:20:2], o)
+        ks = ["tab"] + ["tab%d" % i for i in range(1, 8)]
+        for b in range(4):
+            for a in range(b):
+                c0 = 6 * BLK - 2 * BLK * (b - a)
+                dma("s", "dt%d" % r, 6, ks, ["far%d%d" % (a, b)], T.tab[32 * b:32 * b + 32, c0:c0 + 2 * BLK], T.tab[32 * a:32 * a + 32, 6 * BLK:8 * BLK])
+
+    def tail(i):
+        k = i % 4
+        x, y, o = COMB[k]
+        if i < 4:
+            tt([x, y, "tb6"], ["tb6_%d" % k], T.tb6[:, 4 + k:4 + k + 41:4], T[x][:, 20:42:2], T[y][:, 20:42:2], o)
+        else:
+            tt([x, y, "tb7"], ["tb7_%d" % k], T.tb7[:, k:k + 41:4], T[x][:, 21:42:2], T[y][:, 21:42:2], o)
+
+    def ends():
+        act(["c4"] + ["tab%d" % i for i in range(4, 8)], ["tfa"], T.tf[:, 0:40], T.tab[:, 7 * BLK:8 * BLK], scale=cc(4))
+        act(["c4", "tb7"] + ["tb7_%d" % k for k in range(4)], ["tfb"], T.tf[:, 40:88], T.tb7[:], scale=cc(4))
+
+    cp(["pr1", "pls"], ["pr2"], T.pr2[:, 0:C], T.pr1[:, 0:C].indirect(T.pls[:]))
+    cp(["pr2", "k20p"], ["tr3"], T.tr3[:, 32:352], T.pr2[:, 0:C].indirect(T.k20p[:]))
+    turn(1)
+    turn(2)
+    middle()
+    turn(0)
+    tables(0)
+
+    quant(["xt"], ["q0", "qp0"], T.q0[:], T.qp0[:], T.xt[:])
+    quant(["ut"], ["uq", "up"], T.uq[:], T.up[:], T.ut[:])
+    cp(["uq", "ull", "ull2"], ["u3q"], T.u3q[:].bitcast(dt.uint32), T.uq[:].bitcast(dt.uint32).indirect(T.ull[:]))
+    act(["up", "ull", "ull2"], ["u3p"], T.u3p[:], T.up[:].indirect(T.ull[:]))
+    ts(["pid2"], ["c2"], cc(2), I[:, 2:3], 0.0, A.not_equal)
+    ts(["pid4", "c0"], ["c5"], cc(5), I[:, 4:5], 2.0, A.mult, cc(0), A.add)
+    ts(["c1"], ["c6"], cc(6), cc(1), -2.0, A.mult, 1.0, A.add)
+    for w in range(2):
+        ts(["c5", "c2"], ["c%d" % (8 + w)], cc(8 + w), cc(5), 5.0 - 4 * w, A.not_equal, cc(2), A.mult)
+        ts(["c5", "c6"], ["c%d" % (10 + w)], cc(10 + w), cc(5), 5.0 - 4 * w, A.is_equal, cc(6), A.mult)
+        ts(["c2", "c%d" % (10 + w)], ["c%d" % (12 + w)], cc(12 + w), cc(10 + w), -1e-29, A.add, cc(2), A.mult)
+    cp(["mI"], ["mls"], T.mls[:], T.mI[:])
+    ts(["mI"], ["m2"], T.m2[:], T.mI[:], 2.0, A.mult, 1.0, A.add)
+
+    def unit(b):
+        quant(["e0"], ["eq%d" % b], T.eq[:, 128 * b:128 * b + 128], T.ep[:, 128 * b:128 * b + 128], T.e0[:, 3 - b:515 - b])
+
+    unit(0)
+    unit(1)
+
+    left = [0]
+    for r in range(3):
+        partner = T.cores[rank ^ STEP[r]]
+        data, lst = relays(core, partner, topo)
+        q, qp, p = "q%d" % r, "qp%d" % r, "pr%d" % r
+        need("g", wr[q])
+        fc, fs = [], []
+        for k, c in enumerate(data):
+            es = topo.engines(core, c)
+            es = es[k * len(es) // 2:(k + 1) * len(es) // 2]
+            rid, pid = topo.addr(c, core)
+            a, b = k * HALF, (k + 1) * HALF
+            fc.append(RemoteDMATransfer(dst_ids=[DstId(rid=rid, pnc=pid)], dma_engine_mask=bits(es), remote_sem=T.sem["rc%d" % r],
+                                        src=T[q][:, a:b].bitcast(dt.uint8), dst=T["aq%d" % r][:, a:b].bitcast(dt.uint8)))
+            fs.append(RemoteDMATransfer(dst_ids=[DstId(rid=rid, pnc=pid)], dma_engine_mask=bits(es), remote_sem=T.sem["rs%d" % r],
+                                        src=T[qp][:, a:b], dst=T["ap%d" % r][:, a:b]))
+            left[0] += 2 * len(es)
+        g.remote_dma_fused(fc, local_sem=T.sem.left)
+        g.remote_dma_fused(fs, local_sem=T.sem.left)
+        for w in range(3):
+            mm([q, qp, "u3q", "u3p"], w, T.u3q[:, 128 * w:128 * w + 128], T.u3p[:, 128 * w:128 * w + 128], T[q][:], T[qp][:])
+
+        def own_f(b):
+            mm([q, qp, "eq%d" % b], 3 + b, T.eq[:, 128 * b:128 * b + 128], T.ep[:, 128 * b:128 * b + 128], T[q][:], T[qp][:])
+
+        for b in range(4 if r else 2):
+            own_f(b)
+
+        def signs(w):
+            act(["ps%d" % w, "c%d" % (8 + w), "c%d" % (12 + w)], ["w%d" % (w + 1)], T["w%d" % (w + 1)][:], T["ps%d" % w][:, 0:C], F.Sign, scale=cc(8 + w), bias=cc(12 + w))
+
+        def meanwhile(t):
+            if t == 0:
+                signs(1)
+            elif t == 1:
+                act(["ps2", "c14"], ["wg"], T.wg[:], T.ps2[:, 0:C], F.Sign, bias=cc(14))
+            elif t in (2, 3, 7, 8):
+                b = (2, 3, 7, 8).index(t)
+                act(["ps%d" % (3 + b)], ["fo%d" % b], T["fo%d" % b][:], T["ps%d" % (3 + b)][:, 0:C])
+            elif t == 4:
+                ends()
+
+        signs(0)
+        def differ():
+            tt([p, "pd1", "m2"], ["pd0"], T.pd[:, 0:2 * C:2], T[p][:].indirect(T.m2[:]), T.pd[:, 1:2 * C:2], A.subtract)
+
+        if r:
+            differ()
+        far = ["far%d%d" % (a, b) for b in range(4) for a in range(b)]
+        scan = lambda out, d0, d1: (lambda: g.vector.tensor_tensor_scan(out, d0, d1, 0.0, A.mult, A.add))
+        op("v", ["cg0", "cg1", "cg2", "cg3", "tab"] + far, ["sc0"], scan(T.sc0[:], T.cg[:], T.tab[:, 0:BLK]))
+        ts(["sc0"], ["of0"], T.of0[:], T.sc0[:, 3:BLK:4], BIAS, A.add)
+        for t in range(7):
+            i, j = t % 2, (t + 1) % 2
+            w, lane = "w%d" % (1 + t // 4), t % 4
+            gg, gt = "gg%d" % i, "gt%d" % i
+            cp([w, "of%d" % i], [gg], T[gg][:, 32:128], T[w][:].indirect(T["of%d" % i][:, 0:6]))
+            act([w, "of%d" % i], [gg + "s"], T[gg][:, 128:192], T[w][:].indirect(T["of%d" % i][:, 6:10]))
+            if t < 4:
+                tail(2 * t)
+            op("v", [gg, gg + "s"], [gt], lambda: g.vector.transpose(T[gt][:, 0:160], T[gg][:, 32:192]))
+            if t < 4:
+                tail(2 * t + 1)
+            elif r == 0 and t < 6:
+                unit(t - 2)
+                own_f(t - 2)
+            meanwhile(t)
+            d1 = ["tab%d" % k for k in range(8)] + ["tab"] + far
+            if t < 5:
+                op("v", [gt] + d1, ["sc%d" % j], scan(T["sc%d" % j][:], T[gt][:, lane:160:4], T.tab[:, BLK * (t + 1):BLK * (t + 2)]))
+                ts(["sc%d" % j], ["of%d" % j], T["of%d" % j][:], T["sc%d" % j][:, 3:BLK:4], BIAS, A.add)
+            elif t == 5:
+                op("v", [gt] + d1, ["s5"], scan(T.s5[:], T[gt][:, lane:160:4], T.tab[:, 6 * BLK:7 * BLK]))
+                op("v", [gg, gg + "s", gg + "a", gg + "b"], [gt + "b"], lambda: g.vector.transpose(T[gt][:, 160:352], T[gg][:, 16:208]))
+                ts(["s5"], ["of0"], T.of0[:], T.s5[:, 3:BLK:4], BIAS, A.add)
+                op("v", [gt + "b", "tb6"] + ["tb6_%d" % k for k in range(4)], ["s5b"], scan(T.s5b[:], T[gt][:, 160 + lane:352:4], T.tb6[:]))
+            else:
+                act(["s5", "c3"], ["pm0"], T.pm[:, 0:10:2], T.s5[:, 7:40:8], scale=cc(3))
+                act(["s5", "c3"], ["pm1"], T.pm[:, 10:18:2], T.s5[:, 3:32:8], scale=cc(3))
+                act(["s5b", "c3"], ["pm2"], T.pm[:, 1:10:2], T.s5b[:, 15:48:8], scale=cc(3))
+                act(["s5b", "c3"], ["pm3"], T.pm[:, 11:18:2], T.s5b[:, 11:36:8], scale=cc(3))
+                op("v", [gg, gg + "s", gg + "a", gg + "b"], [gt + "b"], lambda: g.vector.transpose(T[gt][:, 160:352], T[gg][:, 16:208]))
+                op("v", [gt, gt + "b", "tfa", "tfb"], ["s6"], scan(T.s6[:], T[gt][:, lane:352:4], T.tf[:]))
+        ll = "ll%d" % r
+        tt(["s6", "pm0", "pm1", "pm2", "pm3"], ["l32"], T.l32[:], T.s6[:, 3:72:4], T.pm[:], A.add)
+        ts(["l32"], [ll], T[ll][:], T.l32[:], BIAS, A.add)
+        need("g", wr[ll])
+        rid, pid = topo.addr(lst, core)
+        es = topo.engines(core, lst)
+        g.remote_dma(T["al%d" % r][:], T[ll][:], T.sem["rL%d" % r], T.sem.left, pid, rid, bits(es))
+        left[0] += len(es)
+        np_ = "pr%d" % (r + 1)
+        act(["wg", ll], ["be2"], T.be2[:], T.wg[:].indirect(T[ll][:]))
+        meanwhile(7)
+        meanwhile(8)
+        cp(["wg", ll], ["be"], T.be[:], T.wg[:].indirect(T[ll][:]))
+        if r == 0:
+            differ()
+        tt(["be", "be2", "mls"], ["ne1"], T.ne2[:, 1:2 * C:2], T.be[:].indirect(T.mls[:]), T.be2[:], A.not_equal)
+        op("v", ["ne0", "ne1", "pd0", "pd1"], [np_], scan(T[np_][:], T.ne2[:], T.pd[:]))
+        if r < 2:
+            powers(r + 1)
+        else:
+            cp(["idr", ll], ["lo"], T.lo[:], T.idr[:].indirect(T[ll][:]))
+            quant(["vt"], ["vq"], T.vq[:], T.vp[:], T.vt[:])
+            ts(["lo"], ["lo"], T.lo[:], T.lo[:], 4.0, A.mult, BIAS, A.add)
+            ts([np_], ["po"], T.po[:], T[np_][:, 1:2 * C:2], 4.0, A.mult, BIAS, A.add)
+            dma("s", "out", 8, ["lo"], ["pl0"], T.pl[:, 0:C], T.lo[0:128:16, :])
+            dma("s", "out", 8, ["po"], ["pl1"], T.pl[:, C:2 * C], T.po[0:128:16, :])
+        wr["aq"] = [("aq_%d" % r, sum(2 * len(topo.engines(c, core)) for c in relays(partner, core, topo)[0]))]
+        wr["al"] = [("aL_%d" % r, len(topo.engines(relays(partner, core, topo)[1], core)))]
+        count["aq_%d" % r], count["aL_%d" % r] = wr["aq"][0][1], wr["al"][0][1]
+        for b in range(4):
+            mm(["aq", "eq%d" % b], (7 + b) % 8, T.eq[:, 128 * b:128 * b + 128], T.ep[:, 128 * b:128 * b + 128], T["aq%d" % r][:], T["ap%d" % r][:])
+        for b in range(4):
+            act(["ps%d" % ((7 + b) % 8)], ["fp%d" % b], T["fp%d" % b][:], T["ps%d" % ((7 + b) % 8)][:, 0:C])
+        al, zt = T["al%d" % r], T.zt
+        for b in (0, 2, 1, 3):
+            if b < 2:
+                cp(["fp%d" % b, "al"], ["zt%d" % b], zt[:, b:4 * C:4], T["fp%d" % b][:].indirect(al[:]))
+            else:
+                act(["fp%d" % b, "al"], ["zt%d" % b], zt[:, b:4 * C:4], T["fp%d" % b][:].indirect(al[:]))
+        quant(["zt%d" % b for b in range(4)], ["zq"], T.zq[:], T.zp[:], zt[:])
+        if r < 2:
+            rows(3, np_, "tl2", "a")
+            tables(r + 1)
+        for b in range(4):
+            mm(["zq", "wq", "wp"], 3 + b, T.wq[:, 128 * b:128 * b + 128], T.wp[:, 128 * b:128 * b + 128], T.zq[:], T.zp[:])
+        xn = T["xn%d" % r]
+        for b in range(4):
+            act(["ps%d" % (3 + b)], ["hb%d" % b], T["hb%d" % b][:], T["ps%d" % (3 + b)][:, 0:C], scale=0.03125)
+            tt(["hb%d" % b, "fo%d" % b, ll], ["xn%d" % b], xn[:, b:4 * C:4], T["hb%d" % b][:].indirect(T[ll][:]), T["fo%d" % b][:], A.add)
+        if r < 2:
+            act([np_], ["pd1"], T.pd[:, 1:2 * C:2], T[np_][:, 1:2 * C:2])
+        nq, nqp = "q%d" % (r + 1), "qp%d" % (r + 1)
+        quant(["xn%d" % b for b in range(4)], [nq, nqp], T[nq][:], T[nqp][:], xn[:])
+    mm(["q3", "qp3", "vq"], 7, T.vq[:], T.vp[:], T.q3[:], T.qp3[:])
+    dma("s", "out", 8, ["q3"], ["oc"], T.oc[:], T.q3[:].bitcast(dt.uint8))
+    for k in range(4):
+        dma("s" if k % 2 else "a", "out", 8, ["qp3"], ["osc%d" % k], T.osc[4 * k:4 * k + 4, :], T.qp3[32 * k:32 * k + 4, :])
+    act(["ps7"], ["yo"], T.yo[:], T.ps7[:, 0:C])
+    dma("s", "out", 8, ["yo"], ["y"], T.y[:], T.yo[:])
+    g.wait_ge(T.sem.left, left[0])
+    for s in sorted(count):
+        g.wait_ge(T.sem[s], count[s])

@@ -6,7 +6,8 @@ C = 288
 STEP = [4, 1, 2]
 HALF = C // 2
 ENT = 10
-BLK = 4 * ENT
+ROW = 16 * ENT
+CUT = 6
 BIAS = 144.0
 
 SCRATCH = {
@@ -15,37 +16,37 @@ SCRATCH = {
     "pI": ("sbuf", [128, 18], "int32"), "kI": ("sbuf", [128, 18], "int32"), "mI": ("sbuf", [128, 18], "int32"),
     "wq": ("sbuf", [128, 512], "float8_e4m3fn_x4"), "wp": ("sbuf", [128, 512], "uint8"),
     "uq": ("sbuf", [128, 128], "float8_e4m3fn_x4"), "up": ("sbuf", [128, 128], "uint8"),
-    "u3q": ("sbuf", [128, 384], "float8_e4m3fn_x4"), "u3p": ("sbuf", [128, 384], "uint8"),
+    "u1q": ("sbuf", [128, 128], "float8_e4m3fn_x4"), "u1p": ("sbuf", [128, 128], "uint8"),
+    "u2q": ("sbuf", [128, 128], "float8_e4m3fn_x4"), "u2p": ("sbuf", [128, 128], "uint8"),
     "vq": ("sbuf", [128, 128], "float8_e4m3fn_x4"), "vp": ("sbuf", [128, 128], "uint8"),
     "ones": ("sbuf", [128, 516], "bfloat16"), "e0": ("sbuf", [128, 516], "bfloat16"),
     "eq": ("sbuf", [128, 512], "float8_e4m3fn_x4"), "ep": ("sbuf", [128, 512], "uint8"),
-    "ior": ("sbuf", [128, C], "bfloat16"), "idr": ("sbuf", [128, C], "bfloat16"),
-    "pid": ("sbuf", [128, 8], "int32"), "cst": ("sbuf", [128, 32], "float32"),
-    "ulf": ("sbuf", [128, 24], "float32"), "ull": ("sbuf", [128, 24], "uint16"),
-    "m42": ("sbuf", [128, 42], "float32"), "cg": ("sbuf", [128, BLK], "bfloat16"),
-    "pls": ("sbuf", [128, 18], "uint16"), "mls": ("sbuf", [128, 18], "uint16"), "k20": ("sbuf", [128, 20], "uint16"),
-    "kf": ("sbuf", [128, 18], "float32"), "ke": ("sbuf", [128, 20], "float32"), "ko": ("sbuf", [128, 20], "float32"),
-    "tl1": ("sbuf", [128, 20], "uint16"), "tl2": ("sbuf", [128, 20], "uint16"),
-    "xm": ("sbuf", [128, 42], "float32"), "lf": ("sbuf", [128, 20], "float32"),
-    "cP": ("sbuf", [128, 42], "float32"), "cQ": ("sbuf", [128, 42], "float32"), "cR": ("sbuf", [128, 42], "float32"), "cU": ("sbuf", [128, 42], "float32"),
-    "tab": ("sbuf", [128, 8 * BLK], "float32"), "tb6": ("sbuf", [128, 48], "float32"), "tb7": ("sbuf", [128, 48], "float32"), "tf": ("sbuf", [128, 88], "float32"),
-    "w1": ("sbuf", [128, C], "bfloat16"), "w2": ("sbuf", [128, C], "bfloat16"), "wg": ("sbuf", [128, C], "bfloat16"),
-    "s5": ("sbuf", [128, BLK], "float32"), "s5b": ("sbuf", [128, 48], "float32"), "s6": ("sbuf", [128, 88], "float32"),
-    "pm": ("sbuf", [128, 18], "float32"), "l32": ("sbuf", [128, 18], "float32"),
-    "be": ("sbuf", [128, C], "bfloat16"), "be2": ("sbuf", [128, C], "bfloat16"),
-    "ne2": ("sbuf", [128, 2 * C], "bfloat16"), "pd": ("sbuf", [128, 2 * C], "float32"),
-    "m2": ("sbuf", [128, 18], "uint16"), "k20p": ("sbuf", [128, 20], "uint16"),
-    "yo": ("sbuf", [128, C], "float32"), "lo": ("sbuf", [128, C], "float32"), "po": ("sbuf", [128, C], "float32"),
+    "pf": ("sbuf", [128, 1], "float32"), "pw": ("sbuf", [128, 8], "float32"), "bi": ("sbuf", [128, 8], "int32"), "bj": ("sbuf", [128, 8], "int32"),
+    "bit": ("sbuf", [128, 8], "float32"), "sg": ("sbuf", [128, 8], "float32"), "nb": ("sbuf", [128, 8], "float32"),
+    "cst": ("sbuf", [128, 32], "float32"), "quart": ("sbuf", [128, 72], "float32"),
+    "idr": ("sbuf", [128, C], "bfloat16"), "lor": ("sbuf", [128, 32], "float32"), "d16": ("sbuf", [128, 48], "float32"),
+    "own": ("sbuf", [128, C], "bfloat16"), "lane": ("sbuf", [128, 18], "uint16"), "half": ("sbuf", [128, 8], "float32"),
+    "ulf": ("sbuf", [128, 16], "float32"), "ull": ("sbuf", [128, 16], "uint16"),
+    "mls": ("sbuf", [128, 18], "uint16"), "k20": ("sbuf", [128, 20], "uint16"),
+    "kf": ("sbuf", [128, 18], "float32"), "ke": ("sbuf", [128, 40], "float32"),
+    "y1": ("sbuf", [128, C], "bfloat16"), "y2": ("sbuf", [128, C], "bfloat16"), "y3": ("sbuf", [128, C], "bfloat16"),
+    "tr": ("sbuf", [128, 368], "bfloat16"), "tab": ("sbuf", [128, 672], "bfloat16"), "tf": ("sbuf", [128, C], "bfloat16"),
+    "w": ("sbuf", [128, C], "bfloat16"), "wg": ("sbuf", [128, C], "bfloat16"),
+    "of": ("sbuf", [128, 2 * ENT], "uint16"),
+    "s5b": ("sbuf", [128, 176], "bfloat16"), "s6": ("sbuf", [128, C], "bfloat16"), "pm": ("sbuf", [128, 18], "bfloat16"),
+    "be": ("sbuf", [128, C], "bfloat16"), "bm": ("sbuf", [128, C], "bfloat16"), "hs": ("sbuf", [128, 880], "bfloat16"),
+    "prow": ("sbuf", [128, C], "bfloat16"), "mrow": ("sbuf", [128, C], "bfloat16"), "ms": ("sbuf", [128, C], "float32"),
+    "ex": ("sbuf", [128, 54], "float32"), "pn": ("sbuf", [128, 54], "float32"), "hd": ("sbuf", [128, 18], "float32"),
+    "ph": ("sbuf", [128, 18], "float32"), "mh": ("sbuf", [128, 18], "float32"),
+    "yo": ("sbuf", [128, C], "float32"), "lo": ("sbuf", [128, 2 * C], "float32"),
 }
 for _i in range(2):
     SCRATCH["gg%d" % _i] = ("sbuf", [128, 208], "bfloat16")
     SCRATCH["gt%d" % _i] = ("sbuf", [128, 352], "bfloat16")
-    SCRATCH["sc%d" % _i] = ("sbuf", [128, BLK], "float32")
-    SCRATCH["of%d" % _i] = ("sbuf", [128, ENT], "uint16")
+    SCRATCH["sc%d" % _i] = ("sbuf", [128, ROW], "bfloat16")
 for _i in range(4):
-    SCRATCH["tr%d" % _i] = ("sbuf", [128, 368], "bfloat16")
-    SCRATCH["tt%d" % _i] = ("sbuf", [128, 672], "bfloat16")
-    SCRATCH["pr%d" % _i] = ("sbuf", [128, 2 * C], "bfloat16")
+    SCRATCH["dg%d" % _i] = ("sbuf", [128, C], "bfloat16")
+    SCRATCH["pls%d" % _i] = ("sbuf", [128, 18], "uint16")
     SCRATCH["q%d" % _i] = ("sbuf", [128, C], "float8_e4m3fn_x4")
     SCRATCH["qp%d" % _i] = ("sbuf", [128, C], "uint8")
     SCRATCH["fo%d" % _i] = ("sbuf", [128, C], "bfloat16")
@@ -63,7 +64,7 @@ for _i in range(3):
 SEMAPHORES = ["sv", "sa", "st", "sg", "left",
               "lx", "lu", "lv", "lp", "lk", "lm", "lw", "lws", "out"]
 for _i in range(3):
-    SEMAPHORES += ["rc%d" % _i, "rs%d" % _i, "rL%d" % _i, "aq_%d" % _i, "aL_%d" % _i, "dt%d" % _i]
+    SEMAPHORES += ["rc%d" % _i, "rs%d" % _i, "rL%d" % _i, "aq_%d" % _i, "aL_%d" % _i]
 
 
 def relays(core, partner, topo):
@@ -180,8 +181,12 @@ def rank_program(g, core, T, topo):
     def act(reads, writes, out, in_, f=F.Copy, **kw):
         op("a", reads, writes, lambda: g.scalar.activation(out, in_, f, **kw))
 
-    def mm(reads, bank, lhs, lhsp, rhs, rhsp):
-        op("t", reads, ["ps%d" % bank], lambda: g.tensor.matmul_mx(T["ps%d" % bank][:, 0:C], lhs, lhsp, rhs, rhsp, True, True))
+    def mm(reads, bank, lhs, lhsp, q, p, a=0, b=C):
+        op("t", reads, ["ps%d" % bank], lambda: g.tensor.matmul_mx(T["ps%d" % bank][:, 0:b - a], lhs, lhsp, T[q][:, a:b], T[p][:, a:b], True, True))
+
+    def halves(reads, q, p, t):
+        for h in range(2):
+            quant(reads, [q + "ab"[h]], T[q][:, h * HALF:(h + 1) * HALF], T[p][:, h * HALF:(h + 1) * HALF], T[t][:, 4 * h * HALF:4 * (h + 1) * HALF])
 
     def quant(reads, writes, q, p, t):
         op("v", reads, writes, lambda: g.vector.quantize_mx(q, p, t))
@@ -189,313 +194,324 @@ def rank_program(g, core, T, topo):
     def fill(key, ap, c):
         op("v", [], [key], lambda: g.vector.memset(ap, c))
 
-    dma("s", "lp", 1, [], ["pI"], T.pI[:], T.pg[:])
-    dma("a", "lk", 1, [], ["kI"], T.kI[:], T.kg[:])
-    dma("s", "lx", 1, [], ["xt"], T.xt[:], T.x[:])
-    dma("a", "lu", 1, [], ["ut"], T.ut[:], T.u[:])
-    dma("a", "lm", 1, [], ["mI"], T.mI[:], T.mg[:])
-    dma("s", "lw", 1, [], ["wq"], T.wq[:].bitcast(dt.uint8), T.wc[:])
-    dma("s", "lws", 1, [], ["wp"], T.wp[:], T.ws[:])
-    dma("a", "lv", 1, [], ["vt"], T.vt[:], T.v[:])
+    def turn(reads, writes, out, in_):
+        op("v", reads, writes, lambda: g.vector.transpose(out, in_))
 
-    op("g", [], ["pid0"], lambda: g.iota(T.pid[:, 0:1], [[0, 1]], 0, 1))
-    op("g", [], ["ior"], lambda: g.iota(T.ior[:], [[1, C]], -144, 0, allow_small_or_imprecise_dtypes=True))
-    op("g", [], ["ulf"], lambda: g.iota(T.ulf[:, 0:16], [[64, 2], [32, 4], [0, 2]], -96, 0, allow_small_or_imprecise_dtypes=True))
-    op("g", [], ["ulf2"], lambda: g.iota(T.ulf[:, 16:24], [[16, 8]], 0, 0, allow_small_or_imprecise_dtypes=True))
-    fill("ones", T.ones[:], 1.0)
-    op("g", ["ones"], ["e0"], lambda: g.affine_select(T.e0[:], T.ones[:], [[1, 516]], A.is_equal, 0.0, -3, -4))
-    S, I = T.cst, T.pid
-    cc = lambda j: S[:, j:j + 1]
+    def scan(reads, writes, out, d0, d1, first=0.0):
+        op("v", reads, writes, lambda: g.vector.tensor_tensor_scan(out, d0, d1, first, A.mult, A.add))
+
+    def iota(key, out, pattern, base, step=0):
+        op("g", [], [key], lambda: g.iota(out, pattern, base, step, allow_small_or_imprecise_dtypes=True))
 
     def plain(key, out, n, c):
         act(["ones"], [key], out, T.ones[:, 0:n], scale=c)
 
-    fill("ke", T.ke[:], 0.0)
-    fill("ko", T.ko[:], 0.0)
-    plain("pr0", T.pr0[:, 0:2 * C:2], C, 0.0)
-    for i in (1, 2, 3, 0):
-        plain("tr%da" % i, T["tr%d" % i][:, 16:32], 16, 0.0)
-        plain("tr%db" % i, T["tr%d" % i][:, 352:368], 16, 0.0)
-    ts(["pid0"], ["pid1"], I[:, 1:2], I[:, 0:1], 3, A.bitwise_and)
-    ts(["pid0"], ["pid2"], I[:, 2:3], I[:, 0:1], 2, A.logical_shift_right, 3, A.bitwise_and)
-    ts(["pid0"], ["pid3"], I[:, 3:4], I[:, 0:1], 4, A.logical_shift_right, 1, A.bitwise_and)
-    ts(["pid0"], ["pid4"], I[:, 4:5], I[:, 0:1], 5, A.logical_shift_right)
-    ts(["pid3"], ["c3"], cc(3), I[:, 3:4], 0.0, A.is_equal)
-    cp(["pid3"], ["c4"], cc(4), I[:, 3:4])
-    ts(["ior"], ["idr"], T.idr[:], T.ior[:], 0.25, A.mult)
-    cp(["pid1"], ["c0"], cc(0), I[:, 1:2])
-    ts(["pid2"], ["c1"], cc(1), I[:, 2:3], 2.0, A.is_equal)
-    ts(["c0", "c1"], ["c7"], cc(7), cc(0), 16.0, A.mult, cc(1), A.add)
-    ts(["ulf", "c7"], ["ull"], T.ull[:, 0:16], T.ulf[:, 0:16], cc(7), A.add, 0.0, A.max)
-    cp(["ulf2"], ["ull2"], T.ull[:, 16:24], T.ulf[:, 16:24])
+    dma("s", "lp", 1, [], ["pI"], T.pI[:], T.pg[:])
+    dma("a", "lk", 1, [], ["kI"], T.kI[:], T.kg[:])
+    dma("s", "lx", 1, [], ["xt"], T.xt[:], T.x[:])
+    dma("a", "lm", 1, [], ["mI"], T.mI[:], T.mg[:])
+    dma("s", "lu", 1, [], ["ut"], T.ut[:], T.u[:])
+    dma("s", "lw", 1, [], ["wq"], T.wq[:].bitcast(dt.uint8), T.wc[:])
+    dma("s", "lws", 1, [], ["wp"], T.wp[:], T.ws[:])
+    dma("s", "lv", 1, [], ["vt"], T.vt[:], T.v[:])
 
+    iota("pf", T.pf[:], [[0, 1]], 0, 1)
+    iota("quart", T.quart[:], [[1, 72]], -36)
+    iota("ulf", T.ulf[:, 0:8], [[32, 4], [0, 2]], -16)
+    iota("ulf2", T.ulf[:, 8:16], [[16, 8]], 0)
+    iota("lor", T.lor[:], [[-1, 2], [1, 16]], 0)
+    iota("idr", T.idr[:], [[1, C]], -144)
+    fill("half", T.half[:], 0.5)
+    fill("ones", T.ones[:], 1.0)
+    op("g", ["ones"], ["e0"], lambda: g.affine_select(T.e0[:], T.ones[:], [[1, 516]], A.is_equal, 0.0, -3, -4))
+    b = lambda i: T.bit[:, i:i + 1]
+    nb = lambda i: T.nb[:, i:i + 1]
+    sg = lambda i: T.sg[:, i:i + 1]
+    cc = lambda j: T.cst[:, j:j + 1]
+    fill("of", T.of[:], 0)
+    op("v", ["half", "ones"], ["pw"], lambda: g.vector.tensor_tensor_scan(T.pw[:], T.half[:], T.ones[:, 0:8], 256.0, A.mult, A.mult))
+    fill("ke", T.ke[:], 0.0)
+    fill("ex", T.ex[:], 0.0)
+    ts(["pf", "pw"], ["bi"], T.bi[:], T.pw[:], T.pf[:], A.mult)
+    fill("hs0", T.hs[:, 31:880:48], 0.0)
+    ts(["bi"], ["bj"], T.bj[:, 0:7], T.bi[:, 0:7], 7, A.logical_shift_right, 1, A.bitwise_and)
+    ts(["bi"], ["bj7"], T.bj[:, 7:8], T.bi[:, 7:8], 15, A.bitwise_and)
+    cp(["bj"], ["bit"], T.bit[:, 0:7], T.bj[:, 0:7])
+    ts(["bj"], ["nb"], T.nb[:, 0:7], T.bj[:, 0:7], -1.0, A.mult, 1.0, A.add)
+    ts(["bj"], ["sg"], T.sg[:, 0:7], T.bj[:, 0:7], 2.0, A.mult, -1.0, A.add)
+    for i in range(4):
+        act(["bit"], ["c%d" % i], cc(i), b(1), scale=0.25 * i)
+    ts(["sg"], ["c4"], cc(4), sg(2), sg(3), A.mult)
+    for i in range(4):
+        ts(["quart", "nb", "c%d" % i], ["dg3_%d" % i], T.dg3[:, i:C:4], T.quart[:], nb(1), A.mult, cc(i), A.add)
+    d3 = ["dg3_%d" % i for i in range(4)]
+    ts(d3 + ["c4"], ["dg2"], T.dg2[:], T.dg3[:], cc(4), A.mult)
+    plain("tra", T.tr[:, 16:32], 16, 0.0)
+    plain("trb", T.tr[:, 352:368], 16, 0.0)
+    act(d3 + ["sg"], ["dg1"], T.dg1[:], T.dg3[:], scale=sg(3))
+    act(d3 + ["sg"], ["dg0"], T.dg0[:], T.dg3[:], scale=sg(2))
+
+    def power(r, n):
+        src, dst = ["dg3", "y1", "y2"][n], ["y1", "y2", "y3"][n]
+        tt((d3 if n == 0 else [src]) + ["pls%d" % r, "dg%d" % (2 - n)], [dst], T[dst][:], T[src][:].indirect(T["pls%d" % r][:]), T["dg%d" % (2 - n)][:], A.add)
+
+    def starts(cut):
+        if cut:
+            cp(["y3", "k20"], ["tr1"], T.tr[:, 32:32 + 16 * cut], T.y3[:].indirect(T.k20[:, 0:cut]))
+        act(["y3", "k20"], ["tr2"] if cut else ["tr1", "tr2"], T.tr[:, 32 + 16 * cut:352], T.y3[:].indirect(T.k20[:, cut:20]))
+
+    def table(part):
+        if part == 0:
+            turn(["tr1", "tr2"], ["tabA"], T.tab[:, 0:320], T.tr[:, 32:352])
+        else:
+            turn(["tr1", "tr2", "tra", "trb"], ["tabB"], T.tab[:, 320:672], T.tr[:, 16:368])
+
+    cp(["pI"], ["pls0"], T.pls0[:], T.pI[:])
     cp(["kI"], ["kf"], T.kf[:], T.kI[:])
-    cp(["pI"], ["pls"], T.pls[:], T.pI[:])
-    ts(["pI"], ["tl1"], T.tl1[:, 0:18], T.pI[:], 2.0, A.mult, 1.0, A.add)
-    cp(["idr", "pls", "pr0"], ["pr0"], T.pr0[:, 1:2 * C:2], T.idr[:].indirect(T.pls[:]))
+    power(0, 0)
     for h in range(2):
         for y in range(2):
             c0 = 10 * (1 - h) + y
             n = len(range(c0, 18 if h == 0 else 10, 2))
             m0 = 2 * h + y
-            act(["kf", "c3", "ke"], ["ke%d" % m0], T.ke[:, m0:m0 + 4 * n - 3:4], T.kf[:, c0:c0 + 2 * n - 1:2], scale=cc(3))
-    act(["kf", "c4", "ko"], ["ko1"], T.ko[:, 1:20:2], T.kf[:, 0:10], scale=cc(4))
-    act(["kf", "c4", "ko"], ["ko0"], T.ko[:, 0:15:2], T.kf[:, 10:18], scale=cc(4))
-    tt(["ke0", "ke1", "ke2", "ke3", "ko0", "ko1"], ["ke"], T.ke[:], T.ke[:], T.ko[:], A.add)
-    ts(["ke"], ["k20"], T.k20[:], T.ke[:], 2.0, A.mult, 1.0, A.add)
-    cp(["ke"], ["k20p"], T.k20p[:], T.ke[:])
-    cp(["pr0", "tl1"], ["pr1"], T.pr1[:, 0:C], T.pr0[:].indirect(T.tl1[:, 0:18]))
-    act(["pr0", "k20"], ["tr1"], T.tr1[:, 32:352], T.pr0[:].indirect(T.k20[:]))
-    act(["pr1", "k20p"], ["tr2"], T.tr2[:, 32:352], T.pr1[:, 0:C].indirect(T.k20p[:]))
-    act(["idr", "k20p"], ["tr0"], T.tr0[:, 32:352], T.idr[:].indirect(T.k20p[:]))
-    plain("tab", T.tab[:], 8 * BLK, 0.0)
-    act(["c3", "ones"], ["m42"], T.m42[:, 0:42:2], T.ones[:, 0:21], scale=cc(3))
-    act(["c4", "ones"], ["m42b"], T.m42[:, 1:42:2], T.ones[:, 0:21], scale=cc(4))
-    act(["pr0"], ["pd1"], T.pd[:, 1:2 * C:2], T.pr0[:, 1:2 * C:2])
-    plain("cg0", T.cg[:, 0:BLK:4], ENT, 0.0)
-    plain("cg1", T.cg[:, 1:BLK:4], ENT, 1.0)
-    plain("cg2", T.cg[:, 2:BLK:4], ENT, -1.0)
-    plain("cg3", T.cg[:, 3:BLK:4], ENT, 1.0)
-    plain("c14", cc(14), 1, -1e-29)
-    plain("tb6", T.tb6[:], 48, 0.0)
-    plain("tb7", T.tb7[:], 48, 0.0)
+            act(["kf", "nb", "ke"], ["ke%d" % m0], T.ke[:, m0:m0 + 4 * n - 3:4], T.kf[:, c0:c0 + 2 * n - 1:2], scale=nb(4))
+    act(["kf", "bit", "ke"], ["ko1"], T.ke[:, 21:40:2], T.kf[:, 0:10], scale=b(4))
+    act(["kf", "bit", "ke"], ["ko0"], T.ke[:, 20:35:2], T.kf[:, 10:18], scale=b(4))
+    ts(["nb"], ["c5"], cc(5), nb(0), nb(1), A.mult, nb(2), A.mult)
+    ts(["nb"], ["c6"], cc(6), nb(3), nb(5), A.mult, nb(6), A.mult)
+    power(0, 1)
+    ts(["nb", "bit"], ["c7"], cc(7), nb(0), nb(1), A.mult, b(2), A.mult)
+    tt(["ke0", "ke1", "ke2", "ke3", "ko0", "ko1"], ["ke"], T.ke[:, 0:20], T.ke[:, 0:20], T.ke[:, 20:40], A.add)
+    quant(["xt"], ["q0a", "q0b"], T.q0[:], T.qp0[:], T.xt[:])
+    power(0, 2)
+    cp(["ke"], ["k20"], T.k20[:], T.ke[:, 0:20])
+    ts(["bit", "c7"], ["c15"], cc(15), b(3), 16.0, A.mult, cc(7), A.add)
+    act(["nb", "c5"], ["c8"], cc(8), cc(5), F.Identity, scale=-1.0, bias=nb(0))
+    act(["c5"], ["c9"], cc(9), cc(5), F.Identity, scale=-1.0, bias=T.ones[:, 0:1])
+    act(["c6"], ["c10"], cc(10), cc(6), F.Identity, scale=-1.0, bias=T.ones[:, 0:1])
+    plain("c17", cc(17), 1, -1e-29)
+    plain("c18", cc(18), 1, BIAS)
     for i in range(2):
         plain("gg%da" % i, T["gg%d" % i][:, 16:32], 16, 0.0)
         plain("gg%db" % i, T["gg%d" % i][:, 192:208], 16, 0.0)
-    plain("ne0", T.ne2[:, 0:2 * C:2], C, 0.0)
-
-    def turn(n):
-        k, t = "tr%d" % n, "tt%d" % n
-        op("v", [k], [t + "a"], lambda: g.vector.transpose(T[t][:, 0:320], T[k][:, 32:352]))
-        op("v", [k, k + "a", k + "b"], [t + "b"], lambda: g.vector.transpose(T[t][:, 320:672], T[k][:, 16:368]))
-
-    def ent(n):
-        return T["tt%d" % n][:, 0:672:16]
-
-    def aslist(n, name):
-        t = "tt%d" % n
-        tt([t + "a", t + "b", "m42", "m42b"], ["xm"], T.xm[:], ent(n), T.m42[:], A.mult)
-        tt(["xm"], ["lf"], T.lf[:], T.xm[:, 0:20], T.xm[:, 21:41], A.add)
-        ts(["lf"], [name], T[name][:], T.lf[:], 8.0, A.mult, 2 * BIAS + 1, A.add)
-
-    def rows(n, key, lst, e="v"):
-        (cp if e == "v" else act)([key, lst], ["tr%d" % n], T["tr%d" % n][:, 32:352], T[key][:].indirect(T[lst][:]))
-
-    COMB = [("cR", "cU", A.subtract), ("cP", "cQ", A.subtract), ("cR", "cU", A.add), ("cP", "cQ", A.add)]
-
-    def powers(r):
-        p = "pr%d" % r
-        rows(1, p, "k20")
-        turn(1)
-        aslist(1, "tl1")
-        rows(2, p, "tl1")
-        turn(2)
-        aslist(2, "tl2")
-        middle()
-
-    def middle():
-        ks = ["tt1a", "tt1b", "tt2a", "tt2b"]
-        tt(ks, ["cQ"], T.cQ[:], ent(1), ent(2), A.add)
-        tt(ks, ["cU"], T.cU[:], ent(1), ent(2), A.subtract)
-
-    def tables(r):
-        turn(3)
-        ks = ["tt0a", "tt0b", "tt3a", "tt3b"]
-        tt(ks, ["cP"], T.cP[:], ent(0), ent(3), A.add)
-        tt(ks, ["cR"], T.cR[:], ent(3), ent(0), A.subtract)
-        for h in range(2):
-            for k in range(4):
-                x, y, o = COMB[k]
-                c0 = 6 * BLK + BLK * h + k
-                tt([x, y], ["tab"] if h == k == 0 else ["tab%d" % (4 * h + k)], T.tab[:, c0:c0 + BLK - 3:4], T[x][:, h:20:2], T[y][:, h:20:2], o)
-        ks = ["tab"] + ["tab%d" % i for i in range(1, 8)]
-        for b in range(4):
-            for a in range(b):
-                c0 = 6 * BLK - 2 * BLK * (b - a)
-                dma("s", "dt%d" % r, 6, ks, ["far%d%d" % (a, b)], T.tab[32 * b:32 * b + 32, c0:c0 + 2 * BLK], T.tab[32 * a:32 * a + 32, 6 * BLK:8 * BLK])
-
-    def tail(i):
-        k = i % 4
-        x, y, o = COMB[k]
-        if i < 4:
-            tt([x, y, "tb6"], ["tb6_%d" % k], T.tb6[:, 4 + k:4 + k + 41:4], T[x][:, 20:42:2], T[y][:, 20:42:2], o)
-        else:
-            tt([x, y, "tb7"], ["tb7_%d" % k], T.tb7[:, k:k + 41:4], T[x][:, 21:42:2], T[y][:, 21:42:2], o)
-
-    def ends():
-        act(["c4"] + ["tab%d" % i for i in range(4, 8)], ["tfa"], T.tf[:, 0:40], T.tab[:, 7 * BLK:8 * BLK], scale=cc(4))
-        act(["c4", "tb7"] + ["tb7_%d" % k for k in range(4)], ["tfb"], T.tf[:, 40:88], T.tb7[:], scale=cc(4))
-
-    cp(["pr1", "pls"], ["pr2"], T.pr2[:, 0:C], T.pr1[:, 0:C].indirect(T.pls[:]))
-    cp(["pr2", "k20p"], ["tr3"], T.tr3[:, 32:352], T.pr2[:, 0:C].indirect(T.k20p[:]))
-    turn(1)
-    turn(2)
-    middle()
-    turn(0)
-    tables(0)
-
-    quant(["xt"], ["q0", "qp0"], T.q0[:], T.qp0[:], T.xt[:])
+    plain("gt1", T.gt1[:, 0:ROW], ROW, 1.0)
+    plain("gt1", T.gt1[:, 0:ROW:8], 2 * ENT, 0.0)
+    plain("gt1", T.gt1[:, 4:ROW:16], ENT, -1.0)
+    act(["idr", "pls0"], ["prow"], T.prow[:], T.idr[:].indirect(T.pls0[:]))
+    ts(["ulf", "c15"], ["ull"], T.ull[:, 0:8], T.ulf[:, 0:8], cc(15), A.add, 0.0, A.max)
     quant(["ut"], ["uq", "up"], T.uq[:], T.up[:], T.ut[:])
-    cp(["uq", "ull", "ull2"], ["u3q"], T.u3q[:].bitcast(dt.uint32), T.uq[:].bitcast(dt.uint32).indirect(T.ull[:]))
-    act(["up", "ull", "ull2"], ["u3p"], T.u3p[:], T.up[:].indirect(T.ull[:]))
-    ts(["pid2"], ["c2"], cc(2), I[:, 2:3], 0.0, A.not_equal)
-    ts(["pid4", "c0"], ["c5"], cc(5), I[:, 4:5], 2.0, A.mult, cc(0), A.add)
-    ts(["c1"], ["c6"], cc(6), cc(1), -2.0, A.mult, 1.0, A.add)
-    for w in range(2):
-        ts(["c5", "c2"], ["c%d" % (8 + w)], cc(8 + w), cc(5), 5.0 - 4 * w, A.not_equal, cc(2), A.mult)
-        ts(["c5", "c6"], ["c%d" % (10 + w)], cc(10 + w), cc(5), 5.0 - 4 * w, A.is_equal, cc(6), A.mult)
-        ts(["c2", "c%d" % (10 + w)], ["c%d" % (12 + w)], cc(12 + w), cc(10 + w), -1e-29, A.add, cc(2), A.mult)
-    cp(["mI"], ["mls"], T.mls[:], T.mI[:])
-    ts(["mI"], ["m2"], T.m2[:], T.mI[:], 2.0, A.mult, 1.0, A.add)
+    ts(["c8", "c10"], ["c13"], cc(13), cc(8), cc(10), A.mult)
+    ts(["c7", "c6"], ["c11"], cc(11), cc(7), cc(6), A.mult, -2.0, A.mult)
+    cp(["uq", "ull"], ["u1q"], T.u1q[:].bitcast(dt.uint32), T.uq[:].bitcast(dt.uint32).indirect(T.ull[:, 0:8]))
+    act(["up", "ull"], ["u1p"], T.u1p[:], T.up[:].indirect(T.ull[:, 0:8]))
+    ts(["c11", "c9", "c13"], ["c12"], cc(12), cc(11), cc(9), A.add, cc(13), A.subtract)
+    cp(["ulf2"], ["ull2"], T.ull[:, 8:16], T.ulf[:, 8:16])
+    starts(10)
+    ts(["c12", "c9"], ["c14"], cc(14), cc(12), -1e-29, A.add, cc(9), A.mult)
 
     def unit(b):
         quant(["e0"], ["eq%d" % b], T.eq[:, 128 * b:128 * b + 128], T.ep[:, 128 * b:128 * b + 128], T.e0[:, 3 - b:515 - b])
 
-    unit(0)
-    unit(1)
+    def shared(src, lst, dst):
+        cp(src[1] + [lst], [dst + "a"], T[dst][:, 0:160], T[src[0]][:].indirect(T[lst][:, 0:10]))
+        act(src[1] + [lst], [dst + "b"], T[dst][:, 160:C], T[src[0]][:].indirect(T[lst][:, 10:18]))
+
+    def spread(key, src):
+        tt([key, "avg"], ["hd"], T.hd[:], src, T.ex[:, 2:54:3], A.subtract)
+        return lambda: ts(["hd", "c20", "ex"], ["hdl"], T.ex[:, 0:54:3], T.hd[:], cc(20), A.mult)
+
+    ROUND = 12582912.0
+    later = [
+        lambda: cp(["mI"], ["mls"], T.mls[:], T.mI[:]),
+        lambda: cp(["bj7"], ["c16"], cc(16), T.bj[:, 7:8]),
+        lambda: ts(["lor", "c16"], ["d16a"], T.d16[:, 0:16], T.lor[:, 0:16], cc(16), A.not_equal),
+        lambda: ts(["lor", "c16"], ["d16b"], T.d16[:, 16:32], T.lor[:, 16:32], cc(16), A.is_equal, 65535.0, A.mult),
+        lambda: ts(["ones", "c16"], ["lane"], T.lane[:], T.ones[:, 0:18], cc(16), A.mult),
+        lambda: tt(["d16a", "d16b"], ["d16"], T.d16[:, 32:48], T.d16[:, 0:16], T.d16[:, 16:32], A.add),
+        lambda: ts(["c16"], ["c19"], cc(19), cc(16), 15.0, A.is_equal, 2.0 ** -16, A.max),
+        lambda: ts(["c16"], ["c20"], cc(20), cc(16), 15.0, A.is_equal, 2.0 ** -32, A.max),
+        lambda: ts(["pI"], ["ph"], T.ph[:], T.pI[:], 0.5, A.mult),
+    ]
 
     left = [0]
     for r in range(3):
         partner = T.cores[rank ^ STEP[r]]
         data, lst = relays(core, partner, topo)
-        q, qp, p = "q%d" % r, "qp%d" % r, "pr%d" % r
-        need("g", wr[q])
+        q, qp = "q%d" % r, "qp%d" % r
+        both = [q + "a", q + "b"]
+        need("g", wr[q + "a"] + wr[q + "b"])
         fc, fs = [], []
         for k, c in enumerate(data):
             es = topo.engines(core, c)
             es = es[k * len(es) // 2:(k + 1) * len(es) // 2]
             rid, pid = topo.addr(c, core)
-            a, b = k * HALF, (k + 1) * HALF
+            a0, b0 = k * HALF, (k + 1) * HALF
             fc.append(RemoteDMATransfer(dst_ids=[DstId(rid=rid, pnc=pid)], dma_engine_mask=bits(es), remote_sem=T.sem["rc%d" % r],
-                                        src=T[q][:, a:b].bitcast(dt.uint8), dst=T["aq%d" % r][:, a:b].bitcast(dt.uint8)))
+                                        src=T[q][:, a0:b0].bitcast(dt.uint8), dst=T["aq%d" % r][:, a0:b0].bitcast(dt.uint8)))
             fs.append(RemoteDMATransfer(dst_ids=[DstId(rid=rid, pnc=pid)], dma_engine_mask=bits(es), remote_sem=T.sem["rs%d" % r],
-                                        src=T[qp][:, a:b], dst=T["ap%d" % r][:, a:b]))
+                                        src=T[qp][:, a0:b0], dst=T["ap%d" % r][:, a0:b0]))
             left[0] += 2 * len(es)
         g.remote_dma_fused(fc, local_sem=T.sem.left)
         g.remote_dma_fused(fs, local_sem=T.sem.left)
-        for w in range(3):
-            mm([q, qp, "u3q", "u3p"], w, T.u3q[:, 128 * w:128 * w + 128], T.u3p[:, 128 * w:128 * w + 128], T[q][:], T[qp][:])
 
         def own_f(b):
-            mm([q, qp, "eq%d" % b], 3 + b, T.eq[:, 128 * b:128 * b + 128], T.ep[:, 128 * b:128 * b + 128], T[q][:], T[qp][:])
+            mm(both + ["eq%d" % b], 3 + b, T.eq[:, 128 * b:128 * b + 128], T.ep[:, 128 * b:128 * b + 128], q, qp)
 
-        for b in range(4 if r else 2):
-            own_f(b)
+        def first_scores():
+            mm(both + ["u2q", "u2p"], 2, T.u2q[:], T.u2p[:], q, qp)
 
-        def signs(w):
-            act(["ps%d" % w, "c%d" % (8 + w), "c%d" % (12 + w)], ["w%d" % (w + 1)], T["w%d" % (w + 1)][:], T["ps%d" % w][:, 0:C], F.Sign, scale=cc(8 + w), bias=cc(12 + w))
+        def keep_f(b):
+            act(["ps%d" % (3 + b)], ["fo%d" % b], T["fo%d" % b][:], T["ps%d" % (3 + b)][:, 0:C])
 
-        def meanwhile(t):
-            if t == 0:
-                signs(1)
-            elif t == 1:
-                act(["ps2", "c14"], ["wg"], T.wg[:], T.ps2[:, 0:C], F.Sign, bias=cc(14))
-            elif t in (2, 3, 7, 8):
-                b = (2, 3, 7, 8).index(t)
-                act(["ps%d" % (3 + b)], ["fo%d" % b], T["fo%d" % b][:], T["ps%d" % (3 + b)][:, 0:C])
-            elif t == 4:
-                ends()
-
-        signs(0)
-        def differ():
-            tt([p, "pd1", "m2"], ["pd0"], T.pd[:, 0:2 * C:2], T[p][:].indirect(T.m2[:]), T.pd[:, 1:2 * C:2], A.subtract)
-
+        for h in range(2):
+            mm([both[h], "u1q", "u1p"], h, T.u1q[:], T.u1p[:], q, qp, h * HALF, (h + 1) * HALF)
         if r:
-            differ()
-        far = ["far%d%d" % (a, b) for b in range(4) for a in range(b)]
-        scan = lambda out, d0, d1: (lambda: g.vector.tensor_tensor_scan(out, d0, d1, 0.0, A.mult, A.add))
-        op("v", ["cg0", "cg1", "cg2", "cg3", "tab"] + far, ["sc0"], scan(T.sc0[:], T.cg[:], T.tab[:, 0:BLK]))
-        ts(["sc0"], ["of0"], T.of0[:], T.sc0[:, 3:BLK:4], BIAS, A.add)
-        for t in range(7):
-            i, j = t % 2, (t + 1) % 2
-            w, lane = "w%d" % (1 + t // 4), t % 4
-            gg, gt = "gg%d" % i, "gt%d" % i
-            cp([w, "of%d" % i], [gg], T[gg][:, 32:128], T[w][:].indirect(T["of%d" % i][:, 0:6]))
-            act([w, "of%d" % i], [gg + "s"], T[gg][:, 128:192], T[w][:].indirect(T["of%d" % i][:, 6:10]))
-            if t < 4:
-                tail(2 * t)
-            op("v", [gg, gg + "s"], [gt], lambda: g.vector.transpose(T[gt][:, 0:160], T[gg][:, 32:192]))
-            if t < 4:
-                tail(2 * t + 1)
-            elif r == 0 and t < 6:
+            first_scores()
+            for b_ in range(4):
+                own_f(b_)
+        for h in range(2):
+            act(["ps%d" % h, "c13", "c14"], ["w" + "ab"[h]], T.w[:, h * HALF:(h + 1) * HALF], T["ps%d" % h][:, 0:HALF], F.Sign, scale=cc(13), bias=cc(14))
+
+        def vector_fill(t, k):
+            if (t, k) == (0, 0):
+                table(1)
+            elif r:
+                return
+            elif (t, k) == (1, 0):
+                cp(["uq", "ull2"], ["u2q"], T.u2q[:].bitcast(dt.uint32), T.uq[:].bitcast(dt.uint32).indirect(T.ull[:, 8:16]))
+            elif k == 0 and t in (2, 3, 4, 5):
                 unit(t - 2)
                 own_f(t - 2)
-            meanwhile(t)
-            d1 = ["tab%d" % k for k in range(8)] + ["tab"] + far
-            if t < 5:
-                op("v", [gt] + d1, ["sc%d" % j], scan(T["sc%d" % j][:], T[gt][:, lane:160:4], T.tab[:, BLK * (t + 1):BLK * (t + 2)]))
-                ts(["sc%d" % j], ["of%d" % j], T["of%d" % j][:], T["sc%d" % j][:, 3:BLK:4], BIAS, A.add)
-            elif t == 5:
-                op("v", [gt] + d1, ["s5"], scan(T.s5[:], T[gt][:, lane:160:4], T.tab[:, 6 * BLK:7 * BLK]))
-                op("v", [gg, gg + "s", gg + "a", gg + "b"], [gt + "b"], lambda: g.vector.transpose(T[gt][:, 160:352], T[gg][:, 16:208]))
-                ts(["s5"], ["of0"], T.of0[:], T.s5[:, 3:BLK:4], BIAS, A.add)
-                op("v", [gt + "b", "tb6"] + ["tb6_%d" % k for k in range(4)], ["s5b"], scan(T.s5b[:], T[gt][:, 160 + lane:352:4], T.tb6[:]))
+            elif later:
+                later.pop(0)()
+
+        def scalar_fill(t):
+            if r == 0 and t == 0:
+                act(["up", "ull2"], ["u2p"], T.u2p[:], T.up[:].indirect(T.ull[:, 8:16]))
+            elif r == 0 and t == 1:
+                act(["prow", "mls"], ["mrow"], T.mrow[:], T.prow[:].indirect(T.mls[:]))
+                first_scores()
+            elif r == 0 and t == 4:
+                act(["d16", "lane"], ["own"], T.own[:], T.d16[:, 32:48].indirect(T.lane[:]))
+            if t == (0 if r else 2):
+                act(["ps2", "c17"], ["wg"], T.wg[:], T.ps2[:, 0:C], F.Sign, bias=cc(17))
+            if t == 3:
+                act(["bit", "tabA", "tabB"], ["tf"], T.tf[:], T.tab[:, 0:2 * C:2], scale=b(4))
+            if r and t in (1, 2, 4):
+                keep_f((1, 2, 4).index(t))
+            if r == 0 and t == 6:
+                keep_f(0)
+
+        table(0)
+        tabA = T.tab[:, 0:320:2]
+        scan(["gt1", "tabA"], ["sc1"], T.sc1[:], T.gt1[:, 0:ROW], tabA)
+        ts(["sc1", "of"], ["of0"], T.of[0:32, 0:ENT], T.sc1[0:32, 7:ROW:16], BIAS, A.add)
+        for t in range(7):
+            i, a = t % 2, (t + 1) // 2
+            gg, gt, sc, o = "gg%d" % i, "gt%d" % i, "sc%d" % i, ENT * i
+            cp(["wa", "wb", "of", "of%d" % i], [gg], T[gg][:, 32:32 + 16 * CUT], T.w[:].indirect(T.of[:, o:o + CUT]))
+            if t == 6:
+                act(["sc1", "nb"], ["pm0"], T.pm[:, 0:10:2], T.sc1[:, 23:ROW:32], scale=nb(4))
+                act(["sc1", "nb"], ["pm1"], T.pm[:, 10:18:2], T.sc1[:, 7:128:32], scale=nb(4))
+            act(["wa", "wb", "of", "of%d" % i], [gg + "s"], T[gg][:, 32 + 16 * CUT:192], T.w[:].indirect(T.of[:, o + CUT:o + ENT]))
+            vector_fill(t, 0)
+            if t == 6:
+                act(["s5b", "nb"], ["pm2"], T.pm[:, 1:10:2], T.s5b[:, 39:176:32], scale=nb(4))
+                act(["s5b", "nb"], ["pm3"], T.pm[:, 11:18:2], T.s5b[:, 23:128:32], scale=nb(4))
+            turn([gg, gg + "s"], [gt], T[gt][:, 0:ROW], T[gg][:, 32:192])
+            vector_fill(t, 1)
+            scalar_fill(t)
+            if t < 6:
+                scan([gt, "tabA"], [sc], T[sc][:], T[gt][:, 0:ROW], tabA)
+                if t == 5:
+                    turn([gg, gg + "s", gg + "a", gg + "b"], [gt + "b"], T[gt][:, 160:352], T[gg][:, 16:208])
+                else:
+                    vector_fill(t, 2)
+                if i:
+                    ts([sc], ["of0"], T.of[32 * a:32 * a + 32, 0:ENT], T[sc][32 * a:32 * a + 32, 7:ROW:16], BIAS, A.add)
+                else:
+                    ts([sc], ["of1"], T.of[32 * a + 32:32 * a + 64, ENT:2 * ENT], T[sc][32 * a:32 * a + 32, 15:ROW:16], BIAS, A.add)
+                if t == 5:
+                    scan([gt + "b", "tabB"], ["s5b"], T.s5b[:], T[gt][:, 176:352], T.tab[:, 320:672:2])
             else:
-                act(["s5", "c3"], ["pm0"], T.pm[:, 0:10:2], T.s5[:, 7:40:8], scale=cc(3))
-                act(["s5", "c3"], ["pm1"], T.pm[:, 10:18:2], T.s5[:, 3:32:8], scale=cc(3))
-                act(["s5b", "c3"], ["pm2"], T.pm[:, 1:10:2], T.s5b[:, 15:48:8], scale=cc(3))
-                act(["s5b", "c3"], ["pm3"], T.pm[:, 11:18:2], T.s5b[:, 11:36:8], scale=cc(3))
-                op("v", [gg, gg + "s", gg + "a", gg + "b"], [gt + "b"], lambda: g.vector.transpose(T[gt][:, 160:352], T[gg][:, 16:208]))
-                op("v", [gt, gt + "b", "tfa", "tfb"], ["s6"], scan(T.s6[:], T[gt][:, lane:352:4], T.tf[:]))
+                turn([gg, gg + "s", gg + "a", gg + "b"], [gt + "b"], T[gt][:, 160:352], T[gg][:, 16:208])
+                tt(["tf", "pm0", "pm1", "pm2", "pm3"], ["tf"], T.tf[:, 15:C:16], T.tf[:, 15:C:16], T.pm[:], A.add)
+                scan([gt, gt + "b", "tf"], ["s6"], T.s6[:], T[gt][:, 0:C], T.tf[:])
         ll = "ll%d" % r
-        tt(["s6", "pm0", "pm1", "pm2", "pm3"], ["l32"], T.l32[:], T.s6[:, 3:72:4], T.pm[:], A.add)
-        ts(["l32"], [ll], T[ll][:], T.l32[:], BIAS, A.add)
+        ts(["s6"], [ll], T[ll][:], T.s6[:, 15:C:16], BIAS, A.add)
         need("g", wr[ll])
         rid, pid = topo.addr(lst, core)
         es = topo.engines(core, lst)
         g.remote_dma(T["al%d" % r][:], T[ll][:], T.sem["rL%d" % r], T.sem.left, pid, rid, bits(es))
         left[0] += len(es)
-        np_ = "pr%d" % (r + 1)
-        act(["wg", ll], ["be2"], T.be2[:], T.wg[:].indirect(T[ll][:]))
-        meanwhile(7)
-        meanwhile(8)
-        cp(["wg", ll], ["be"], T.be[:], T.wg[:].indirect(T[ll][:]))
+        pn = "pls%d" % (r + 1)
         if r == 0:
-            differ()
-        tt(["be", "be2", "mls"], ["ne1"], T.ne2[:, 1:2 * C:2], T.be[:].indirect(T.mls[:]), T.be2[:], A.not_equal)
-        op("v", ["ne0", "ne1", "pd0", "pd1"], [np_], scan(T[np_][:], T.ne2[:], T.pd[:]))
+            scan(["own", "mrow"], ["ms"], T.ms[:], T.own[:], T.mrow[:])
+        shared(("wg", ["wg"]), ll, "be")
+        if r == 0:
+            ts(["ms", "c19"], ["mh"], T.mh[:], T.ms[:, 15:C:16], cc(19), A.mult, ROUND, A.add)
+            ts(["mh"], ["mh"], T.mh[:], T.mh[:], BIAS - ROUND, A.add, 0.5, A.mult)
+        shared(("be", ["bea", "beb"]), "mls", "bm")
+        if r == 0:
+            tt(["mh", "ph", "ex"], ["avg"], T.ex[:, 2:54:3], T.ph[:], T.mh[:], A.add)
+        scan(["own", "bea", "beb"], ["hs1"], T.hs[:, 2:2 + 3 * C:3], T.own[:], T.be[:])
+        if r == 0:
+            scaled = spread("pI", T.pI[:])
+        scan(["own", "bma", "bmb"], ["hs2"], T.hs[:, 18:880:3], T.own[:], T.bm[:])
+        if r == 0:
+            scaled()
+        scan(["hs0", "hs1", "hs2", "ex", "avg", "hdl"], ["pn"], T.pn[:], T.hs[:, 31:880:16], T.ex[:])
+        cp(["pn"], [pn], T[pn][:], T.pn[:, 2:54:3])
         if r < 2:
-            powers(r + 1)
-        else:
-            cp(["idr", ll], ["lo"], T.lo[:], T.idr[:].indirect(T[ll][:]))
-            quant(["vt"], ["vq"], T.vq[:], T.vp[:], T.vt[:])
-            ts(["lo"], ["lo"], T.lo[:], T.lo[:], 4.0, A.mult, BIAS, A.add)
-            ts([np_], ["po"], T.po[:], T[np_][:, 1:2 * C:2], 4.0, A.mult, BIAS, A.add)
-            dma("s", "out", 8, ["lo"], ["pl0"], T.pl[:, 0:C], T.lo[0:128:16, :])
-            dma("s", "out", 8, ["po"], ["pl1"], T.pl[:, C:2 * C], T.po[0:128:16, :])
+            scaled = spread("pn", T.pn[:, 2:54:3])
         wr["aq"] = [("aq_%d" % r, sum(2 * len(topo.engines(c, core)) for c in relays(partner, core, topo)[0]))]
         wr["al"] = [("aL_%d" % r, len(topo.engines(relays(partner, core, topo)[1], core)))]
         count["aq_%d" % r], count["aL_%d" % r] = wr["aq"][0][1], wr["al"][0][1]
-        for b in range(4):
-            mm(["aq", "eq%d" % b], (7 + b) % 8, T.eq[:, 128 * b:128 * b + 128], T.ep[:, 128 * b:128 * b + 128], T["aq%d" % r][:], T["ap%d" % r][:])
-        for b in range(4):
-            act(["ps%d" % ((7 + b) % 8)], ["fp%d" % b], T["fp%d" % b][:], T["ps%d" % ((7 + b) % 8)][:, 0:C])
+        for b_ in range(4):
+            mm(["aq", "eq%d" % b_], (7 + b_) % 8, T.eq[:, 128 * b_:128 * b_ + 128], T.ep[:, 128 * b_:128 * b_ + 128], "aq%d" % r, "ap%d" % r)
+        for b_ in range(4):
+            act(["ps%d" % ((7 + b_) % 8)], ["fp%d" % b_], T["fp%d" % b_][:], T["ps%d" % ((7 + b_) % 8)][:, 0:C])
+        for b_ in range(1 if r == 0 else 3, 4):
+            keep_f(b_)
+        if r < 2:
+            power(r + 1, 0)
+            scaled()
+            power(r + 1, 1)
+        else:
+            quant(["vt"], ["vq"], T.vq[:], T.vp[:], T.vt[:])
+            ts(["idr", ll], ["lo0"], T.lo[:, 0:C], T.idr[:].indirect(T[ll][:]), BIAS, A.add)
+            ts(["idr", pn], ["lo1"], T.lo[:, C:2 * C], T.idr[:].indirect(T[pn][:]), BIAS, A.add)
+            dma("s", "out", 7, ["lo0", "lo1"], ["pl"], T.pl[:], T.lo[0:128:16, :])
         al, zt = T["al%d" % r], T.zt
-        for b in (0, 2, 1, 3):
-            if b < 2:
-                cp(["fp%d" % b, "al"], ["zt%d" % b], zt[:, b:4 * C:4], T["fp%d" % b][:].indirect(al[:]))
-            else:
-                act(["fp%d" % b, "al"], ["zt%d" % b], zt[:, b:4 * C:4], T["fp%d" % b][:].indirect(al[:]))
-        quant(["zt%d" % b for b in range(4)], ["zq"], T.zq[:], T.zp[:], zt[:])
+        for b_ in (0, 2, 1, 3):
+            (cp if b_ < 2 else act)(["fp%d" % b_, "al"], ["zt%d" % b_], zt[:, b_:4 * C:4], T["fp%d" % b_][:].indirect(al[:]))
+        halves(["zt%d" % b_ for b_ in range(4)], "zq", "zp", "zt")
         if r < 2:
-            rows(3, np_, "tl2", "a")
-            tables(r + 1)
-        for b in range(4):
-            mm(["zq", "wq", "wp"], 3 + b, T.wq[:, 128 * b:128 * b + 128], T.wp[:, 128 * b:128 * b + 128], T.zq[:], T.zp[:])
+            power(r + 1, 2)
+        for h in range(2):
+            mm(["zq" + "ab"[h], "wq", "wp"], 3 + 4 * h, T.wq[:, 0:128], T.wp[:, 0:128], "zq", "zp", h * HALF, (h + 1) * HALF)
+        for b_ in range(1, 4):
+            mm(["zqa", "zqb", "wq", "wp"], 3 + b_, T.wq[:, 128 * b_:128 * b_ + 128], T.wp[:, 128 * b_:128 * b_ + 128], "zq", "zp")
         xn = T["xn%d" % r]
-        for b in range(4):
-            act(["ps%d" % (3 + b)], ["hb%d" % b], T["hb%d" % b][:], T["ps%d" % (3 + b)][:, 0:C], scale=0.03125)
-            tt(["hb%d" % b, "fo%d" % b, ll], ["xn%d" % b], xn[:, b:4 * C:4], T["hb%d" % b][:].indirect(T[ll][:]), T["fo%d" % b][:], A.add)
+        for b_ in range(4):
+            hb = "hb%d" % b_
+            if b_ == 0:
+                for h in range(2):
+                    act(["ps%d" % (3 + 4 * h)], [hb + "ab"[h]], T[hb][:, h * HALF:(h + 1) * HALF], T["ps%d" % (3 + 4 * h)][:, 0:HALF], scale=0.03125)
+            else:
+                act(["ps%d" % (3 + b_)], [hb + "a", hb + "b"], T[hb][:], T["ps%d" % (3 + b_)][:, 0:C], scale=0.03125)
+            tt([hb + "a", hb + "b", "fo%d" % b_, ll], ["xn%d" % b_], xn[:, b_:4 * C:4], T[hb][:].indirect(T[ll][:]), T["fo%d" % b_][:], A.add)
         if r < 2:
-            act([np_], ["pd1"], T.pd[:, 1:2 * C:2], T[np_][:, 1:2 * C:2])
-        nq, nqp = "q%d" % (r + 1), "qp%d" % (r + 1)
-        quant(["xn%d" % b for b in range(4)], [nq, nqp], T[nq][:], T[nqp][:], xn[:])
-    mm(["q3", "qp3", "vq"], 7, T.vq[:], T.vp[:], T.q3[:], T.qp3[:])
-    dma("s", "out", 8, ["q3"], ["oc"], T.oc[:], T.q3[:].bitcast(dt.uint8))
+            starts(0)
+        halves(["xn%d" % b_ for b_ in range(4)], "q%d" % (r + 1), "qp%d" % (r + 1), "xn%d" % r)
+    for h in range(2):
+        mm(["q3" + "ab"[h], "vq"], h, T.vq[:], T.vp[:], "q3", "qp3", h * HALF, (h + 1) * HALF)
+    dma("s", "out", 7, ["q3a", "q3b"], ["oc"], T.oc[:], T.q3[:].bitcast(dt.uint8))
     for k in range(4):
-        dma("s" if k % 2 else "a", "out", 8, ["qp3"], ["osc%d" % k], T.osc[4 * k:4 * k + 4, :], T.qp3[32 * k:32 * k + 4, :])
-    act(["ps7"], ["yo"], T.yo[:], T.ps7[:, 0:C])
-    dma("s", "out", 8, ["yo"], ["y"], T.y[:], T.yo[:])
+        dma("s", "out", 7, ["q3a", "q3b"], ["osc%d" % k], T.osc[4 * k:4 * k + 4, :], T.qp3[32 * k:32 * k + 4, :])
+    for h in range(2):
+        act(["ps%d" % h], ["yo%d" % h], T.yo[:, h * HALF:(h + 1) * HALF], T["ps%d" % h][:, 0:HALF])
+    dma("a", "out", 7, ["yo0", "yo1"], ["y"], T.y[:], T.yo[:])
     g.wait_ge(T.sem.left, left[0])
     for s in sorted(count):
         g.wait_ge(T.sem[s], count[s])

@@ -7,7 +7,8 @@ STEP = [4, 1, 2]
 HALF = C // 2
 ENT = 10
 ROW = 16 * ENT
-CUT = 6
+RUNS = ((0, 160), (160, C))
+CHAIN = ((("s", 6, ENT), ("v", 0, 6)), (("s", 0, 4), ("v", 4, 8), ("t", 8, ENT)))
 BIAS = 144.0
 
 SCRATCH = {
@@ -30,10 +31,11 @@ SCRATCH = {
     "mls": ("sbuf", [128, 18], "uint16"), "k20": ("sbuf", [128, 20], "uint16"),
     "kf": ("sbuf", [128, 18], "float32"), "ke": ("sbuf", [128, 40], "float32"),
     "y1": ("sbuf", [128, C], "bfloat16"), "y2": ("sbuf", [128, C], "bfloat16"), "y3": ("sbuf", [128, C], "bfloat16"),
-    "tr": ("sbuf", [128, 368], "bfloat16"), "tab": ("sbuf", [128, 672], "bfloat16"), "tf": ("sbuf", [128, C], "bfloat16"),
+    "tr": ("sbuf", [128, 368], "bfloat16"), "tab": ("sbuf", [128, 672], "bfloat16"), "tf": ("sbuf", [128, 512], "bfloat16"),
     "w": ("sbuf", [128, C], "bfloat16"), "wg": ("sbuf", [128, C], "bfloat16"),
     "of": ("sbuf", [128, 2 * ENT], "uint16"),
-    "s5b": ("sbuf", [128, 176], "bfloat16"), "s6": ("sbuf", [128, C], "bfloat16"), "pm": ("sbuf", [128, 18], "bfloat16"),
+    "sc0": ("sbuf", [128, ROW], "bfloat16"), "sc1": ("sbuf", [128, 624], "bfloat16"),
+    "po": ("sbuf", [128, 6], "float32"), "pmo": ("sbuf", [128, 2], "uint16"),
     "be": ("sbuf", [128, C], "bfloat16"), "bm": ("sbuf", [128, C], "bfloat16"), "hs": ("sbuf", [128, 880], "bfloat16"),
     "prow": ("sbuf", [128, C], "bfloat16"), "mrow": ("sbuf", [128, C], "bfloat16"), "ms": ("sbuf", [128, C], "float32"),
     "ex": ("sbuf", [128, 54], "float32"), "pn": ("sbuf", [128, 54], "float32"), "hd": ("sbuf", [128, 18], "float32"),
@@ -43,7 +45,6 @@ SCRATCH = {
 for _i in range(2):
     SCRATCH["gg%d" % _i] = ("sbuf", [128, 208], "bfloat16")
     SCRATCH["gt%d" % _i] = ("sbuf", [128, 352], "bfloat16")
-    SCRATCH["sc%d" % _i] = ("sbuf", [128, ROW], "bfloat16")
 for _i in range(4):
     SCRATCH["dg%d" % _i] = ("sbuf", [128, C], "bfloat16")
     SCRATCH["pls%d" % _i] = ("sbuf", [128, 18], "uint16")
@@ -58,7 +59,7 @@ for _i in range(3):
     SCRATCH["xn%d" % _i] = ("sbuf", [128, 4 * C], "bfloat16")
     SCRATCH["aq%d" % _i] = ("sbuf", [128, C], "float8_e4m3fn_x4")
     SCRATCH["ap%d" % _i] = ("sbuf", [128, C], "uint8")
-    SCRATCH["ll%d" % _i] = ("sbuf", [128, 18], "uint16")
+    SCRATCH["ll%d" % _i] = ("sbuf", [128, 32], "uint16")
     SCRATCH["al%d" % _i] = ("sbuf", [128, 18], "uint16")
 
 SEMAPHORES = ["sv", "sa", "st", "sg", "left",
@@ -185,8 +186,8 @@ def rank_program(g, core, T, topo):
         op("t", reads, ["ps%d" % bank], lambda: g.tensor.matmul_mx(T["ps%d" % bank][:, 0:b - a], lhs, lhsp, T[q][:, a:b], T[p][:, a:b], True, True))
 
     def halves(reads, q, p, t):
-        for h in range(2):
-            quant(reads, [q + "ab"[h]], T[q][:, h * HALF:(h + 1) * HALF], T[p][:, h * HALF:(h + 1) * HALF], T[t][:, 4 * h * HALF:4 * (h + 1) * HALF])
+        for h, (a, b) in enumerate(RUNS):
+            quant([k + "ab"[h] for k in reads], [q + "ab"[h]], T[q][:, a:b], T[p][:, a:b], T[t][:, 4 * a:4 * b])
 
     def quant(reads, writes, q, p, t):
         op("v", reads, writes, lambda: g.vector.quantize_mx(q, p, t))
@@ -279,35 +280,35 @@ def rank_program(g, core, T, topo):
     act(["kf", "bit", "ke"], ["ko0"], T.ke[:, 20:35:2], T.kf[:, 10:18], scale=b(4))
     ts(["nb"], ["c5"], cc(5), nb(0), nb(1), A.mult, nb(2), A.mult)
     ts(["nb"], ["c6"], cc(6), nb(3), nb(5), A.mult, nb(6), A.mult)
-    power(0, 1)
     ts(["nb", "bit"], ["c7"], cc(7), nb(0), nb(1), A.mult, b(2), A.mult)
-    tt(["ke0", "ke1", "ke2", "ke3", "ko0", "ko1"], ["ke"], T.ke[:, 0:20], T.ke[:, 0:20], T.ke[:, 20:40], A.add)
-    quant(["xt"], ["q0a", "q0b"], T.q0[:], T.qp0[:], T.xt[:])
-    power(0, 2)
-    cp(["ke"], ["k20"], T.k20[:], T.ke[:, 0:20])
-    ts(["bit", "c7"], ["c15"], cc(15), b(3), 16.0, A.mult, cc(7), A.add)
-    act(["nb", "c5"], ["c8"], cc(8), cc(5), F.Identity, scale=-1.0, bias=nb(0))
-    act(["c5"], ["c9"], cc(9), cc(5), F.Identity, scale=-1.0, bias=T.ones[:, 0:1])
-    act(["c6"], ["c10"], cc(10), cc(6), F.Identity, scale=-1.0, bias=T.ones[:, 0:1])
+    power(0, 1)
+    line = lambda key, x, s, c: act(["nb", "bit", "ones"] + ["c%d" % i for i in (x, s, c) if i in range(32)], ["c%d" % key], cc(key), cc(x), F.Identity,
+                                    scale=cc(s) if s in range(32) else s[0], bias=cc(c) if c in range(32) else c[0])
+    plain("gt1v", T.gt1[:, 0:ROW], ROW, 1.0)
+    act(["bit", "c7"], ["c15"], cc(15), b(3), F.Identity, scale=16.0, bias=cc(7))
+    line(8, 5, [-1.0], [nb(0)])
+    line(10, 6, [-1.0], [T.ones[:, 0:1]])
+    plain("gt1v", T.gt1[:, 0:ROW:8], 2 * ENT, 0.0)
+    line(9, 7, [-2.0], 8)
+    act(["c8", "c10"], ["c13"], cc(13), cc(8), scale=cc(10))
+    plain("gt1s", T.gt1[:, 4:ROW:16], ENT, -1.0)
+    line(11, 9, 6, [b(0)])
     plain("c17", cc(17), 1, -1e-29)
-    plain("c18", cc(18), 1, BIAS)
     for i in range(2):
         plain("gg%da" % i, T["gg%d" % i][:, 16:32], 16, 0.0)
         plain("gg%db" % i, T["gg%d" % i][:, 192:208], 16, 0.0)
-    plain("gt1", T.gt1[:, 0:ROW], ROW, 1.0)
-    plain("gt1", T.gt1[:, 0:ROW:8], 2 * ENT, 0.0)
-    plain("gt1", T.gt1[:, 4:ROW:16], ENT, -1.0)
+    line(14, 13, [-1e-29], 11)
     act(["idr", "pls0"], ["prow"], T.prow[:], T.idr[:].indirect(T.pls0[:]))
+    quant(["xt"], ["q0a", "q0b"], T.q0[:], T.qp0[:], T.xt[:])
+    tt(["ke0", "ke1", "ke2", "ke3", "ko0", "ko1"], ["ke"], T.ke[:, 0:20], T.ke[:, 0:20], T.ke[:, 20:40], A.add)
     ts(["ulf", "c15"], ["ull"], T.ull[:, 0:8], T.ulf[:, 0:8], cc(15), A.add, 0.0, A.max)
+    power(0, 2)
+    cp(["ke"], ["k20"], T.k20[:], T.ke[:, 0:20])
     quant(["ut"], ["uq", "up"], T.uq[:], T.up[:], T.ut[:])
-    ts(["c8", "c10"], ["c13"], cc(13), cc(8), cc(10), A.mult)
-    ts(["c7", "c6"], ["c11"], cc(11), cc(7), cc(6), A.mult, -2.0, A.mult)
-    cp(["uq", "ull"], ["u1q"], T.u1q[:].bitcast(dt.uint32), T.uq[:].bitcast(dt.uint32).indirect(T.ull[:, 0:8]))
-    act(["up", "ull"], ["u1p"], T.u1p[:], T.up[:].indirect(T.ull[:, 0:8]))
-    ts(["c11", "c9", "c13"], ["c12"], cc(12), cc(11), cc(9), A.add, cc(13), A.subtract)
     cp(["ulf2"], ["ull2"], T.ull[:, 8:16], T.ulf[:, 8:16])
+    act(["up", "ull"], ["u1p"], T.u1p[:], T.up[:].indirect(T.ull[:, 0:8]))
+    cp(["uq", "ull"], ["u1q"], T.u1q[:].bitcast(dt.uint32), T.uq[:].bitcast(dt.uint32).indirect(T.ull[:, 0:8]))
     starts(10)
-    ts(["c12", "c9"], ["c14"], cc(14), cc(12), -1e-29, A.add, cc(9), A.mult)
 
     def unit(b):
         quant(["e0"], ["eq%d" % b], T.eq[:, 128 * b:128 * b + 128], T.ep[:, 128 * b:128 * b + 128], T.e0[:, 3 - b:515 - b])
@@ -324,13 +325,23 @@ def rank_program(g, core, T, topo):
     later = [
         lambda: cp(["mI"], ["mls"], T.mls[:], T.mI[:]),
         lambda: cp(["bj7"], ["c16"], cc(16), T.bj[:, 7:8]),
+        lambda: ts(["pI"], ["ph"], T.ph[:], T.pI[:], 0.5, A.mult),
+        lambda: ts(["bit"], ["c21"], cc(21), b(0), 160.0, A.mult, 7.0, A.add),
         lambda: ts(["lor", "c16"], ["d16a"], T.d16[:, 0:16], T.lor[:, 0:16], cc(16), A.not_equal),
         lambda: ts(["lor", "c16"], ["d16b"], T.d16[:, 16:32], T.lor[:, 16:32], cc(16), A.is_equal, 65535.0, A.mult),
         lambda: ts(["ones", "c16"], ["lane"], T.lane[:], T.ones[:, 0:18], cc(16), A.mult),
         lambda: tt(["d16a", "d16b"], ["d16"], T.d16[:, 32:48], T.d16[:, 0:16], T.d16[:, 16:32], A.add),
         lambda: ts(["c16"], ["c19"], cc(19), cc(16), 15.0, A.is_equal, 2.0 ** -16, A.max),
         lambda: ts(["c16"], ["c20"], cc(20), cc(16), 15.0, A.is_equal, 2.0 ** -32, A.max),
-        lambda: ts(["pI"], ["ph"], T.ph[:], T.pI[:], 0.5, A.mult),
+        lambda: ts(["c16"], ["po0"], T.po[:, 0:1], cc(16), 10.0, A.is_ge, -176.0, A.mult),
+        lambda: ts(["c16"], ["po2"], T.po[:, 2:4], T.lor[:, 1:7:5], cc(16), A.add, 16.0, A.mult),
+        lambda: tt(["po0", "po2"], ["po2"], T.po[:, 2:3], T.po[:, 2:3], T.po[:, 0:1], A.add),
+        lambda: ts(["c16"], ["po4"], T.po[:, 4:6], T.lor[:, 0:17:16], cc(16), A.add, 16.0, A.mult),
+        lambda: ts(["po2", "c21", "nb"], ["po2"], T.po[:, 2:4], T.po[:, 2:4], cc(21), A.add, nb(4), A.mult),
+        lambda: ts(["po4"], ["po5"], T.po[:, 5:6], T.po[:, 5:6], 272.0, A.add, 272.0, A.min),
+        lambda: ts(["po4", "po5", "bit"], ["po4"], T.po[:, 4:6], T.po[:, 4:6], 351.0, A.add, b(4), A.mult),
+        lambda: tt(["po2", "po4"], ["po2"], T.po[:, 2:4], T.po[:, 2:4], T.po[:, 4:6], A.add),
+        lambda: cp(["po2"], ["pmo"], T.pmo[:], T.po[:, 2:4]),
     ]
 
     left = [0]
@@ -363,26 +374,29 @@ def rank_program(g, core, T, topo):
         def keep_f(b):
             act(["ps%d" % (3 + b)], ["fo%d" % b], T["fo%d" % b][:], T["ps%d" % (3 + b)][:, 0:C])
 
-        for h in range(2):
-            mm([both[h], "u1q", "u1p"], h, T.u1q[:], T.u1p[:], q, qp, h * HALF, (h + 1) * HALF)
+        for h, (a0, b0) in enumerate(RUNS):
+            mm([both[h], "u1q", "u1p"], h, T.u1q[:], T.u1p[:], q, qp, a0, b0)
         if r:
             first_scores()
             for b_ in range(4):
                 own_f(b_)
-        for h in range(2):
-            act(["ps%d" % h, "c13", "c14"], ["w" + "ab"[h]], T.w[:, h * HALF:(h + 1) * HALF], T["ps%d" % h][:, 0:HALF], F.Sign, scale=cc(13), bias=cc(14))
+        for h, (a0, b0) in enumerate(RUNS):
+            act(["ps%d" % h, "c13", "c14"], ["w" + "ab"[h]], T.w[:, a0:b0], T["ps%d" % h][:, 0:b0 - a0], F.Sign, scale=cc(13), bias=cc(14))
 
-        def vector_fill(t, k):
-            if (t, k) == (0, 0):
-                table(1)
-            elif r:
+        def vector_fill(t):
+            if r:
                 return
-            elif (t, k) == (1, 0):
+            if t == 0:
                 cp(["uq", "ull2"], ["u2q"], T.u2q[:].bitcast(dt.uint32), T.uq[:].bitcast(dt.uint32).indirect(T.ull[:, 8:16]))
-            elif k == 0 and t in (2, 3, 4, 5):
-                unit(t - 2)
-                own_f(t - 2)
-            elif later:
+                first_scores()
+            elif t == 1:
+                table(1)
+            elif t < 5:
+                unit(max(t - 1, 0))
+                own_f(max(t - 1, 0))
+
+        def small(e):
+            if later and e == "s":
                 later.pop(0)()
 
         def scalar_fill(t):
@@ -390,59 +404,65 @@ def rank_program(g, core, T, topo):
                 act(["up", "ull2"], ["u2p"], T.u2p[:], T.up[:].indirect(T.ull[:, 8:16]))
             elif r == 0 and t == 1:
                 act(["prow", "mls"], ["mrow"], T.mrow[:], T.prow[:].indirect(T.mls[:]))
-                first_scores()
-            elif r == 0 and t == 4:
+            elif r == 0 and t == 6:
                 act(["d16", "lane"], ["own"], T.own[:], T.d16[:, 32:48].indirect(T.lane[:]))
             if t == (0 if r else 2):
                 act(["ps2", "c17"], ["wg"], T.wg[:], T.ps2[:, 0:C], F.Sign, bias=cc(17))
-            if t == 3:
-                act(["bit", "tabA", "tabB"], ["tf"], T.tf[:], T.tab[:, 0:2 * C:2], scale=b(4))
-            if r and t in (1, 2, 4):
-                keep_f((1, 2, 4).index(t))
-            if r == 0 and t == 6:
-                keep_f(0)
+            if r and t in (1, 2, 3, 4):
+                keep_f(t - 1)
+            if r == 0 and t in (3, 4, 5):
+                keep_f(t - 3)
 
         table(0)
         tabA = T.tab[:, 0:320:2]
-        scan(["gt1", "tabA"], ["sc1"], T.sc1[:], T.gt1[:, 0:ROW], tabA)
-        ts(["sc1", "of"], ["of0"], T.of[0:32, 0:ENT], T.sc1[0:32, 7:ROW:16], BIAS, A.add)
+        if r:
+            table(1)
+        small("s")
+        small("s")
+        every = lambda k, c0=0, c1=ENT: [k + "_%d" % c for c in range(c0, c1, 2)]
+        scan(every("gt1") + ["gt1v", "gt1s", "tabA"], every("sc1"), T.sc1[:, 0:ROW], T.gt1[:, 0:ROW], tabA)
+        small("s")
+        small("s")
+        ts(every("sc1") + ["of"], every("of0"), T.of[0:32, 0:ENT], T.sc1[0:32, 7:ROW:16], BIAS, A.add)
+        vector_fill(-1)
+        runs = CHAIN[min(r, 1)]
         for t in range(7):
             i, a = t % 2, (t + 1) // 2
             gg, gt, sc, o = "gg%d" % i, "gt%d" % i, "sc%d" % i, ENT * i
-            cp(["wa", "wb", "of", "of%d" % i], [gg], T[gg][:, 32:32 + 16 * CUT], T.w[:].indirect(T.of[:, o:o + CUT]))
-            if t == 6:
-                act(["sc1", "nb"], ["pm0"], T.pm[:, 0:10:2], T.sc1[:, 23:ROW:32], scale=nb(4))
-                act(["sc1", "nb"], ["pm1"], T.pm[:, 10:18:2], T.sc1[:, 7:128:32], scale=nb(4))
-            act(["wa", "wb", "of", "of%d" % i], [gg + "s"], T[gg][:, 32 + 16 * CUT:192], T.w[:].indirect(T.of[:, o + CUT:o + ENT]))
-            vector_fill(t, 0)
-            if t == 6:
-                act(["s5b", "nb"], ["pm2"], T.pm[:, 1:10:2], T.s5b[:, 39:176:32], scale=nb(4))
-                act(["s5b", "nb"], ["pm3"], T.pm[:, 11:18:2], T.s5b[:, 23:128:32], scale=nb(4))
-            turn([gg, gg + "s"], [gt], T[gt][:, 0:ROW], T[gg][:, 32:192])
-            vector_fill(t, 1)
-            scalar_fill(t)
+            for e, c0, c1 in runs:
+                (cp if e == "v" else act)(["wa", "wb", "of"] + every("of%d" % i, c0, c1), every(gg, c0, c1), T[gg][:, 32 + 16 * c0:32 + 16 * c1],
+                                          T.w[:].indirect(T.of[:, o + c0:o + c1]))
             if t < 6:
-                scan([gt, "tabA"], [sc], T[sc][:], T[gt][:, 0:ROW], tabA)
+                for e, c0, c1 in runs:
+                    turn(every(gg, c0, c1), every(gt, c0, c1), T[gt][:, 16 * c0:16 * c1], T[gg][:, 32 + 16 * c0:32 + 16 * c1])
+                    small(e)
+                scalar_fill(t)
+                for e, c0, c1 in runs:
+                    scan(every(gt, c0, c1) + ["tabA"], every(sc, c0, c1), T[sc][:, 16 * c0:16 * c1], T[gt][:, 16 * c0:16 * c1], T.tab[:, 32 * c0:32 * c1:2])
+                    small(e)
+                for e, c0, c1 in runs:
+                    if i:
+                        ts(every(sc, c0, c1), every("of0", c0, c1), T.of[32 * a:32 * a + 32, c0:c1], T[sc][32 * a:32 * a + 32, 16 * c0 + 7:16 * c1:16], BIAS, A.add)
+                    else:
+                        ts(every(sc, c0, c1), every("of1", c0, c1), T.of[32 * a + 32:32 * a + 64, ENT + c0:ENT + c1],
+                           T[sc][32 * a:32 * a + 32, 16 * c0 + 15:16 * c1:16], BIAS, A.add)
+                    small(e)
+                vector_fill(t)
                 if t == 5:
-                    turn([gg, gg + "s", gg + "a", gg + "b"], [gt + "b"], T[gt][:, 160:352], T[gg][:, 16:208])
-                else:
-                    vector_fill(t, 2)
-                if i:
-                    ts([sc], ["of0"], T.of[32 * a:32 * a + 32, 0:ENT], T[sc][32 * a:32 * a + 32, 7:ROW:16], BIAS, A.add)
-                else:
-                    ts([sc], ["of1"], T.of[32 * a + 32:32 * a + 64, ENT:2 * ENT], T[sc][32 * a:32 * a + 32, 15:ROW:16], BIAS, A.add)
-                if t == 5:
-                    scan([gt + "b", "tabB"], ["s5b"], T.s5b[:], T[gt][:, 176:352], T.tab[:, 320:672:2])
+                    turn(every(gg) + [gg + "a", gg + "b"], [gt + "b"], T[gt][:, 160:352], T[gg][:, 16:208])
             else:
-                turn([gg, gg + "s", gg + "a", gg + "b"], [gt + "b"], T[gt][:, 160:352], T[gg][:, 16:208])
-                tt(["tf", "pm0", "pm1", "pm2", "pm3"], ["tf"], T.tf[:, 15:C:16], T.tf[:, 15:C:16], T.pm[:], A.add)
-                scan([gt, gt + "b", "tf"], ["s6"], T.s6[:], T[gt][:, 0:C], T.tf[:])
+                scan(["gt1b", "tabB"], ["s5b"], T.sc1[:, ROW:336], T.gt1[:, 176:352], T.tab[:, 320:672:2])
+                scalar_fill(t)
+                turn(every(gg), every(gt), T[gt][:, 0:ROW], T[gg][:, 32:192])
+                turn(every(gg) + [gg + "a", gg + "b"], [gt + "b"], T[gt][:, 160:C], T[gg][:, 16:144])
+                scan(every(gt) + ["tabA"], ["s6a"], T.sc1[:, 336:496], T[gt][:, 0:ROW], tabA)
+                scan([gt + "b", "tabB"], ["s6b"], T.sc1[:, 496:624], T[gt][:, ROW:C], T.tab[:, 320:2 * C:2])
         ll = "ll%d" % r
-        ts(["s6"], [ll], T[ll][:], T.s6[:, 15:C:16], BIAS, A.add)
+        ts(every("sc1") + ["s5b", "s6a", "s6b", "pmo"], [ll], T[ll][:], T.sc1[:].indirect(T.pmo[:]), BIAS, A.add)
         need("g", wr[ll])
         rid, pid = topo.addr(lst, core)
         es = topo.engines(core, lst)
-        g.remote_dma(T["al%d" % r][:], T[ll][:], T.sem["rL%d" % r], T.sem.left, pid, rid, bits(es))
+        g.remote_dma(T["al%d" % r][:], T[ll][:, 0:18], T.sem["rL%d" % r], T.sem.left, pid, rid, bits(es))
         left[0] += len(es)
         pn = "pls%d" % (r + 1)
         if r == 0:
@@ -471,47 +491,68 @@ def rank_program(g, core, T, topo):
             mm(["aq", "eq%d" % b_], (7 + b_) % 8, T.eq[:, 128 * b_:128 * b_ + 128], T.ep[:, 128 * b_:128 * b_ + 128], "aq%d" % r, "ap%d" % r)
         for b_ in range(4):
             act(["ps%d" % ((7 + b_) % 8)], ["fp%d" % b_], T["fp%d" % b_][:], T["ps%d" % ((7 + b_) % 8)][:, 0:C])
-        for b_ in range(1 if r == 0 else 3, 4):
-            keep_f(b_)
+        if r == 0:
+            keep_f(3)
         if r < 2:
             power(r + 1, 0)
             scaled()
             power(r + 1, 1)
         else:
             quant(["vt"], ["vq"], T.vq[:], T.vp[:], T.vt[:])
-            ts(["idr", ll], ["lo0"], T.lo[:, 0:C], T.idr[:].indirect(T[ll][:]), BIAS, A.add)
+            ts(["idr", ll], ["lo0"], T.lo[:, 0:C], T.idr[:].indirect(T[ll][:, 0:18]), BIAS, A.add)
             ts(["idr", pn], ["lo1"], T.lo[:, C:2 * C], T.idr[:].indirect(T[pn][:]), BIAS, A.add)
-            dma("s", "out", 7, ["lo0", "lo1"], ["pl"], T.pl[:], T.lo[0:128:16, :])
+            dma("s", "out", 9, ["lo0", "lo1"], ["pl"], T.pl[:], T.lo[0:128:16, :])
         al, zt = T["al%d" % r], T.zt
-        for b_ in (0, 2, 1, 3):
-            (cp if b_ < 2 else act)(["fp%d" % b_, "al"], ["zt%d" % b_], zt[:, b_:4 * C:4], T["fp%d" % b_][:].indirect(al[:]))
+        for b_ in (0, 2):
+            (cp if b_ < 2 else act)(["fp%d" % b_, "al"], ["zt%da" % b_, "zt%db" % b_], zt[:, b_:4 * C:4], T["fp%d" % b_][:].indirect(al[:]))
+        for h, (a0, b0) in enumerate(RUNS):
+            for b_ in (1, 3):
+                (cp if b_ < 2 else act)(["fp%d" % b_, "al"], ["zt%d%s" % (b_, "ab"[h])], zt[:, 4 * a0 + b_:4 * b0:4], T["fp%d" % b_][:].indirect(al[:, a0 // 16:b0 // 16]))
         halves(["zt%d" % b_ for b_ in range(4)], "zq", "zp", "zt")
         if r < 2:
             power(r + 1, 2)
-        for h in range(2):
-            mm(["zq" + "ab"[h], "wq", "wp"], 3 + 4 * h, T.wq[:, 0:128], T.wp[:, 0:128], "zq", "zp", h * HALF, (h + 1) * HALF)
+        for h, (a0, b0) in enumerate(RUNS):
+            mm(["zq" + "ab"[h], "wq", "wp"], 3 + 4 * h, T.wq[:, 0:128], T.wp[:, 0:128], "zq", "zp", a0, b0)
         for b_ in range(1, 4):
             mm(["zqa", "zqb", "wq", "wp"], 3 + b_, T.wq[:, 128 * b_:128 * b_ + 128], T.wp[:, 128 * b_:128 * b_ + 128], "zq", "zp")
         xn = T["xn%d" % r]
+
+        def state(b_, h):
+            a0, b0 = RUNS[h] if h < 2 else (0, C)
+            hb = "hb%d" % b_
+            tt([hb + "a", hb + "b", "fo%d" % b_, ll], ["xn%d%s" % (b_, k) for k in ("a", "b", "ab")[h]], xn[:, 4 * a0 + b_:4 * b0:4],
+               T[hb][:].indirect(T[ll][:, a0 // 16:b0 // 16]), T["fo%d" % b_][:, a0:b0], A.add)
+
         for b_ in range(4):
             hb = "hb%d" % b_
             if b_ == 0:
-                for h in range(2):
-                    act(["ps%d" % (3 + 4 * h)], [hb + "ab"[h]], T[hb][:, h * HALF:(h + 1) * HALF], T["ps%d" % (3 + 4 * h)][:, 0:HALF], scale=0.03125)
+                for h, (a0, b0) in enumerate(RUNS):
+                    act(["ps%d" % (3 + 4 * h)], [hb + "ab"[h]], T[hb][:, a0:b0], T["ps%d" % (3 + 4 * h)][:, 0:b0 - a0], scale=0.03125)
             else:
                 act(["ps%d" % (3 + b_)], [hb + "a", hb + "b"], T[hb][:], T["ps%d" % (3 + b_)][:, 0:C], scale=0.03125)
-            tt([hb + "a", hb + "b", "fo%d" % b_, ll], ["xn%d" % b_], xn[:, b_:4 * C:4], T[hb][:].indirect(T[ll][:]), T["fo%d" % b_][:], A.add)
         if r < 2:
+            for b_, h in ((0, 2), (1, 2), (2, 2), (3, 0), (3, 1)):
+                state(b_, h)
             starts(0)
-        halves(["xn%d" % b_ for b_ in range(4)], "q%d" % (r + 1), "qp%d" % (r + 1), "xn%d" % r)
-    for h in range(2):
-        mm(["q3" + "ab"[h], "vq"], h, T.vq[:], T.vp[:], "q3", "qp3", h * HALF, (h + 1) * HALF)
-    dma("s", "out", 7, ["q3a", "q3b"], ["oc"], T.oc[:], T.q3[:].bitcast(dt.uint8))
-    for k in range(4):
-        dma("s", "out", 7, ["q3a", "q3b"], ["osc%d" % k], T.osc[4 * k:4 * k + 4, :], T.qp3[32 * k:32 * k + 4, :])
-    for h in range(2):
-        act(["ps%d" % h], ["yo%d" % h], T.yo[:, h * HALF:(h + 1) * HALF], T["ps%d" % h][:, 0:HALF])
-    dma("a", "out", 7, ["yo0", "yo1"], ["y"], T.y[:], T.yo[:])
+            halves(["xn%d" % b_ for b_ in range(4)], "q%d" % (r + 1), "qp%d" % (r + 1), "xn%d" % r)
+
+    def store(h):
+        a0, b0 = RUNS[h]
+        quant(["xn%d%s" % (b_, "ab"[h]) for b_ in range(4)], ["q3%d" % h], T.q3[:, a0:b0], T.qp3[:, a0:b0], xn[:, 4 * a0:4 * b0])
+        mm(["q3%d" % h, "vq"], h, T.vq[:], T.vp[:], "q3", "qp3", a0, b0)
+        dma("s", "out", 9, ["q3%d" % h], ["oc%d" % h], T.oc[:, 4 * a0:4 * b0], T.q3[:, a0:b0].bitcast(dt.uint8))
+        if h:
+            for k in range(4):
+                dma("s", "out", 9, ["q30", "q31"], ["osc%d" % k], T.osc[4 * k:4 * k + 4, :], T.qp3[32 * k:32 * k + 4, :])
+        act(["ps%d" % h], ["yo%d" % h], T.yo[:, a0:b0], T["ps%d" % h][:, 0:b0 - a0])
+        dma("a", "out", 9, ["yo%d" % h], ["y%d" % h], T.y[:, a0:b0], T.yo[:, a0:b0])
+
+    for b_, h in ((0, 0), (0, 1), (1, 0), (2, 0), (3, 0), (1, 1)):
+        state(b_, h)
+    store(0)
+    state(2, 1)
+    state(3, 1)
+    store(1)
     g.wait_ge(T.sem.left, left[0])
     for s in sorted(count):
         g.wait_ge(T.sem[s], count[s])

@@ -8,8 +8,11 @@ HALF = C // 2
 ENT = 10
 ROW = 16 * ENT
 RUNS = ((0, 160), (160, C))
-CHAIN = ((("s", 6, ENT), ("v", 0, 6)), (("s", 0, 4), ("v", 4, 8), ("t", 8, ENT)))
+TWO = (("s", 6, ENT), ("v", 0, 6))
+THREE = (("s", 0, 4), ("v", 4, 8), ("t", 8, ENT))
+WHOLE = (("s", 0, ENT),)
 BIAS = 144.0
+EVEN, EVENB, ODD, ODDB, EV4, EV4B, OD4, OD4B, RES = 0, 160, 336, 496, 624, 664, 708, 748, 788
 
 SCRATCH = {
     "zt": ("sbuf", [128, 4 * C], "bfloat16"), "zq": ("sbuf", [128, C], "float8_e4m3fn_x4"), "zp": ("sbuf", [128, C], "uint8"),
@@ -17,29 +20,30 @@ SCRATCH = {
     "pI": ("sbuf", [128, 18], "int32"), "kI": ("sbuf", [128, 18], "int32"), "mI": ("sbuf", [128, 18], "int32"),
     "wq": ("sbuf", [128, 512], "float8_e4m3fn_x4"), "wp": ("sbuf", [128, 512], "uint8"),
     "uq": ("sbuf", [128, 128], "float8_e4m3fn_x4"), "up": ("sbuf", [128, 128], "uint8"),
-    "u1q": ("sbuf", [128, 128], "float8_e4m3fn_x4"), "u1p": ("sbuf", [128, 128], "uint8"),
-    "u2q": ("sbuf", [128, 128], "float8_e4m3fn_x4"), "u2p": ("sbuf", [128, 128], "uint8"),
     "vq": ("sbuf", [128, 128], "float8_e4m3fn_x4"), "vp": ("sbuf", [128, 128], "uint8"),
     "ones": ("sbuf", [128, 516], "bfloat16"), "e0": ("sbuf", [128, 516], "bfloat16"),
     "eq": ("sbuf", [128, 512], "float8_e4m3fn_x4"), "ep": ("sbuf", [128, 512], "uint8"),
     "pf": ("sbuf", [128, 1], "float32"), "pw": ("sbuf", [128, 8], "float32"), "bi": ("sbuf", [128, 8], "int32"), "bj": ("sbuf", [128, 8], "int32"),
     "bit": ("sbuf", [128, 8], "float32"), "sg": ("sbuf", [128, 8], "float32"), "nb": ("sbuf", [128, 8], "float32"),
-    "cst": ("sbuf", [128, 32], "float32"), "quart": ("sbuf", [128, 72], "float32"),
+    "cst": ("sbuf", [128, 48], "float32"), "quart": ("sbuf", [128, 72], "float32"), "sel": ("sbuf", [128, 16], "float32"),
     "idr": ("sbuf", [128, C], "bfloat16"), "lor": ("sbuf", [128, 32], "float32"), "d16": ("sbuf", [128, 48], "float32"),
     "own": ("sbuf", [128, C], "bfloat16"), "lane": ("sbuf", [128, 18], "uint16"), "half": ("sbuf", [128, 8], "float32"),
-    "ulf": ("sbuf", [128, 16], "float32"), "ull": ("sbuf", [128, 16], "uint16"),
+    "ulf": ("sbuf", [128, 16], "float32"), "ull": ("sbuf", [128, 24], "uint16"), "base": ("sbuf", [128, C], "bfloat16"),
+    "fr": ("sbuf", [128, 64], "float32"), "ft": ("sbuf", [128, 64], "float32"), "fin": ("sbuf", [128, 2], "uint16"), "tlo": ("sbuf", [128, 4], "uint16"),
+    "four": ("sbuf", [128, 256], "bfloat16"),
     "mls": ("sbuf", [128, 18], "uint16"), "k20": ("sbuf", [128, 20], "uint16"),
     "kf": ("sbuf", [128, 18], "float32"), "ke": ("sbuf", [128, 40], "float32"),
     "y1": ("sbuf", [128, C], "bfloat16"), "y2": ("sbuf", [128, C], "bfloat16"), "y3": ("sbuf", [128, C], "bfloat16"),
-    "tr": ("sbuf", [128, 368], "bfloat16"), "tab": ("sbuf", [128, 672], "bfloat16"), "tf": ("sbuf", [128, 512], "bfloat16"),
-    "w": ("sbuf", [128, C], "bfloat16"), "wg": ("sbuf", [128, C], "bfloat16"),
-    "of": ("sbuf", [128, 2 * ENT], "uint16"),
-    "sc0": ("sbuf", [128, ROW], "bfloat16"), "sc1": ("sbuf", [128, 624], "bfloat16"),
-    "po": ("sbuf", [128, 6], "float32"), "pmo": ("sbuf", [128, 2], "uint16"),
+    "tr": ("sbuf", [128, 368], "bfloat16"), "tab": ("sbuf", [128, 672], "bfloat16"),
+    "te": ("sbuf", [128, 84], "float32"), "to": ("sbuf", [128, 84], "float32"), "tl": ("sbuf", [128, 64], "uint16"),
+    "w": ("sbuf", [128, C], "bfloat16"), "wg": ("sbuf", [128, C], "bfloat16"), "wa": ("sbuf", [128, C], "bfloat16"),
+    "of": ("sbuf", [128, 2 * ENT], "uint16"), "res": ("sbuf", [128, RES], "bfloat16"),
+    "gi": ("sbuf", [128, 4 * ROW], "bfloat16"), "ys": ("sbuf", [128, 4 * 192], "bfloat16"),
+    "yt": ("sbuf", [128, 2 * ROW], "bfloat16"), "s1": ("sbuf", [128, 2 * ROW], "bfloat16"),
     "be": ("sbuf", [128, C], "bfloat16"), "bm": ("sbuf", [128, C], "bfloat16"), "hs": ("sbuf", [128, 880], "bfloat16"),
     "prow": ("sbuf", [128, C], "bfloat16"), "mrow": ("sbuf", [128, C], "bfloat16"), "ms": ("sbuf", [128, C], "float32"),
-    "ex": ("sbuf", [128, 54], "float32"), "pn": ("sbuf", [128, 54], "float32"), "hd": ("sbuf", [128, 18], "float32"),
-    "ph": ("sbuf", [128, 18], "float32"), "mh": ("sbuf", [128, 18], "float32"),
+    "ex": ("sbuf", [128, 54], "float32"), "pn": ("sbuf", [128, 54], "float32"), "hd": ("sbuf", [128, 54], "float32"),
+    "fo": ("sbuf", [128, 4 * C], "bfloat16"), "fp": ("sbuf", [128, 4 * C], "bfloat16"), "hb": ("sbuf", [128, 4 * C], "float32"),
     "yo": ("sbuf", [128, C], "float32"), "lo": ("sbuf", [128, 2 * C], "float32"),
 }
 for _i in range(2):
@@ -50,12 +54,11 @@ for _i in range(4):
     SCRATCH["pls%d" % _i] = ("sbuf", [128, 18], "uint16")
     SCRATCH["q%d" % _i] = ("sbuf", [128, C], "float8_e4m3fn_x4")
     SCRATCH["qp%d" % _i] = ("sbuf", [128, C], "uint8")
-    SCRATCH["fo%d" % _i] = ("sbuf", [128, C], "bfloat16")
-    SCRATCH["fp%d" % _i] = ("sbuf", [128, C], "bfloat16")
-    SCRATCH["hb%d" % _i] = ("sbuf", [128, C], "float32")
 for _i in range(8):
     SCRATCH["ps%d" % _i] = ("psum", [128, 512], "float32")
 for _i in range(3):
+    SCRATCH["u%dq" % _i] = ("sbuf", [128, 128], "float8_e4m3fn_x4")
+    SCRATCH["u%dp" % _i] = ("sbuf", [128, 128], "uint8")
     SCRATCH["xn%d" % _i] = ("sbuf", [128, 4 * C], "bfloat16")
     SCRATCH["aq%d" % _i] = ("sbuf", [128, C], "float8_e4m3fn_x4")
     SCRATCH["ap%d" % _i] = ("sbuf", [128, C], "uint8")
@@ -77,6 +80,29 @@ def relays(core, partner, topo):
 
 def bits(es):
     return sum(1 << e for e in es)
+
+
+def place(a, y, e):
+    odd, back = e % 2, e + 1 if e < 10 else e - 10
+    if a < 2:
+        return EVEN + 160 * odd + 16 * back + 7 if y == 0 else ODD + 16 * min(e, 17) + 15
+    if a == 2:
+        return EV4 + 40 * odd + 4 * back + 3 if y == 0 else OD4 + 40 * (1 - odd) + 4 * (back - odd) + 3
+    return (EV4B if e < 10 else EV4) + 4 * back + 3 if y == 0 else OD4 + 4 * e + 3
+
+
+def pieces(v):
+    out, i = [], 0
+    while i < len(v):
+        s2, n, m = v[i + 1] - v[i], 2, 1
+        while i + n < len(v) and v[i + n] - v[i + n - 1] == s2:
+            n += 1
+        s1 = v[i + 2] - v[i] if i + 3 < len(v) else 0
+        while i + 2 * m + 1 < len(v) and (v[i + 2 * m], v[i + 2 * m + 1]) == (v[i] + m * s1, v[i] + m * s1 + s2):
+            m += 1
+        out.append((i, n, [[s2, n]], v[i]) if n >= 2 * m else (i, 2 * m, [[s1, m], [s2, 2]], v[i]))
+        i += out[-1][1]
+    return out
 
 
 def relay_program(g, core, T, topo):
@@ -198,8 +224,8 @@ def rank_program(g, core, T, topo):
     def turn(reads, writes, out, in_):
         op("v", reads, writes, lambda: g.vector.transpose(out, in_))
 
-    def scan(reads, writes, out, d0, d1, first=0.0):
-        op("v", reads, writes, lambda: g.vector.tensor_tensor_scan(out, d0, d1, first, A.mult, A.add))
+    def scan(reads, writes, out, d0, d1):
+        op("v", reads, writes, lambda: g.vector.tensor_tensor_scan(out, d0, d1, 0.0, A.mult, A.add))
 
     def iota(key, out, pattern, base, step=0):
         op("g", [], [key], lambda: g.iota(out, pattern, base, step, allow_small_or_imprecise_dtypes=True))
@@ -218,43 +244,94 @@ def rank_program(g, core, T, topo):
 
     iota("pf", T.pf[:], [[0, 1]], 0, 1)
     iota("quart", T.quart[:], [[1, 72]], -36)
+    iota("lor", T.lor[:], [[-1, 2], [1, 16]], 0)
     iota("ulf", T.ulf[:, 0:8], [[32, 4], [0, 2]], -16)
     iota("ulf2", T.ulf[:, 8:16], [[16, 8]], 0)
-    iota("lor", T.lor[:], [[-1, 2], [1, 16]], 0)
     iota("idr", T.idr[:], [[1, C]], -144)
     fill("half", T.half[:], 0.5)
     fill("ones", T.ones[:], 1.0)
     op("g", ["ones"], ["e0"], lambda: g.affine_select(T.e0[:], T.ones[:], [[1, 516]], A.is_equal, 0.0, -3, -4))
+    op("g", ["ones"], ["four"], lambda: g.affine_select(T.four[:], T.ones[:, 0:256], [[0, 64], [1, 4]], A.is_gt, 0.0, 0, 0))
     b = lambda i: T.bit[:, i:i + 1]
     nb = lambda i: T.nb[:, i:i + 1]
     sg = lambda i: T.sg[:, i:i + 1]
     cc = lambda j: T.cst[:, j:j + 1]
+    op("v", ["half"], ["pw"], lambda: g.vector.tensor_tensor_scan(T.pw[:], T.half[:], T.half[:], 256.0, A.mult, A.max))
     fill("of", T.of[:], 0)
-    op("v", ["half", "ones"], ["pw"], lambda: g.vector.tensor_tensor_scan(T.pw[:], T.half[:], T.ones[:, 0:8], 256.0, A.mult, A.mult))
     fill("ke", T.ke[:], 0.0)
-    fill("ex", T.ex[:], 0.0)
     ts(["pf", "pw"], ["bi"], T.bi[:], T.pw[:], T.pf[:], A.mult)
-    fill("hs0", T.hs[:, 31:880:48], 0.0)
+    fill("ex", T.ex[:], 0.0)
+    fill("sg5", T.sg[:, 5:6], 1.0)
     ts(["bi"], ["bj"], T.bj[:, 0:7], T.bi[:, 0:7], 7, A.logical_shift_right, 1, A.bitwise_and)
     ts(["bi"], ["bj7"], T.bj[:, 7:8], T.bi[:, 7:8], 15, A.bitwise_and)
+    fill("hs0", T.hs[:, 31:880:48], 0.0)
     cp(["bj"], ["bit"], T.bit[:, 0:7], T.bj[:, 0:7])
     ts(["bj"], ["nb"], T.nb[:, 0:7], T.bj[:, 0:7], -1.0, A.mult, 1.0, A.add)
-    ts(["bj"], ["sg"], T.sg[:, 0:7], T.bj[:, 0:7], 2.0, A.mult, -1.0, A.add)
+    ts(["bj"], ["sg"], T.sg[:, 0:4], T.bj[:, 0:4], 2.0, A.mult, -1.0, A.add)
+    cp(["bj7"], ["c16"], cc(16), T.bj[:, 7:8])
+    ts(["bit"], ["c1"], cc(1), b(1), 0.25, A.mult, b(0), A.max)
+    ts(["bit", "nb"], ["c0"], cc(0), b(0), 4.0, A.mult, nb(1), A.max)
+    ts(["sg"], ["sg4"], sg(4), sg(2), sg(3), A.mult)
+    ts(["lor", "c1"], ["sel8"], T.sel[:, 8:12], T.lor[:, 0:4], cc(1), A.mult)
+    ts(["lor", "c16"], ["sel4"], T.sel[:, 4:8], T.lor[:, 1:8:2], cc(16), A.is_equal)
+    ts(["sg", "sg4", "sg5", "nb"], ["sel12"], T.sel[:, 12:16], T.sg[:, 2:6], nb(0), A.mult)
     for i in range(4):
-        act(["bit"], ["c%d" % i], cc(i), b(1), scale=0.25 * i)
-    ts(["sg"], ["c4"], cc(4), sg(2), sg(3), A.mult)
-    for i in range(4):
-        ts(["quart", "nb", "c%d" % i], ["dg3_%d" % i], T.dg3[:, i:C:4], T.quart[:], nb(1), A.mult, cc(i), A.add)
-    d3 = ["dg3_%d" % i for i in range(4)]
-    ts(d3 + ["c4"], ["dg2"], T.dg2[:], T.dg3[:], cc(4), A.mult)
+        ts(["quart", "c0", "sel8"], ["base%d" % i], T.base[:, i:C:4], T.quart[:], cc(0), A.mult, T.sel[:, 8 + i:9 + i], A.add)
+        if i == 1:
+            tt(["sel4", "sel12"], ["sel"], T.sel[:, 0:4], T.sel[:, 4:8], T.sel[:, 12:16], A.add)
+    whole = ["sel"] + ["base%d" % i for i in range(4)]
+    cp(["pI"], ["pls0"], T.pls0[:], T.pI[:])
+    ts(whole, ["dg3"], T.dg3[:], T.base[:], T.sel[:, 3:4], A.mult)
+    ts(whole, ["dg2"], T.dg2[:], T.base[:], T.sel[:, 2:3], A.mult)
+
+    def line(key, x, s, c=None, part=slice(0, 128)):
+        col = lambda v: T[v[1]][part, v[2]:v[2] + 1] if isinstance(v, tuple) else v
+        kw = {} if c is None else {"bias": col(c)}
+        act([v[0] for v in (x, s, c) if isinstance(v, tuple)], ["c%d" % key], T.cst[part, key:key + 1], col(x), F.Copy if c is None else F.Identity, scale=col(s), **kw)
+
+    K = lambda j: ("c%d" % j, "cst", j)
+    B = lambda j: ("bit", "bit", j)
+    NB = lambda j: ("nb", "nb", j)
+    SG = lambda j: ("sg", "sg", j)
+    ONE = ("ones", "ones", 0)
+    late = slice(64, 128)
     plain("tra", T.tr[:, 16:32], 16, 0.0)
     plain("trb", T.tr[:, 352:368], 16, 0.0)
-    act(d3 + ["sg"], ["dg1"], T.dg1[:], T.dg3[:], scale=sg(3))
-    act(d3 + ["sg"], ["dg0"], T.dg0[:], T.dg3[:], scale=sg(2))
+    plain("c17", cc(17), 1, -1e-29)
+    plain("c23", cc(23), 1, 352.0)
+    plain("c24", cc(24), 1, 0.5)
+    plain("gt1v", T.gt1[:, 0:ROW], ROW, 1.0)
+    for i in range(2):
+        plain("gg%da" % i, T["gg%d" % i][:, 16:32], 16, 0.0)
+        plain("gg%db" % i, T["gg%d" % i][:, 192:208], 16, 0.0)
+    plain("gt1v", T.gt1[:, 0:ROW:8], 2 * ENT, 0.0)
+    plain("gt1s", T.gt1[:, 4:ROW:16], ENT, -1.0)
+    plain("ysa", T.ys[:, 3:64:4], 16, 0.0)
+    line(2, NB(4), 1.0, part=slice(0, 64))
+    line(26, B(0), -672.0, K(23))
+    line(25, B(0), 320.0)
+    line(2, NB(5), 1.0, part=late)
+    line(32, SG(0), SG(2))
+    line(33, NB(2), NB(3))
+    line(34, NB(0), NB(1))
+    line(31, B(3), NB(2))
+    line(27, K(16), 32.0, K(25))
+    line(3, K(2), -1.0, ONE)
+    line(42, K(32), -0.5, K(24))
+    line(29, K(33), -1.0, ONE)
+    line(35, K(34), -1.0, ONE)
+    line(40, K(31), NB(0))
+    line(28, K(26), B(4), K(27))
+    line(36, SG(0), 0.25)
+    line(39, SG(1), 0.25)
+    line(41, K(40), -2.0, ONE)
+    act(whole, ["dg1"], T.dg1[:], T.base[:], scale=T.sel[:, 1:2])
+    line(30, K(29), -1e-29)
+    line(37, K(39), K(41))
 
     def power(r, n):
         src, dst = ["dg3", "y1", "y2"][n], ["y1", "y2", "y3"][n]
-        tt((d3 if n == 0 else [src]) + ["pls%d" % r, "dg%d" % (2 - n)], [dst], T[dst][:], T[src][:].indirect(T["pls%d" % r][:]), T["dg%d" % (2 - n)][:], A.add)
+        tt([src, "pls%d" % r, "dg%d" % (2 - n)], [dst], T[dst][:], T[src][:].indirect(T["pls%d" % r][:]), T["dg%d" % (2 - n)][:], A.add)
 
     def starts(cut):
         if cut:
@@ -267,7 +344,6 @@ def rank_program(g, core, T, topo):
         else:
             turn(["tr1", "tr2", "tra", "trb"], ["tabB"], T.tab[:, 320:672], T.tr[:, 16:368])
 
-    cp(["pI"], ["pls0"], T.pls0[:], T.pI[:])
     cp(["kI"], ["kf"], T.kf[:], T.kI[:])
     power(0, 0)
     for h in range(2):
@@ -275,39 +351,44 @@ def rank_program(g, core, T, topo):
             c0 = 10 * (1 - h) + y
             n = len(range(c0, 18 if h == 0 else 10, 2))
             m0 = 2 * h + y
-            act(["kf", "nb", "ke"], ["ke%d" % m0], T.ke[:, m0:m0 + 4 * n - 3:4], T.kf[:, c0:c0 + 2 * n - 1:2], scale=nb(4))
-    act(["kf", "bit", "ke"], ["ko1"], T.ke[:, 21:40:2], T.kf[:, 0:10], scale=b(4))
-    act(["kf", "bit", "ke"], ["ko0"], T.ke[:, 20:35:2], T.kf[:, 10:18], scale=b(4))
+            act(["kf", "c2", "ke"], ["ke%d" % m0], T.ke[:, m0:m0 + 4 * n - 3:4], T.kf[:, c0:c0 + 2 * n - 1:2], scale=cc(2))
+    act(["kf", "c3", "ke"], ["ko1"], T.ke[:, 21:40:2], T.kf[:, 0:10], scale=cc(3))
+    act(["kf", "c3", "ke"], ["ko0"], T.ke[:, 20:35:2], T.kf[:, 10:18], scale=cc(3))
     ts(["nb"], ["c5"], cc(5), nb(0), nb(1), A.mult, nb(2), A.mult)
     ts(["nb"], ["c6"], cc(6), nb(3), nb(5), A.mult, nb(6), A.mult)
     ts(["nb", "bit"], ["c7"], cc(7), nb(0), nb(1), A.mult, b(2), A.mult)
     power(0, 1)
-    line = lambda key, x, s, c: act(["nb", "bit", "ones"] + ["c%d" % i for i in (x, s, c) if i in range(32)], ["c%d" % key], cc(key), cc(x), F.Identity,
-                                    scale=cc(s) if s in range(32) else s[0], bias=cc(c) if c in range(32) else c[0])
-    plain("gt1v", T.gt1[:, 0:ROW], ROW, 1.0)
-    act(["bit", "c7"], ["c15"], cc(15), b(3), F.Identity, scale=16.0, bias=cc(7))
-    line(8, 5, [-1.0], [nb(0)])
-    line(10, 6, [-1.0], [T.ones[:, 0:1]])
-    plain("gt1v", T.gt1[:, 0:ROW:8], 2 * ENT, 0.0)
-    line(9, 7, [-2.0], 8)
-    act(["c8", "c10"], ["c13"], cc(13), cc(8), scale=cc(10))
-    plain("gt1s", T.gt1[:, 4:ROW:16], ENT, -1.0)
-    line(11, 9, 6, [b(0)])
-    plain("c17", cc(17), 1, -1e-29)
-    for i in range(2):
-        plain("gg%da" % i, T["gg%d" % i][:, 16:32], 16, 0.0)
-        plain("gg%db" % i, T["gg%d" % i][:, 192:208], 16, 0.0)
-    line(14, 13, [-1e-29], 11)
+    early = slice(0, 64)
+    line(15, B(3), 16.0, K(7))
+    act(whole, ["dg0"], T.dg0[:], T.base[:], scale=T.sel[:, 0:1])
+    line(8, K(5), -1.0, NB(0))
+    line(10, K(6), -1.0, ONE)
+    line(38, K(37), SG(0))
+    line(13, K(29), K(35), part=late)
+    line(9, K(7), -2.0, K(8))
+    line(43, K(8), K(10))
+    line(14, K(13), -1e-29, part=late)
+    line(11, K(9), K(6), B(0))
+    line(13, K(43), 1.0, part=early)
     act(["idr", "pls0"], ["prow"], T.prow[:], T.idr[:].indirect(T.pls0[:]))
+    line(14, K(43), -1e-29, K(11), early)
     quant(["xt"], ["q0a", "q0b"], T.q0[:], T.qp0[:], T.xt[:])
     tt(["ke0", "ke1", "ke2", "ke3", "ko0", "ko1"], ["ke"], T.ke[:, 0:20], T.ke[:, 0:20], T.ke[:, 20:40], A.add)
-    ts(["ulf", "c15"], ["ull"], T.ull[:, 0:8], T.ulf[:, 0:8], cc(15), A.add, 0.0, A.max)
+    ts(["ulf", "c15"], ["ull0"], T.ull[:, 0:4], T.ulf[:, 0:4], cc(15), A.add, 0.0, A.max)
     power(0, 2)
     cp(["ke"], ["k20"], T.k20[:], T.ke[:, 0:20])
+    ts(["ulf", "c42", "ull0"], ["ull0"], T.ull[:, 4:8], T.ulf[:, 4:8], cc(42), A.add)
     quant(["ut"], ["uq", "up"], T.uq[:], T.up[:], T.ut[:])
-    cp(["ulf2"], ["ull2"], T.ull[:, 8:16], T.ulf[:, 8:16])
-    act(["up", "ull"], ["u1p"], T.u1p[:], T.up[:].indirect(T.ull[:, 0:8]))
-    cp(["uq", "ull"], ["u1q"], T.u1q[:].bitcast(dt.uint32), T.uq[:].bitcast(dt.uint32).indirect(T.ull[:, 0:8]))
+    ts(["ulf", "c31"], ["ull1"], T.ull[:, 8:16], T.ulf[:, 0:8], cc(31), A.add, 16.0, A.add)
+
+    def codes_of_u(i):
+        cp(["uq", "ull%d" % i], ["u%dq" % i], T["u%dq" % i][:].bitcast(dt.uint32), T.uq[:].bitcast(dt.uint32).indirect(T.ull[:, 8 * i:8 * i + 8]))
+
+    def scales_of_u(i):
+        act(["up", "ull%d" % i], ["u%dp" % i], T["u%dp" % i][:], T.up[:].indirect(T.ull[:, 8 * i:8 * i + 8]))
+
+    scales_of_u(0)
+    codes_of_u(0)
     starts(10)
 
     def unit(b):
@@ -318,32 +399,15 @@ def rank_program(g, core, T, topo):
         act(src[1] + [lst], [dst + "b"], T[dst][:, 160:C], T[src[0]][:].indirect(T[lst][:, 10:18]))
 
     def spread(key, src):
-        tt([key, "avg"], ["hd"], T.hd[:], src, T.ex[:, 2:54:3], A.subtract)
-        return lambda: ts(["hd", "c20", "ex"], ["hdl"], T.ex[:, 0:54:3], T.hd[:], cc(20), A.mult)
+        tt([key, "avg"], ["hd"], T.hd[:, 0:18], src, T.ex[:, 2:54:3], A.subtract)
+        return lambda: ts(["hd", "c20", "ex"], ["hdl"], T.ex[:, 0:54:3], T.hd[:, 0:18], cc(20), A.mult)
+
+    part = lambda name, b, a0=0, b0=C: T[name][:, C * b + a0:C * b + b0]
+    ph, mh = T.hd[:, 18:36], T.hd[:, 36:54]
 
     ROUND = 12582912.0
-    later = [
-        lambda: cp(["mI"], ["mls"], T.mls[:], T.mI[:]),
-        lambda: cp(["bj7"], ["c16"], cc(16), T.bj[:, 7:8]),
-        lambda: ts(["pI"], ["ph"], T.ph[:], T.pI[:], 0.5, A.mult),
-        lambda: ts(["bit"], ["c21"], cc(21), b(0), 160.0, A.mult, 7.0, A.add),
-        lambda: ts(["lor", "c16"], ["d16a"], T.d16[:, 0:16], T.lor[:, 0:16], cc(16), A.not_equal),
-        lambda: ts(["lor", "c16"], ["d16b"], T.d16[:, 16:32], T.lor[:, 16:32], cc(16), A.is_equal, 65535.0, A.mult),
-        lambda: ts(["ones", "c16"], ["lane"], T.lane[:], T.ones[:, 0:18], cc(16), A.mult),
-        lambda: tt(["d16a", "d16b"], ["d16"], T.d16[:, 32:48], T.d16[:, 0:16], T.d16[:, 16:32], A.add),
-        lambda: ts(["c16"], ["c19"], cc(19), cc(16), 15.0, A.is_equal, 2.0 ** -16, A.max),
-        lambda: ts(["c16"], ["c20"], cc(20), cc(16), 15.0, A.is_equal, 2.0 ** -32, A.max),
-        lambda: ts(["c16"], ["po0"], T.po[:, 0:1], cc(16), 10.0, A.is_ge, -176.0, A.mult),
-        lambda: ts(["c16"], ["po2"], T.po[:, 2:4], T.lor[:, 1:7:5], cc(16), A.add, 16.0, A.mult),
-        lambda: tt(["po0", "po2"], ["po2"], T.po[:, 2:3], T.po[:, 2:3], T.po[:, 0:1], A.add),
-        lambda: ts(["c16"], ["po4"], T.po[:, 4:6], T.lor[:, 0:17:16], cc(16), A.add, 16.0, A.mult),
-        lambda: ts(["po2", "c21", "nb"], ["po2"], T.po[:, 2:4], T.po[:, 2:4], cc(21), A.add, nb(4), A.mult),
-        lambda: ts(["po4"], ["po5"], T.po[:, 5:6], T.po[:, 5:6], 272.0, A.add, 272.0, A.min),
-        lambda: ts(["po4", "po5", "bit"], ["po4"], T.po[:, 4:6], T.po[:, 4:6], 351.0, A.add, b(4), A.mult),
-        lambda: tt(["po2", "po4"], ["po2"], T.po[:, 2:4], T.po[:, 2:4], T.po[:, 4:6], A.add),
-        lambda: cp(["po2"], ["pmo"], T.pmo[:], T.po[:, 2:4]),
-    ]
-
+    every = lambda k, c0=0, c1=ENT: [k + "_%d" % c for c in range(c0, c1, 2)]
+    rows = []
     left = [0]
     for r in range(3):
         partner = T.cores[rank ^ STEP[r]]
@@ -364,101 +428,176 @@ def rank_program(g, core, T, topo):
             left[0] += 2 * len(es)
         g.remote_dma_fused(fc, local_sem=T.sem.left)
         g.remote_dma_fused(fs, local_sem=T.sem.left)
+        if r == 0:
+            for a, p0, p1 in ((0, 0, 64), (2, 64, 96), (3, 96, 128)):
+                if a == 2:
+                    need("g", [("sg", count["sg"])])
+                for k in range(2):
+                    for i0, n, pattern, first in pieces([place(a, y, 16 * k + i) for y in range(2) for i in range(16)]):
+                        rows.append("fr%d" % len(rows))
+                        iota(rows[-1], T.fr[p0:p1, 32 * k + i0:32 * k + i0 + n], pattern, first)
 
         def own_f(b):
             mm(both + ["eq%d" % b], 3 + b, T.eq[:, 128 * b:128 * b + 128], T.ep[:, 128 * b:128 * b + 128], q, qp)
 
-        def first_scores():
-            mm(both + ["u2q", "u2p"], 2, T.u2q[:], T.u2p[:], q, qp)
+        def scores(i):
+            mm(both + ["u%dq" % i, "u%dp" % i], (0, 2, 7)[i], T["u%dq" % i][:], T["u%dp" % i][:], q, qp)
 
         def keep_f(b):
-            act(["ps%d" % (3 + b)], ["fo%d" % b], T["fo%d" % b][:], T["ps%d" % (3 + b)][:, 0:C])
+            act(["ps%d" % (3 + b)], ["fo%d" % b], part("fo", b), T["ps%d" % (3 + b)][:, 0:C])
 
         for h, (a0, b0) in enumerate(RUNS):
-            mm([both[h], "u1q", "u1p"], h, T.u1q[:], T.u1p[:], q, qp, a0, b0)
+            mm([both[h], "u0q", "u0p"], h, T.u0q[:], T.u0p[:], q, qp, a0, b0)
         if r:
-            first_scores()
+            scores(1)
+            scores(2)
             for b_ in range(4):
                 own_f(b_)
         for h, (a0, b0) in enumerate(RUNS):
-            act(["ps%d" % h, "c13", "c14"], ["w" + "ab"[h]], T.w[:, a0:b0], T["ps%d" % h][:, 0:b0 - a0], F.Sign, scale=cc(13), bias=cc(14))
+            act(["ps%d" % h, "c13", "c14"], ["w" + "xy"[h]], T.w[:, a0:b0], T["ps%d" % h][:, 0:b0 - a0], F.Sign, scale=cc(13), bias=cc(14))
 
-        def vector_fill(t):
-            if r:
-                return
-            if t == 0:
-                cp(["uq", "ull2"], ["u2q"], T.u2q[:].bitcast(dt.uint32), T.uq[:].bitcast(dt.uint32).indirect(T.ull[:, 8:16]))
-                first_scores()
-            elif t == 1:
-                table(1)
-            elif t < 5:
-                unit(max(t - 1, 0))
-                own_f(max(t - 1, 0))
+        def lists():
+            ts(["tabA", "tabB", "tlo"], ["tl"], T.tl[:], T.tab[:].indirect(T.tlo[:]), BIAS, A.add)
 
-        def small(e):
-            if later and e == "s":
-                later.pop(0)()
+        def ahead(n, c0=0, c1=ENT):
+            out, src = T.gi[:, 64 * c0 + n:64 * c1:4], T.wa[:].indirect(T.tl[:, 16 * n + c0:16 * n + c1])
+            if n < 3:
+                act(["wa", "tl", "c%d" % (36 + n)], every("gi%d" % n), out, src, scale=cc(36 + n))
+            else:
+                ts(["wa", "tl"], every("gi3", c0, c1), out, src, 0.25, A.mult)
 
-        def scalar_fill(t):
-            if r == 0 and t == 0:
-                act(["up", "ull2"], ["u2p"], T.u2p[:], T.up[:].indirect(T.ull[:, 8:16]))
-            elif r == 0 and t == 1:
-                act(["prow", "mls"], ["mrow"], T.mrow[:], T.prow[:].indirect(T.mls[:]))
-            elif r == 0 and t == 6:
-                act(["d16", "lane"], ["own"], T.own[:], T.d16[:, 32:48].indirect(T.lane[:]))
-            if t == (0 if r else 2):
-                act(["ps2", "c17"], ["wg"], T.wg[:], T.ps2[:, 0:C], F.Sign, bias=cc(17))
-            if r and t in (1, 2, 3, 4):
-                keep_f(t - 1)
-            if r == 0 and t in (3, 4, 5):
-                keep_f(t - 3)
+        def summed(c0, c1):
+            scan(["four"] + [k for n in range(4) for k in every("gi%d" % n, c0, c1)], every("ys", c0, c1),
+                 T.ys[:, 64 + 64 * c0:64 + 64 * c1], T.four[:, 0:64 * (c1 - c0)], T.gi[:, 64 * c0:64 * c1])
+
+        def turned(part):
+            if part == 0:
+                turn(every("ys"), ["ytA"], T.yt[:, 0:ROW], T.ys[:, 67:704:4])
+            else:
+                turn(every("ys") + ["ysa"], ["ytB"], T.yt[:, ROW:2 * ROW], T.ys[:, 3:640:4])
+
+        def pack(h, k):
+            name = ("te", "to")[h]
+            tt(["tabA", "tabB"], [name + str(k)], T[name][late, k:84:4], T.tab[late, 16 * h + 4 * k:672:32], T.tab[late, 16 * h + 4 * k + 2:672:32], A.add)
+
+        te, to = ["te%d" % k for k in range(4)], ["to%d" % k for k in range(4)]
+        pads = lambda k: every(k) + [k + "a", k + "b"]
+        first = [
+            lambda: cp(["mI"], ["mls"], T.mls[:], T.mI[:]),
+            lambda: ts(["pI"], ["ph"], ph, T.pI[:], 0.5, A.mult),
+            lambda: ts(["lor", "c16"], ["d16a"], T.d16[:, 0:16], T.lor[:, 0:16], cc(16), A.not_equal),
+            lambda: ts(["lor", "c16"], ["d16b"], T.d16[:, 16:32], T.lor[:, 16:32], cc(16), A.is_equal, 65535.0, A.mult),
+            lambda: ts(["ones", "c16"], ["lane"], T.lane[:], T.ones[:, 0:18], cc(16), A.mult),
+            lambda: cp(["ulf2"], ["ull2"], T.ull[:, 16:24], T.ulf[:, 8:16]),
+            lambda: tt(["d16a", "d16b"], ["d16"], T.d16[:, 32:48], T.d16[:, 0:16], T.d16[:, 16:32], A.add),
+            lambda: ts(["c16"], ["c19"], cc(19), cc(16), 15.0, A.is_equal, 2.0 ** -16, A.max),
+            lambda: ts(["c16"], ["c20"], cc(20), cc(16), 15.0, A.is_equal, 2.0 ** -32, A.max),
+            lambda: turn(rows, ["ft"], T.ft[:], T.fr[:]),
+            lambda: ts(["ft"], ["fin"], T.fin[:], T.ft[:, 0:64:32], RES - 1.0, A.min),
+        ]
+
+        def both_f(b):
+            unit(b)
+            own_f(b)
+
+        P = lambda h, k: (lambda: pack(h, k))
+        waits = {
+            (0, 0): [lists], (0, 1): [P(1, 0), P(1, 1)], (0, 2): [P(1, 2), P(1, 3)], (0, 3): [P(0, 0), P(0, 1)],
+            (1, 0): [lambda: ahead(3, 0, 4)], (1, 1): [lambda: ahead(3, 4, 8)], (1, 2): [lambda: ahead(3, 8, ENT)], (1, 3): [P(0, 2), P(0, 3)],
+            (2, 1): [lambda: summed(0, 4)], (2, 2): [lambda: summed(4, 8)], (2, 3): [lambda: summed(8, ENT), lambda: turn(pads("gg0"), ["gt0b"], T.gt0[:, ROW:C], T.gg0[:, 16:144])],
+            (2, 0): [lambda: turn(pads("gg1"), ["gt1b"], T.gt1[:, ROW:352], T.gg1[:, 16:208])],
+            (3, 0): [lambda: turned(0)],
+            (3, 1): [lambda: scan(["gt1b", "tabB"], ["evenB"], T.res[:, EVENB:EVENB + 176], T.gt1[:, 176:352], T.tab[:, 320:672:2])],
+            (3, 2): [lambda: turned(1)],
+            (3, 3): [lambda: scan(["gt0b", "tabB"], ["oddB"], T.res[:, ODDB:ODDB + 128], T.gt0[:, ROW:C], T.tab[:, 320:2 * C:2])],
+        }
+        behind = {0: [lambda: act(["ps2", "c29", "c30"], ["wa"], T.wa[:], T.ps2[:, 0:C], F.Sign, scale=cc(29), bias=cc(30)), lambda: ahead(0)],
+                  1: [lambda: ahead(1), lambda: ahead(2)]}
+        signs = lambda: act(["ps7", "c17"], ["wg"], T.wg[:], T.ps7[:, 0:C], F.Sign, bias=cc(17))
+        if r:
+            behind.update({2: [signs, lambda: keep_f(0)], 3: [lambda: keep_f(1), lambda: keep_f(2)], 4: [lambda: keep_f(3)]})
+        else:
+            behind.update({2: [lambda: scales_of_u(2), lambda: act(["prow", "mls"], ["mrow"], T.mrow[:], T.prow[:].indirect(T.mls[:]))],
+                           3: [lambda: act(["d16", "lane"], ["own"], T.own[:], T.d16[:, 32:48].indirect(T.lane[:])), signs],
+                           4: [lambda: keep_f(0), lambda: keep_f(1), lambda: keep_f(2)]})
+            waits[2, 0] += [lambda: codes_of_u(2), lambda: scores(2)]
+            waits[1, 3] = [lambda: both_f(0)]
+            waits[3, 0] += [P(0, 2)]
+            waits[3, 1] += [P(0, 3)]
+            waits[3, 3] += [lambda: both_f(1)]
+            waits[3, 4] = [lambda: both_f(2)]
+
+        def wait(t, k):
+            for call in waits.get((t, k), []):
+                call()
+
+        def pick(i, runs):
+            for e, c0, c1 in runs:
+                (cp if e == "v" else act)(["wx", "wy", "of"] + every("of%d" % i, c0, c1), every("gg%d" % i, c0, c1), T["gg%d" % i][:, 32 + 16 * c0:32 + 16 * c1],
+                                          T.w[:].indirect(T.of[:, ENT * i + c0:ENT * i + c1]))
 
         table(0)
         tabA = T.tab[:, 0:320:2]
-        if r:
-            table(1)
-        small("s")
-        small("s")
-        every = lambda k, c0=0, c1=ENT: [k + "_%d" % c for c in range(c0, c1, 2)]
-        scan(every("gt1") + ["gt1v", "gt1s", "tabA"], every("sc1"), T.sc1[:, 0:ROW], T.gt1[:, 0:ROW], tabA)
-        small("s")
-        small("s")
-        ts(every("sc1") + ["of"], every("of0"), T.of[0:32, 0:ENT], T.sc1[0:32, 7:ROW:16], BIAS, A.add)
-        vector_fill(-1)
-        runs = CHAIN[min(r, 1)]
-        for t in range(7):
+        table(1)
+        scan(every("gt1") + ["gt1v", "gt1s", "tabA"], every("even"), T.res[:, EVEN:EVEN + ROW], T.gt1[:, 0:ROW], tabA)
+        if r == 0:
+            ts(["lor", "c28"], ["tlo"], T.tlo[:], T.lor[:, 1:8:2], cc(28), A.add, 671.0, A.min)
+            first.pop(0)()
+        ts(every("even") + ["of"], every("of0"), T.of[0:32, 0:ENT], T.res[0:32, EVEN + 7:EVEN + ROW:16], BIAS, A.add)
+        if r == 0:
+            scales_of_u(1)
+            codes_of_u(1)
+            scores(1)
+        for t in range(3):
             i, a = t % 2, (t + 1) // 2
-            gg, gt, sc, o = "gg%d" % i, "gt%d" % i, "sc%d" % i, ENT * i
-            for e, c0, c1 in runs:
-                (cp if e == "v" else act)(["wa", "wb", "of"] + every("of%d" % i, c0, c1), every(gg, c0, c1), T[gg][:, 32 + 16 * c0:32 + 16 * c1],
-                                          T.w[:].indirect(T.of[:, o + c0:o + c1]))
-            if t < 6:
-                for e, c0, c1 in runs:
-                    turn(every(gg, c0, c1), every(gt, c0, c1), T[gt][:, 16 * c0:16 * c1], T[gg][:, 32 + 16 * c0:32 + 16 * c1])
-                    small(e)
-                scalar_fill(t)
-                for e, c0, c1 in runs:
-                    scan(every(gt, c0, c1) + ["tabA"], every(sc, c0, c1), T[sc][:, 16 * c0:16 * c1], T[gt][:, 16 * c0:16 * c1], T.tab[:, 32 * c0:32 * c1:2])
-                    small(e)
-                for e, c0, c1 in runs:
-                    if i:
-                        ts(every(sc, c0, c1), every("of0", c0, c1), T.of[32 * a:32 * a + 32, c0:c1], T[sc][32 * a:32 * a + 32, 16 * c0 + 7:16 * c1:16], BIAS, A.add)
-                    else:
-                        ts(every(sc, c0, c1), every("of1", c0, c1), T.of[32 * a + 32:32 * a + 64, ENT + c0:ENT + c1],
-                           T[sc][32 * a:32 * a + 32, 16 * c0 + 15:16 * c1:16], BIAS, A.add)
-                    small(e)
-                vector_fill(t)
-                if t == 5:
-                    turn(every(gg) + [gg + "a", gg + "b"], [gt + "b"], T[gt][:, 160:352], T[gg][:, 16:208])
+            gg, gt, sc, o = "gg%d" % i, "gt%d" % i, ("odd", "even")[i], (ODD, EVEN)[i]
+            pick(i, TWO)
+            if t == 0:
+                wait(t, 0)
+            for call in behind[t]:
+                call()
+            if t:
+                wait(t, 0)
+            turn(every(gg), every(gt), T[gt][:, 0:ROW], T[gg][:, 32:192])
+            wait(t, 1)
+            scan(every(gt) + ["tabA"], every(sc), T.res[:, o:o + ROW], T[gt][:, 0:ROW], tabA)
+            wait(t, 2)
+            if i:
+                ts(every(sc), every("of0"), T.of[32 * a:32 * a + 32, 0:ENT], T.res[32 * a:32 * a + 32, o + 7:o + ROW:16], BIAS, A.add)
             else:
-                scan(["gt1b", "tabB"], ["s5b"], T.sc1[:, ROW:336], T.gt1[:, 176:352], T.tab[:, 320:672:2])
-                scalar_fill(t)
-                turn(every(gg), every(gt), T[gt][:, 0:ROW], T[gg][:, 32:192])
-                turn(every(gg) + [gg + "a", gg + "b"], [gt + "b"], T[gt][:, 160:C], T[gg][:, 16:144])
-                scan(every(gt) + ["tabA"], ["s6a"], T.sc1[:, 336:496], T[gt][:, 0:ROW], tabA)
-                scan([gt + "b", "tabB"], ["s6b"], T.sc1[:, 496:624], T[gt][:, ROW:C], T.tab[:, 320:2 * C:2])
+                ts(every(sc), every("of1"), T.of[32 * a + 32:32 * a + 64, ENT:2 * ENT], T.res[32 * a:32 * a + 32, o + 15:o + ROW:16], BIAS, A.add)
+            wait(t, 3)
+            if r == 0:
+                for k in range(3):
+                    first.pop(0)()
+        pick(1, TWO)
+        for call in behind[3]:
+            call()
+        wait(3, 0)
+        turn(every("gg1"), every("gt1"), T.gt1[:, 0:ROW], T.gg1[:, 32:192])
+        wait(3, 1)
+        scan(every("gt1") + ["ytA"], ["s1A"], T.s1[late, 0:ROW], T.gt1[late, 0:ROW], T.yt[late, 0:ROW])
+        wait(3, 2)
+        scan(["s1A"] + to, ["od4"], T.res[late, OD4:OD4 + 40], T.s1[late, 3:ROW:4], T.to[late, 0:40])
+        wait(3, 3)
+        ts(["od4"], every("of1"), T.of[96:128, ENT:2 * ENT], T.res[64:96, OD4 + 3:OD4 + 40:4], BIAS, A.add)
+        wait(3, 4)
+        pick(1, TWO)
+        for call in behind[4]:
+            call()
+        if r == 0:
+            both_f(3)
+        turn(every("gg1"), every("gt1"), T.gt1[:, 0:ROW], T.gg1[:, 32:192])
+        turn(pads("gg1"), ["gt1b"], T.gt1[:, ROW:352], T.gg1[:, 16:208])
+        if r == 0:
+            first.pop(0)()
+        scan(every("gt1") + ["ytA"], ["s1A"], T.s1[late, 0:ROW], T.gt1[late, 0:ROW], T.yt[late, 0:ROW])
+        scan(["gt1b", "ytB"], ["s1B"], T.s1[late, ROW:2 * ROW], T.gt1[late, ROW:2 * ROW], T.yt[late, ROW:2 * ROW])
+        scan(every("gt1") + te, ["ev4"], T.res[late, EV4:EV4 + 40], T.gt1[late, 1:ROW:4], T.te[late, 0:40])
+        scan(["gt1b"] + te, ["ev4B"], T.res[late, EV4B:EV4B + 44], T.gt1[late, 177:352:4], T.te[late, 40:84])
+        scan(["s1A", "s1B"] + to, ["od4"], T.res[late, OD4:RES], T.s1[late, 3:2 * ROW:4], T.to[late, 0:80])
         ll = "ll%d" % r
-        ts(every("sc1") + ["s5b", "s6a", "s6b", "pmo"], [ll], T[ll][:], T.sc1[:].indirect(T.pmo[:]), BIAS, A.add)
+        ts(every("even") + every("odd") + ["evenB", "oddB", "ev4", "ev4B", "od4", "fin"], [ll], T[ll][:], T.res[:].indirect(T.fin[:]), BIAS, A.add)
         need("g", wr[ll])
         rid, pid = topo.addr(lst, core)
         es = topo.engines(core, lst)
@@ -469,11 +608,11 @@ def rank_program(g, core, T, topo):
             scan(["own", "mrow"], ["ms"], T.ms[:], T.own[:], T.mrow[:])
         shared(("wg", ["wg"]), ll, "be")
         if r == 0:
-            ts(["ms", "c19"], ["mh"], T.mh[:], T.ms[:, 15:C:16], cc(19), A.mult, ROUND, A.add)
-            ts(["mh"], ["mh"], T.mh[:], T.mh[:], BIAS - ROUND, A.add, 0.5, A.mult)
+            ts(["ms", "c19"], ["mh"], mh, T.ms[:, 15:C:16], cc(19), A.mult, ROUND, A.add)
+            ts(["mh"], ["mh"], mh, mh, BIAS - ROUND, A.add, 0.5, A.mult)
         shared(("be", ["bea", "beb"]), "mls", "bm")
         if r == 0:
-            tt(["mh", "ph", "ex"], ["avg"], T.ex[:, 2:54:3], T.ph[:], T.mh[:], A.add)
+            tt(["mh", "ph", "ex"], ["avg"], T.ex[:, 2:54:3], ph, mh, A.add)
         scan(["own", "bea", "beb"], ["hs1"], T.hs[:, 2:2 + 3 * C:3], T.own[:], T.be[:])
         if r == 0:
             scaled = spread("pI", T.pI[:])
@@ -488,9 +627,9 @@ def rank_program(g, core, T, topo):
         wr["al"] = [("aL_%d" % r, len(topo.engines(relays(partner, core, topo)[1], core)))]
         count["aq_%d" % r], count["aL_%d" % r] = wr["aq"][0][1], wr["al"][0][1]
         for b_ in range(4):
-            mm(["aq", "eq%d" % b_], (7 + b_) % 8, T.eq[:, 128 * b_:128 * b_ + 128], T.ep[:, 128 * b_:128 * b_ + 128], "aq%d" % r, "ap%d" % r)
+            mm(["aq", "eq%d" % b_], (0, 1, 2, 7)[b_], T.eq[:, 128 * b_:128 * b_ + 128], T.ep[:, 128 * b_:128 * b_ + 128], "aq%d" % r, "ap%d" % r)
         for b_ in range(4):
-            act(["ps%d" % ((7 + b_) % 8)], ["fp%d" % b_], T["fp%d" % b_][:], T["ps%d" % ((7 + b_) % 8)][:, 0:C])
+            act(["ps%d" % (0, 1, 2, 7)[b_]], ["fp%d" % b_], part("fp", b_), T["ps%d" % (0, 1, 2, 7)[b_]][:, 0:C])
         if r == 0:
             keep_f(3)
         if r < 2:
@@ -504,10 +643,10 @@ def rank_program(g, core, T, topo):
             dma("s", "out", 9, ["lo0", "lo1"], ["pl"], T.pl[:], T.lo[0:128:16, :])
         al, zt = T["al%d" % r], T.zt
         for b_ in (0, 2):
-            (cp if b_ < 2 else act)(["fp%d" % b_, "al"], ["zt%da" % b_, "zt%db" % b_], zt[:, b_:4 * C:4], T["fp%d" % b_][:].indirect(al[:]))
+            (cp if b_ < 2 else act)(["fp%d" % b_, "al"], ["zt%da" % b_, "zt%db" % b_], zt[:, b_:4 * C:4], part("fp", b_).indirect(al[:]))
         for h, (a0, b0) in enumerate(RUNS):
             for b_ in (1, 3):
-                (cp if b_ < 2 else act)(["fp%d" % b_, "al"], ["zt%d%s" % (b_, "ab"[h])], zt[:, 4 * a0 + b_:4 * b0:4], T["fp%d" % b_][:].indirect(al[:, a0 // 16:b0 // 16]))
+                (cp if b_ < 2 else act)(["fp%d" % b_, "al"], ["zt%d%s" % (b_, "ab"[h])], zt[:, 4 * a0 + b_:4 * b0:4], part("fp", b_).indirect(al[:, a0 // 16:b0 // 16]))
         halves(["zt%d" % b_ for b_ in range(4)], "zq", "zp", "zt")
         if r < 2:
             power(r + 1, 2)
@@ -521,15 +660,15 @@ def rank_program(g, core, T, topo):
             a0, b0 = RUNS[h] if h < 2 else (0, C)
             hb = "hb%d" % b_
             tt([hb + "a", hb + "b", "fo%d" % b_, ll], ["xn%d%s" % (b_, k) for k in ("a", "b", "ab")[h]], xn[:, 4 * a0 + b_:4 * b0:4],
-               T[hb][:].indirect(T[ll][:, a0 // 16:b0 // 16]), T["fo%d" % b_][:, a0:b0], A.add)
+               part("hb", b_).indirect(T[ll][:, a0 // 16:b0 // 16]), part("fo", b_, a0, b0), A.add)
 
         for b_ in range(4):
             hb = "hb%d" % b_
             if b_ == 0:
                 for h, (a0, b0) in enumerate(RUNS):
-                    act(["ps%d" % (3 + 4 * h)], [hb + "ab"[h]], T[hb][:, a0:b0], T["ps%d" % (3 + 4 * h)][:, 0:b0 - a0], scale=0.03125)
+                    act(["ps%d" % (3 + 4 * h)], [hb + "ab"[h]], part("hb", b_, a0, b0), T["ps%d" % (3 + 4 * h)][:, 0:b0 - a0], scale=0.03125)
             else:
-                act(["ps%d" % (3 + b_)], [hb + "a", hb + "b"], T[hb][:], T["ps%d" % (3 + b_)][:, 0:C], scale=0.03125)
+                act(["ps%d" % (3 + b_)], [hb + "a", hb + "b"], part("hb", b_), T["ps%d" % (3 + b_)][:, 0:C], scale=0.03125)
         if r < 2:
             for b_, h in ((0, 2), (1, 2), (2, 2), (3, 0), (3, 1)):
                 state(b_, h)

@@ -30,7 +30,7 @@ SCRATCH = {
     "own": ("sbuf", [128, C], "bfloat16"), "lane": ("sbuf", [128, 18], "uint16"), "half": ("sbuf", [128, 8], "float32"),
     "ulf": ("sbuf", [128, 16], "float32"), "ull": ("sbuf", [128, 24], "uint16"), "base": ("sbuf", [128, C], "bfloat16"),
     "fr": ("sbuf", [128, 64], "float32"), "ft": ("sbuf", [128, 64], "float32"), "fin": ("sbuf", [128, 2], "uint16"), "tlo": ("sbuf", [128, 4], "uint16"),
-    "four": ("sbuf", [128, 256], "bfloat16"),
+    "four": ("sbuf", [128, 384], "bfloat16"),
     "mls": ("sbuf", [128, 18], "uint16"), "k20": ("sbuf", [128, 20], "uint16"),
     "kf": ("sbuf", [128, 18], "float32"), "ke": ("sbuf", [128, 40], "float32"),
     "y1": ("sbuf", [128, C], "bfloat16"), "y2": ("sbuf", [128, C], "bfloat16"), "y3": ("sbuf", [128, C], "bfloat16"),
@@ -84,9 +84,9 @@ def bits(es):
 
 def place(a, y, e):
     odd, back = e % 2, e + 1 if e < 10 else e - 10
-    if a < 2:
+    if a == 0:
         return EVEN + 160 * odd + 16 * back + 7 if y == 0 else ODD + 16 * min(e, 17) + 15
-    if a == 2:
+    if a != 2:
         return EV4 + 40 * odd + 4 * back + 3 if y == 0 else OD4 + 40 * (1 - odd) + 4 * (back - odd) + 3
     return (EV4B if e < 10 else EV4) + 4 * back + 3 if y == 0 else OD4 + 4 * e + 3
 
@@ -249,22 +249,21 @@ def rank_program(g, core, T, topo):
     iota("ulf2", T.ulf[:, 8:16], [[16, 8]], 0)
     iota("idr", T.idr[:], [[1, C]], -144)
     fill("half", T.half[:], 0.5)
-    fill("ones", T.ones[:], 1.0)
-    op("g", ["ones"], ["e0"], lambda: g.affine_select(T.e0[:], T.ones[:], [[1, 516]], A.is_equal, 0.0, -3, -4))
-    op("g", ["ones"], ["four"], lambda: g.affine_select(T.four[:], T.ones[:, 0:256], [[0, 64], [1, 4]], A.is_gt, 0.0, 0, 0))
+    fill("of", T.of[:], 0)
+    fill("ke", T.ke[:], 0.0)
+    op("v", ["half"], ["pw"], lambda: g.vector.tensor_tensor_scan(T.pw[:], T.half[:], T.half[:], 256.0, A.mult, A.max))
+    fill("ones", T.ones[:, 0:256], 1.0)
+    ts(["pf", "pw"], ["bi"], T.bi[:], T.pw[:], T.pf[:], A.mult)
+    fill("ones2", T.ones[:, 256:516], 1.0)
+    op("g", ["ones", "ones2"], ["e0"], lambda: g.affine_select(T.e0[:], T.ones[:], [[1, 516]], A.is_equal, 0.0, -3, -4))
+    op("g", ["ones", "ones2"], ["four"], lambda: g.affine_select(T.four[:], T.ones[:, 0:384], [[0, 96], [1, 4]], A.is_gt, 0.0, 0, 0))
     b = lambda i: T.bit[:, i:i + 1]
     nb = lambda i: T.nb[:, i:i + 1]
     sg = lambda i: T.sg[:, i:i + 1]
     cc = lambda j: T.cst[:, j:j + 1]
-    op("v", ["half"], ["pw"], lambda: g.vector.tensor_tensor_scan(T.pw[:], T.half[:], T.half[:], 256.0, A.mult, A.max))
-    fill("of", T.of[:], 0)
-    fill("ke", T.ke[:], 0.0)
-    ts(["pf", "pw"], ["bi"], T.bi[:], T.pw[:], T.pf[:], A.mult)
-    fill("ex", T.ex[:], 0.0)
-    fill("sg5", T.sg[:, 5:6], 1.0)
     ts(["bi"], ["bj"], T.bj[:, 0:7], T.bi[:, 0:7], 7, A.logical_shift_right, 1, A.bitwise_and)
     ts(["bi"], ["bj7"], T.bj[:, 7:8], T.bi[:, 7:8], 15, A.bitwise_and)
-    fill("hs0", T.hs[:, 31:880:48], 0.0)
+    fill("sg5", T.sg[:, 5:6], 1.0)
     cp(["bj"], ["bit"], T.bit[:, 0:7], T.bj[:, 0:7])
     ts(["bj"], ["nb"], T.nb[:, 0:7], T.bj[:, 0:7], -1.0, A.mult, 1.0, A.add)
     ts(["bj"], ["sg"], T.sg[:, 0:4], T.bj[:, 0:4], 2.0, A.mult, -1.0, A.add)
@@ -280,9 +279,11 @@ def rank_program(g, core, T, topo):
         if i == 1:
             tt(["sel4", "sel12"], ["sel"], T.sel[:, 0:4], T.sel[:, 4:8], T.sel[:, 12:16], A.add)
     whole = ["sel"] + ["base%d" % i for i in range(4)]
-    cp(["pI"], ["pls0"], T.pls0[:], T.pI[:])
+    fill("ex", T.ex[:], 0.0)
+    fill("hs0", T.hs[:, 31:880:48], 0.0)
     ts(whole, ["dg3"], T.dg3[:], T.base[:], T.sel[:, 3:4], A.mult)
     ts(whole, ["dg2"], T.dg2[:], T.base[:], T.sel[:, 2:3], A.mult)
+    cp(["pI"], ["pls0"], T.pls0[:], T.pI[:])
 
     def line(key, x, s, c=None, part=slice(0, 128)):
         col = lambda v: T[v[1]][part, v[2]:v[2] + 1] if isinstance(v, tuple) else v
@@ -294,7 +295,7 @@ def rank_program(g, core, T, topo):
     NB = lambda j: ("nb", "nb", j)
     SG = lambda j: ("sg", "sg", j)
     ONE = ("ones", "ones", 0)
-    late = slice(64, 128)
+    late, early = slice(0, 128), slice(0, 32)
     plain("tra", T.tr[:, 16:32], 16, 0.0)
     plain("trb", T.tr[:, 352:368], 16, 0.0)
     plain("c17", cc(17), 1, -1e-29)
@@ -307,10 +308,10 @@ def rank_program(g, core, T, topo):
     plain("gt1v", T.gt1[:, 0:ROW:8], 2 * ENT, 0.0)
     plain("gt1s", T.gt1[:, 4:ROW:16], ENT, -1.0)
     plain("ysa", T.ys[:, 3:64:4], 16, 0.0)
-    line(2, NB(4), 1.0, part=slice(0, 64))
+    line(2, B(5), 1.0)
     line(26, B(0), -672.0, K(23))
     line(25, B(0), 320.0)
-    line(2, NB(5), 1.0, part=late)
+    line(2, NB(4), 1.0, part=early)
     line(32, SG(0), SG(2))
     line(33, NB(2), NB(3))
     line(34, NB(0), NB(1))
@@ -345,6 +346,7 @@ def rank_program(g, core, T, topo):
             turn(["tr1", "tr2", "tra", "trb"], ["tabB"], T.tab[:, 320:672], T.tr[:, 16:368])
 
     cp(["kI"], ["kf"], T.kf[:], T.kI[:])
+    cp(["ulf2"], ["ull2"], T.ull[:, 16:24], T.ulf[:, 8:16])
     power(0, 0)
     for h in range(2):
         for y in range(2):
@@ -358,7 +360,6 @@ def rank_program(g, core, T, topo):
     ts(["nb"], ["c6"], cc(6), nb(3), nb(5), A.mult, nb(6), A.mult)
     ts(["nb", "bit"], ["c7"], cc(7), nb(0), nb(1), A.mult, b(2), A.mult)
     power(0, 1)
-    early = slice(0, 64)
     line(15, B(3), 16.0, K(7))
     act(whole, ["dg0"], T.dg0[:], T.base[:], scale=T.sel[:, 0:1])
     line(8, K(5), -1.0, NB(0))
@@ -370,26 +371,27 @@ def rank_program(g, core, T, topo):
     line(14, K(13), -1e-29, part=late)
     line(11, K(9), K(6), B(0))
     line(13, K(43), 1.0, part=early)
-    act(["idr", "pls0"], ["prow"], T.prow[:], T.idr[:].indirect(T.pls0[:]))
     line(14, K(43), -1e-29, K(11), early)
     quant(["xt"], ["q0a", "q0b"], T.q0[:], T.qp0[:], T.xt[:])
     tt(["ke0", "ke1", "ke2", "ke3", "ko0", "ko1"], ["ke"], T.ke[:, 0:20], T.ke[:, 0:20], T.ke[:, 20:40], A.add)
-    ts(["ulf", "c15"], ["ull0"], T.ull[:, 0:4], T.ulf[:, 0:4], cc(15), A.add, 0.0, A.max)
+    ts(["ulf", "c15"], ["ull0"], T.ull[:, 0:2], T.ulf[:, 0:2], cc(15), A.add, 0.0, A.max)
+    ts(["ulf", "c42"], ["ull0b"], T.ull[:, 2:8], T.ulf[:, 2:8], cc(42), A.add)
+    quant(["ut"], ["uq", "up"], T.uq[:], T.up[:], T.ut[:])
     power(0, 2)
     cp(["ke"], ["k20"], T.k20[:], T.ke[:, 0:20])
-    ts(["ulf", "c42", "ull0"], ["ull0"], T.ull[:, 4:8], T.ulf[:, 4:8], cc(42), A.add)
-    quant(["ut"], ["uq", "up"], T.uq[:], T.up[:], T.ut[:])
     ts(["ulf", "c31"], ["ull1"], T.ull[:, 8:16], T.ulf[:, 0:8], cc(31), A.add, 16.0, A.add)
 
     def codes_of_u(i):
-        cp(["uq", "ull%d" % i], ["u%dq" % i], T["u%dq" % i][:].bitcast(dt.uint32), T.uq[:].bitcast(dt.uint32).indirect(T.ull[:, 8 * i:8 * i + 8]))
+        cp(["uq", "ull0b", "ull%d" % i], ["u%dq" % i], T["u%dq" % i][:].bitcast(dt.uint32), T.uq[:].bitcast(dt.uint32).indirect(T.ull[:, 8 * i:8 * i + 8]))
 
     def scales_of_u(i):
-        act(["up", "ull%d" % i], ["u%dp" % i], T["u%dp" % i][:], T.up[:].indirect(T.ull[:, 8 * i:8 * i + 8]))
+        act(["up", "ull0b", "ull%d" % i], ["u%dp" % i], T["u%dp" % i][:], T.up[:].indirect(T.ull[:, 8 * i:8 * i + 8]))
 
     scales_of_u(0)
     codes_of_u(0)
-    starts(10)
+    starts(4)
+    ts(["lor", "c28"], ["tlo"], T.tlo[:], T.lor[:, 1:8:2], cc(28), A.add, 671.0, A.min)
+    scales_of_u(1)
 
     def unit(b):
         quant(["e0"], ["eq%d" % b], T.eq[:, 128 * b:128 * b + 128], T.ep[:, 128 * b:128 * b + 128], T.e0[:, 3 - b:515 - b])
@@ -429,8 +431,9 @@ def rank_program(g, core, T, topo):
         g.remote_dma_fused(fc, local_sem=T.sem.left)
         g.remote_dma_fused(fs, local_sem=T.sem.left)
         if r == 0:
-            for a, p0, p1 in ((0, 0, 64), (2, 64, 96), (3, 96, 128)):
-                if a == 2:
+            for a in range(4):
+                p0, p1 = 32 * a, 32 * a + 32
+                if a == 1:
                     need("g", [("sg", count["sg"])])
                 for k in range(2):
                     for i0, n, pattern, first in pieces([place(a, y, 16 * k + i) for y in range(2) for i in range(16)]):
@@ -441,7 +444,10 @@ def rank_program(g, core, T, topo):
             mm(both + ["eq%d" % b], 3 + b, T.eq[:, 128 * b:128 * b + 128], T.ep[:, 128 * b:128 * b + 128], q, qp)
 
         def scores(i):
-            mm(both + ["u%dq" % i, "u%dp" % i], (0, 2, 7)[i], T["u%dq" % i][:], T["u%dp" % i][:], q, qp)
+            if i == 2:
+                return mm(both + ["u2q", "u2p"], 0, T.u2q[:], T.u2p[:], q, qp)
+            for h, (a0, b0) in enumerate(RUNS):
+                mm([both[h], "u1q", "u1p"], (2, 7)[h], T.u1q[:], T.u1p[:], q, qp, a0, b0)
 
         def keep_f(b):
             act(["ps%d" % (3 + b)], ["fo%d" % b], part("fo", b), T["ps%d" % (3 + b)][:, 0:C])
@@ -450,21 +456,22 @@ def rank_program(g, core, T, topo):
             mm([both[h], "u0q", "u0p"], h, T.u0q[:], T.u0p[:], q, qp, a0, b0)
         if r:
             scores(1)
+        for h, (a0, b0) in enumerate(RUNS):
+            act(["ps%d" % h, "c13", "c14"], ["w" + "xy"[h]], T.w[:, a0:b0], T["ps%d" % h][:, 0:b0 - a0], F.Sign, scale=cc(13), bias=cc(14))
+        if r:
             scores(2)
             for b_ in range(4):
                 own_f(b_)
-        for h, (a0, b0) in enumerate(RUNS):
-            act(["ps%d" % h, "c13", "c14"], ["w" + "xy"[h]], T.w[:, a0:b0], T["ps%d" % h][:, 0:b0 - a0], F.Sign, scale=cc(13), bias=cc(14))
 
         def lists():
             ts(["tabA", "tabB", "tlo"], ["tl"], T.tl[:], T.tab[:].indirect(T.tlo[:]), BIAS, A.add)
 
         def ahead(n, c0=0, c1=ENT):
             out, src = T.gi[:, 64 * c0 + n:64 * c1:4], T.wa[:].indirect(T.tl[:, 16 * n + c0:16 * n + c1])
-            if n < 3:
-                act(["wa", "tl", "c%d" % (36 + n)], every("gi%d" % n), out, src, scale=cc(36 + n))
+            if n < 2 or (n, c1) == (2, ENT):
+                act(["wa0", "wa1", "tl", "c%d" % (36 + n)], every("gi%d" % n, c0, c1), out, src, scale=cc(36 + n))
             else:
-                ts(["wa", "tl"], every("gi3", c0, c1), out, src, 0.25, A.mult)
+                ts(["wa0", "wa1", "tl", "c38"], every("gi%d" % n, c0, c1), out, src, cc(38) if n == 2 else 0.25, A.mult)
 
         def summed(c0, c1):
             scan(["four"] + [k for n in range(4) for k in every("gi%d" % n, c0, c1)], every("ys", c0, c1),
@@ -488,7 +495,6 @@ def rank_program(g, core, T, topo):
             lambda: ts(["lor", "c16"], ["d16a"], T.d16[:, 0:16], T.lor[:, 0:16], cc(16), A.not_equal),
             lambda: ts(["lor", "c16"], ["d16b"], T.d16[:, 16:32], T.lor[:, 16:32], cc(16), A.is_equal, 65535.0, A.mult),
             lambda: ts(["ones", "c16"], ["lane"], T.lane[:], T.ones[:, 0:18], cc(16), A.mult),
-            lambda: cp(["ulf2"], ["ull2"], T.ull[:, 16:24], T.ulf[:, 8:16]),
             lambda: tt(["d16a", "d16b"], ["d16"], T.d16[:, 32:48], T.d16[:, 0:16], T.d16[:, 16:32], A.add),
             lambda: ts(["c16"], ["c19"], cc(19), cc(16), 15.0, A.is_equal, 2.0 ** -16, A.max),
             lambda: ts(["c16"], ["c20"], cc(20), cc(16), 15.0, A.is_equal, 2.0 ** -32, A.max),
@@ -502,30 +508,28 @@ def rank_program(g, core, T, topo):
 
         P = lambda h, k: (lambda: pack(h, k))
         waits = {
-            (0, 0): [lists], (0, 1): [P(1, 0), P(1, 1)], (0, 2): [P(1, 2), P(1, 3)], (0, 3): [P(0, 0), P(0, 1)],
-            (1, 0): [lambda: ahead(3, 0, 4)], (1, 1): [lambda: ahead(3, 4, 8)], (1, 2): [lambda: ahead(3, 8, ENT)], (1, 3): [P(0, 2), P(0, 3)],
-            (2, 1): [lambda: summed(0, 4)], (2, 2): [lambda: summed(4, 8)], (2, 3): [lambda: summed(8, ENT), lambda: turn(pads("gg0"), ["gt0b"], T.gt0[:, ROW:C], T.gg0[:, 16:144])],
-            (2, 0): [lambda: turn(pads("gg1"), ["gt1b"], T.gt1[:, ROW:352], T.gg1[:, 16:208])],
-            (3, 0): [lambda: turned(0)],
-            (3, 1): [lambda: scan(["gt1b", "tabB"], ["evenB"], T.res[:, EVENB:EVENB + 176], T.gt1[:, 176:352], T.tab[:, 320:672:2])],
-            (3, 2): [lambda: turned(1)],
-            (3, 3): [lambda: scan(["gt0b", "tabB"], ["oddB"], T.res[:, ODDB:ODDB + 128], T.gt0[:, ROW:C], T.tab[:, 320:2 * C:2])],
+            (0, 0): [lambda: ahead(3, 0, 4)], (0, 1): [lambda: ahead(3, 4, ENT)], (0, 2): [lambda: ahead(2, 0, 4)], (0, 3): [P(1, 2), lambda: summed(0, 4)],
+            (1, 0): [lambda: summed(4, ENT)], (1, 1): [lambda: turned(0), P(1, 3)],
+            (1, 2): [lambda: turn(pads("gg1"), ["gt1b"], T.gt1[:, ROW:352], T.gg1[:, 16:208])], (1, 3): [lambda: turned(1), P(0, 1)],
+            (1, 4): [lambda: turn(pads("gg0"), ["gt0b"], T.gt0[:, ROW:C], T.gg0[:, 16:144]), P(0, 0)],
+            (2, 0): [lambda: scan(["gt0b", "tabB"], ["oddB"], T.res[:, ODDB:ODDB + 128], T.gt0[:, ROW:C], T.tab[:, 320:2 * C:2]), P(0, 2)],
+            (2, 1): [lambda: scan(["gt1b", "tabB"], ["evenB"], T.res[:, EVENB:EVENB + 176], T.gt1[:, 176:352], T.tab[:, 320:672:2])],
+            (2, 2): [P(0, 3)],
         }
-        behind = {0: [lambda: act(["ps2", "c29", "c30"], ["wa"], T.wa[:], T.ps2[:, 0:C], F.Sign, scale=cc(29), bias=cc(30)), lambda: ahead(0)],
-                  1: [lambda: ahead(1), lambda: ahead(2)]}
-        signs = lambda: act(["ps7", "c17"], ["wg"], T.wg[:], T.ps7[:, 0:C], F.Sign, bias=cc(17))
+        behind = {0: [lambda: ahead(0), lambda: ahead(1), lambda: ahead(2, 4, ENT)]}
+        signs = lambda: act(["ps0", "c17"], ["wg"], T.wg[:], T.ps0[:, 0:C], F.Sign, bias=cc(17))
         if r:
-            behind.update({2: [signs, lambda: keep_f(0)], 3: [lambda: keep_f(1), lambda: keep_f(2)], 4: [lambda: keep_f(3)]})
+            behind.update({1: [signs, lambda: keep_f(0), lambda: keep_f(1)], 2: [lambda: keep_f(2), lambda: keep_f(3)], 3: []})
         else:
-            behind.update({2: [lambda: scales_of_u(2), lambda: act(["prow", "mls"], ["mrow"], T.mrow[:], T.prow[:].indirect(T.mls[:]))],
-                           3: [lambda: act(["d16", "lane"], ["own"], T.own[:], T.d16[:, 32:48].indirect(T.lane[:])), signs],
-                           4: [lambda: keep_f(0), lambda: keep_f(1), lambda: keep_f(2)]})
-            waits[2, 0] += [lambda: codes_of_u(2), lambda: scores(2)]
-            waits[1, 3] = [lambda: both_f(0)]
-            waits[3, 0] += [P(0, 2)]
-            waits[3, 1] += [P(0, 3)]
-            waits[3, 3] += [lambda: both_f(1)]
-            waits[3, 4] = [lambda: both_f(2)]
+            behind.update({1: [lambda: scales_of_u(2), lambda: act(["idr", "pls0"], ["prow"], T.prow[:], T.idr[:].indirect(T.pls0[:]))],
+                           2: [lambda: act(["prow", "mls"], ["mrow"], T.mrow[:], T.prow[:].indirect(T.mls[:])), signs],
+                           3: [lambda: act(["d16", "lane"], ["own"], T.own[:], T.d16[:, 32:48].indirect(T.lane[:]))]})
+            waits[2, 3] = waits[1, 4] + [waits[2, 0][0]]
+            waits[2, 0] = [P(0, 2)]
+            waits[1, 4] = [lambda: codes_of_u(2), lambda: scores(2)]
+            for t, k, n in ((1, 1, 1), (1, 2, 1), (1, 3, 1), (2, 0, 2), (2, 1, 1), (2, 2, 2), (2, 3, 1)):
+                waits[t, k] = waits.get((t, k), []) + n * [lambda: first.pop(0)()]
+            waits[2, 4] = [lambda: both_f(0), lambda: both_f(1)]
 
         def wait(t, k):
             for call in waits.get((t, k), []):
@@ -536,57 +540,47 @@ def rank_program(g, core, T, topo):
                 (cp if e == "v" else act)(["wx", "wy", "of"] + every("of%d" % i, c0, c1), every("gg%d" % i, c0, c1), T["gg%d" % i][:, 32 + 16 * c0:32 + 16 * c1],
                                           T.w[:].indirect(T.of[:, ENT * i + c0:ENT * i + c1]))
 
+        if r == 0:
+            codes_of_u(1)
+            scores(1)
         table(0)
         tabA = T.tab[:, 0:320:2]
         table(1)
         scan(every("gt1") + ["gt1v", "gt1s", "tabA"], every("even"), T.res[:, EVEN:EVEN + ROW], T.gt1[:, 0:ROW], tabA)
-        if r == 0:
-            ts(["lor", "c28"], ["tlo"], T.tlo[:], T.lor[:, 1:8:2], cc(28), A.add, 671.0, A.min)
-            first.pop(0)()
+        lists()
         ts(every("even") + ["of"], every("of0"), T.of[0:32, 0:ENT], T.res[0:32, EVEN + 7:EVEN + ROW:16], BIAS, A.add)
-        if r == 0:
-            scales_of_u(1)
-            codes_of_u(1)
-            scores(1)
-        for t in range(3):
-            i, a = t % 2, (t + 1) // 2
-            gg, gt, sc, o = "gg%d" % i, "gt%d" % i, ("odd", "even")[i], (ODD, EVEN)[i]
-            pick(i, TWO)
-            if t == 0:
-                wait(t, 0)
-            for call in behind[t]:
+        pack(1, 0)
+        pack(1, 1)
+        for h, (a0, b0) in enumerate(RUNS):
+            act(["ps%d" % (2, 7)[h], "c29", "c30"], ["wa%d" % h], T.wa[:, a0:b0], T["ps%d" % (2, 7)[h]][:, 0:b0 - a0], F.Sign, scale=cc(29), bias=cc(30))
+        pick(0, (("v", 0, ENT),))
+        for call in behind[0]:
+            call()
+        wait(0, 0)
+        turn(every("gg0"), every("gt0"), T.gt0[:, 0:ROW], T.gg0[:, 32:192])
+        wait(0, 1)
+        scan(every("gt0") + ["tabA"], every("odd"), T.res[:, ODD:ODD + ROW], T.gt0[:, 0:ROW], tabA)
+        wait(0, 2)
+        ts(every("odd"), every("of1"), T.of[32:64, ENT:2 * ENT], T.res[0:32, ODD + 15:ODD + ROW:16], BIAS, A.add)
+        wait(0, 3)
+        for a in (1, 2):
+            pick(1, TWO if a == 2 else (("s", 4, ENT), ("v", 0, 4)))
+            for call in behind[a]:
                 call()
-            if t:
-                wait(t, 0)
-            turn(every(gg), every(gt), T[gt][:, 0:ROW], T[gg][:, 32:192])
-            wait(t, 1)
-            scan(every(gt) + ["tabA"], every(sc), T.res[:, o:o + ROW], T[gt][:, 0:ROW], tabA)
-            wait(t, 2)
-            if i:
-                ts(every(sc), every("of0"), T.of[32 * a:32 * a + 32, 0:ENT], T.res[32 * a:32 * a + 32, o + 7:o + ROW:16], BIAS, A.add)
-            else:
-                ts(every(sc), every("of1"), T.of[32 * a + 32:32 * a + 64, ENT:2 * ENT], T.res[32 * a:32 * a + 32, o + 15:o + ROW:16], BIAS, A.add)
-            wait(t, 3)
-            if r == 0:
-                for k in range(3):
-                    first.pop(0)()
+            wait(a, 0)
+            turn(every("gg1"), every("gt1"), T.gt1[:, 0:ROW], T.gg1[:, 32:192])
+            wait(a, 1)
+            scan(every("gt1") + ["ytA"], ["s1A"], T.s1[late, 0:ROW], T.gt1[late, 0:ROW], T.yt[late, 0:ROW])
+            wait(a, 2)
+            scan(["s1A"] + to, ["od4"], T.res[late, OD4:OD4 + 40], T.s1[late, 3:ROW:4], T.to[late, 0:40])
+            wait(a, 3)
+            ts(["od4"], every("of1"), T.of[32 * a + 32:32 * a + 64, ENT:2 * ENT], T.res[32 * a:32 * a + 32, OD4 + 3:OD4 + 40:4], BIAS, A.add)
+            wait(a, 4)
         pick(1, TWO)
         for call in behind[3]:
             call()
-        wait(3, 0)
-        turn(every("gg1"), every("gt1"), T.gt1[:, 0:ROW], T.gg1[:, 32:192])
-        wait(3, 1)
-        scan(every("gt1") + ["ytA"], ["s1A"], T.s1[late, 0:ROW], T.gt1[late, 0:ROW], T.yt[late, 0:ROW])
-        wait(3, 2)
-        scan(["s1A"] + to, ["od4"], T.res[late, OD4:OD4 + 40], T.s1[late, 3:ROW:4], T.to[late, 0:40])
-        wait(3, 3)
-        ts(["od4"], every("of1"), T.of[96:128, ENT:2 * ENT], T.res[64:96, OD4 + 3:OD4 + 40:4], BIAS, A.add)
-        wait(3, 4)
-        pick(1, TWO)
-        for call in behind[4]:
-            call()
         if r == 0:
-            both_f(3)
+            both_f(2)
         turn(every("gg1"), every("gt1"), T.gt1[:, 0:ROW], T.gg1[:, 32:192])
         turn(pads("gg1"), ["gt1b"], T.gt1[:, ROW:352], T.gg1[:, 16:208])
         if r == 0:
@@ -605,13 +599,16 @@ def rank_program(g, core, T, topo):
         left[0] += len(es)
         pn = "pls%d" % (r + 1)
         if r == 0:
+            both_f(3)
             scan(["own", "mrow"], ["ms"], T.ms[:], T.own[:], T.mrow[:])
         shared(("wg", ["wg"]), ll, "be")
         if r == 0:
+            keep_f(0)
             ts(["ms", "c19"], ["mh"], mh, T.ms[:, 15:C:16], cc(19), A.mult, ROUND, A.add)
             ts(["mh"], ["mh"], mh, mh, BIAS - ROUND, A.add, 0.5, A.mult)
         shared(("be", ["bea", "beb"]), "mls", "bm")
         if r == 0:
+            keep_f(1)
             tt(["mh", "ph", "ex"], ["avg"], T.ex[:, 2:54:3], ph, mh, A.add)
         scan(["own", "bea", "beb"], ["hs1"], T.hs[:, 2:2 + 3 * C:3], T.own[:], T.be[:])
         if r == 0:
@@ -631,6 +628,7 @@ def rank_program(g, core, T, topo):
         for b_ in range(4):
             act(["ps%d" % (0, 1, 2, 7)[b_]], ["fp%d" % b_], part("fp", b_), T["ps%d" % (0, 1, 2, 7)[b_]][:, 0:C])
         if r == 0:
+            keep_f(2)
             keep_f(3)
         if r < 2:
             power(r + 1, 0)

from concourse.bass import DstId, RemoteDMATransfer
from concourse.mybir import dt, AluOpType, ActivationFunctionType

N = 8
C = 288
STEP = [4, 1, 2]
HALF = C // 2
ENT = 10
ROW = 16 * ENT
RUNS = ((0, 160), (160, C))
TWO = (("s", 6, ENT), ("v", 0, 6))
THREE = (("s", 0, 4), ("v", 4, 8), ("t", 8, ENT))
WHOLE = (("s", 0, ENT),)
BIAS = 144.0
EVEN, EVENB, ODD, ODDB, EV4, EV4B, OD4, OD4B, RES = 0, 160, 336, 496, 624, 664, 708, 748, 788

SCRATCH = {
    "zt": ("sbuf", [128, 4 * C], "bfloat16"), "zq": ("sbuf", [128, C], "float8_e4m3fn_x4"), "zp": ("sbuf", [128, C], "uint8"),
    "xt": ("sbuf", [128, 4 * C], "bfloat16"), "ut": ("sbuf", [128, 512], "bfloat16"), "vt": ("sbuf", [128, 512], "bfloat16"),
    "pI": ("sbuf", [128, 18], "int32"), "kI": ("sbuf", [128, 18], "int32"), "mI": ("sbuf", [128, 18], "int32"),
    "wq": ("sbuf", [128, 512], "float8_e4m3fn_x4"), "wp": ("sbuf", [128, 512], "uint8"),
    "uq": ("sbuf", [128, 128], "float8_e4m3fn_x4"), "up": ("sbuf", [128, 128], "uint8"),
    "vq": ("sbuf", [128, 128], "float8_e4m3fn_x4"), "vp": ("sbuf", [128, 128], "uint8"),
    "ones": ("sbuf", [128, 516], "bfloat16"), "e0": ("sbuf", [128, 516], "bfloat16"),
    "eq": ("sbuf", [128, 512], "float8_e4m3fn_x4"), "ep": ("sbuf", [128, 512], "uint8"),
    "pf": ("sbuf", [128, 1], "float32"), "pw": ("sbuf", [128, 8], "float32"), "bi": ("sbuf", [128, 8], "int32"), "bj": ("sbuf", [128, 8], "int32"),
    "bit": ("sbuf", [128, 8], "float32"), "sg": ("sbuf", [128, 8], "float32"), "nb": ("sbuf", [128, 8], "float32"),
    "cst": ("sbuf", [128, 48], "float32"), "quart": ("sbuf", [128, 72], "float32"), "sel": ("sbuf", [128, 16], "float32"),
    "idr": ("sbuf", [128, C], "bfloat16"), "lor": ("sbuf", [128, 32], "float32"), "d16": ("sbuf", [128, 48], "float32"),
    "own": ("sbuf", [128, C], "bfloat16"), "lane": ("sbuf", [128, 18], "uint16"), "half": ("sbuf", [128, 8], "float32"),
    "ulf": ("sbuf", [128, 16], "float32"), "ull": ("sbuf", [128, 24], "uint16"), "base": ("sbuf", [128, C], "bfloat16"),
    "fr": ("sbuf", [128, 64], "float32"), "ft": ("sbuf", [128, 64], "float32"), "fin": ("sbuf", [128, 2], "uint16"), "tlo": ("sbuf", [128, 4], "uint16"),
    "four": ("sbuf", [128, 384], "bfloat16"),
    "mls": ("sbuf", [128, 18], "uint16"), "k20": ("sbuf", [128, 20], "uint16"),
    "kf": ("sbuf", [128, 18], "float32"), "ke": ("sbuf", [128, 40], "float32"),
    "y1": ("sbuf", [128, C], "bfloat16"), "y2": ("sbuf", [128, C], "bfloat16"), "y3": ("sbuf", [128, C], "bfloat16"),
    "tr": ("sbuf", [128, 368], "bfloat16"), "tab": ("sbuf", [128, 672], "bfloat16"),
    "te": ("sbuf", [128, 84], "float32"), "to": ("sbuf", [128, 84], "float32"), "tl": ("sbuf", [128, 64], "uint16"),
    "w": ("sbuf", [128, C], "bfloat16"), "wg": ("sbuf", [128, C], "bfloat16"), "wa": ("sbuf", [128, C], "bfloat16"),
    "of": ("sbuf", [128, 2 * ENT], "uint16"), "res": ("sbuf", [128, RES], "bfloat16"),
    "gi": ("sbuf", [128, 4 * ROW], "bfloat16"), "ys": ("sbuf", [128, 4 * 192], "bfloat16"),
    "yt": ("sbuf", [128, 2 * ROW], "bfloat16"), "s1": ("sbuf", [128, 2 * ROW], "bfloat16"),
    "be": ("sbuf", [128, C], "bfloat16"), "bm": ("sbuf", [128, C], "bfloat16"), "hs": ("sbuf", [128, 880], "bfloat16"),
    "prow": ("sbuf", [128, C], "bfloat16"), "mrow": ("sbuf", [128, C], "bfloat16"), "ms": ("sbuf", [128, C], "float32"),
    "ex": ("sbuf", [128, 54], "float32"), "pn": ("sbuf", [128, 54], "float32"), "hd": ("sbuf", [128, 54], "float32"),
    "fo": ("sbuf", [128, 4 * C], "bfloat16"), "fp": ("sbuf", [128, 4 * C], "bfloat16"), "hb": ("sbuf", [128, 4 * C], "float32"),
    "yo": ("sbuf", [128, C], "float32"), "lo": ("sbuf", [128, 2 * C], "float32"),
}
for _i in range(2):
    SCRATCH["gg%d" % _i] = ("sbuf", [128, 208], "bfloat16")
    SCRATCH["gt%d" % _i] = ("sbuf", [128, 352], "bfloat16")
for _i in range(4):
    SCRATCH["dg%d" % _i] = ("sbuf", [128, C], "bfloat16")
    SCRATCH["pls%d" % _i] = ("sbuf", [128, 18], "uint16")
    SCRATCH["q%d" % _i] = ("sbuf", [128, C], "float8_e4m3fn_x4")
    SCRATCH["qp%d" % _i] = ("sbuf", [128, C], "uint8")
for _i in range(8):
    SCRATCH["ps%d" % _i] = ("psum", [128, 512], "float32")
for _i in range(3):
    SCRATCH["u%dq" % _i] = ("sbuf", [128, 128], "float8_e4m3fn_x4")
    SCRATCH["u%dp" % _i] = ("sbuf", [128, 128], "uint8")
    SCRATCH["xn%d" % _i] = ("sbuf", [128, 4 * C], "bfloat16")
    SCRATCH["aq%d" % _i] = ("sbuf", [128, C], "float8_e4m3fn_x4")
    SCRATCH["ap%d" % _i] = ("sbuf", [128, C], "uint8")
    SCRATCH["ll%d" % _i] = ("sbuf", [128, 32], "uint16")
    SCRATCH["al%d" % _i] = ("sbuf", [128, 18], "uint16")

SEMAPHORES = ["sv", "sa", "st", "sg", "left",
              "lx", "lu", "lv", "lp", "lk", "lm", "lw", "lws", "out"]
for _i in range(3):
    SEMAPHORES += ["rc%d" % _i, "rs%d" % _i, "rL%d" % _i, "aq_%d" % _i, "aL_%d" % _i]


def relays(core, partner, topo):
    may = [c for c in topo.cores_of(core) if c != core and topo.may_write(c, partner)]
    same = [c for c in may if topo.die(c) == topo.die(core)]
    other = [c for c in may if topo.die(c) != topo.die(core)]
    return [same[0], other[0]], same[0]


def bits(es):
    return sum(1 << e for e in es)


def place(a, y, e):
    odd, back = e % 2, e + 1 if e < 10 else e - 10
    if a == 0:
        return EVEN + 160 * odd + 16 * back + 7 if y == 0 else ODD + 16 * min(e, 17) + 15
    if a != 2:
        return EV4 + 40 * odd + 4 * back + 3 if y == 0 else OD4 + 40 * (1 - odd) + 4 * (back - odd) + 3
    return (EV4B if e < 10 else EV4) + 4 * back + 3 if y == 0 else OD4 + 4 * e + 3


def pieces(v):
    out, i = [], 0
    while i < len(v):
        s2, n, m = v[i + 1] - v[i], 2, 1
        while i + n < len(v) and v[i + n] - v[i + n - 1] == s2:
            n += 1
        s1 = v[i + 2] - v[i] if i + 3 < len(v) else 0
        while i + 2 * m + 1 < len(v) and (v[i + 2 * m], v[i + 2 * m + 1]) == (v[i] + m * s1, v[i] + m * s1 + s2):
            m += 1
        out.append((i, n, [[s2, n]], v[i]) if n >= 2 * m else (i, 2 * m, [[s1, m], [s2, 2]], v[i]))
        i += out[-1][1]
    return out


def relay_program(g, core, T, topo):
    home = [c for c in topo.cores_of(core) if T.rank_of(c) is not None]
    if not home:
        return
    home = home[0]
    left = 0
    for r in range(3):
        partner = T.cores[T.rank_of(home) ^ STEP[r]]
        data, lst = relays(home, partner, topo)
        rid, pid = topo.addr(partner, core) if core in data or core == lst else (0, 0)
        es = topo.engines(core, partner)
        if core in data:
            k = data.index(core)
            n_in = len(topo.engines(home, core)) // 2
            a, b = k * HALF, (k + 1) * HALF
            g.wait_ge(T.sem["rc%d" % r], n_in)
            g.remote_dma(T["aq%d" % r][:, a:b].bitcast(dt.uint8), T["aq%d" % r][:, a:b].bitcast(dt.uint8), T.sem["aq_%d" % r], T.sem.left, pid, rid, bits(es))
            g.wait_ge(T.sem["rs%d" % r], n_in)
            g.remote_dma(T["ap%d" % r][:, a:b], T["ap%d" % r][:, a:b], T.sem["aq_%d" % r], T.sem.left, pid, rid, bits(es))
            left += 2 * len(es)
        if core == lst:
            g.wait_ge(T.sem["rL%d" % r], len(topo.engines(home, core)))
            g.remote_dma(T["al%d" % r][:], T["al%d" % r][:], T.sem["aL_%d" % r], T.sem.left, pid, rid, bits(es))
            left += len(es)
    if left:
        g.wait_ge(T.sem.left, left)


def rank_program(g, core, T, topo):
    rank = T.rank_of(core)
    if rank is None:
        return relay_program(g, core, T, topo)
    A = AluOpType
    F = ActivationFunctionType
    queue = {"v": g.vector, "a": g.scalar, "t": g.tensor, "g": g, "s": g.sync}
    own = {"v": "sv", "a": "sa", "t": "st", "g": "sg"}
    known = {e: {} for e in queue}
    count, snap, wr, rd = {}, {}, {}, {}

    def need(e, deps):
        deps = [d for d in set(deps) if known[e].get(d[0], 0) < d[1]]
        deps.sort(key=lambda d: -sum(snap.get(d, {}).values()))
        for d in deps:
            if known[e].get(d[0], 0) >= d[1]:
                continue
            queue[e].wait_ge(T.sem[d[0]], d[1])
            for s, n in list(snap.get(d, {}).items()) + [d]:
                known[e][s] = max(known[e].get(s, 0), n)

    def before(e, reads, writes):
        deps = []
        for k in reads:
            deps += wr.get(k, [])
        for k in writes:
            deps += wr.get(k, []) + rd.get(k, [])
        need(e, deps)

    def after(reads, writes, d):
        for k in reads:
            rd[k] = [x for x in rd.get(k, []) if x[0] != d[0]] + [d]
        for k in writes:
            wr[k] = [d]
            rd[k] = []

    def op(e, reads, writes, call):
        before(e, reads, writes)
        s = own[e]
        count[s] = count.get(s, 0) + 1
        call().then_inc(T.sem[s], 1)
        d = (s, count[s])
        snap[d] = dict(known[e])
        snap[d][s] = count[s]
        after(reads, writes, d)

    def dma(e, sem, total, reads, writes, out, in_):
        before(e, reads, writes)
        queue[e].dma_start(out, in_).then_inc(T.sem[sem], 16)
        count[sem] = 16 * total
        d = (sem, 16 * total)
        m = snap.setdefault(d, {})
        for s, n in known[e].items():
            m[s] = max(m.get(s, 0), n)
        for k in reads:
            rd[k] = [x for x in rd.get(k, []) if x != d] + [d]
        for k in writes:
            wr[k] = [x for x in wr.get(k, []) if x == d] or [d]
            rd[k] = []

    def ts(reads, writes, out, in0, s1, op0, s2=None, op1=None):
        if op1 is None:
            op("v", reads, writes, lambda: g.vector.tensor_scalar(out, in0, s1, None, op0))
        else:
            op("v", reads, writes, lambda: g.vector.tensor_scalar(out, in0, s1, s2, op0, op1))

    def tt(reads, writes, out, in0, in1, o):
        op("v", reads, writes, lambda: g.vector.tensor_tensor(out, in0, in1, o))

    def cp(reads, writes, out, in_):
        op("v", reads, writes, lambda: g.vector.tensor_copy(out, in_))

    def act(reads, writes, out, in_, f=F.Copy, **kw):
        op("a", reads, writes, lambda: g.scalar.activation(out, in_, f, **kw))

    def mm(reads, bank, lhs, lhsp, q, p, a=0, b=C):
        op("t", reads, ["ps%d" % bank], lambda: g.tensor.matmul_mx(T["ps%d" % bank][:, 0:b - a], lhs, lhsp, T[q][:, a:b], T[p][:, a:b], True, True))

    def halves(reads, q, p, t):
        for h, (a, b) in enumerate(RUNS):
            quant([k + "ab"[h] for k in reads], [q + "ab"[h]], T[q][:, a:b], T[p][:, a:b], T[t][:, 4 * a:4 * b])

    def quant(reads, writes, q, p, t):
        op("v", reads, writes, lambda: g.vector.quantize_mx(q, p, t))

    def fill(key, ap, c):
        op("v", [], [key], lambda: g.vector.memset(ap, c))

    def turn(reads, writes, out, in_):
        op("v", reads, writes, lambda: g.vector.transpose(out, in_))

    def scan(reads, writes, out, d0, d1):
        op("v", reads, writes, lambda: g.vector.tensor_tensor_scan(out, d0, d1, 0.0, A.mult, A.add))

    def iota(key, out, pattern, base, step=0):
        op("g", [], [key], lambda: g.iota(out, pattern, base, step, allow_small_or_imprecise_dtypes=True))

    def plain(key, out, n, c):
        act(["ones"], [key], out, T.ones[:, 0:n], scale=c)

    dma("s", "lp", 1, [], ["pI"], T.pI[:], T.pg[:])
    dma("a", "lk", 1, [], ["kI"], T.kI[:], T.kg[:])
    dma("s", "lx", 1, [], ["xt"], T.xt[:], T.x[:])
    dma("a", "lm", 1, [], ["mI"], T.mI[:], T.mg[:])
    dma("s", "lu", 1, [], ["ut"], T.ut[:], T.u[:])
    dma("s", "lw", 1, [], ["wq"], T.wq[:].bitcast(dt.uint8), T.wc[:])
    dma("s", "lws", 1, [], ["wp"], T.wp[:], T.ws[:])
    dma("s", "lv", 1, [], ["vt"], T.vt[:], T.v[:])

    iota("pf", T.pf[:], [[0, 1]], 0, 1)
    iota("quart", T.quart[:], [[1, 72]], -36)
    iota("lor", T.lor[:], [[-1, 2], [1, 16]], 0)
    iota("ulf", T.ulf[:, 0:8], [[32, 4], [0, 2]], -16)
    iota("ulf2", T.ulf[:, 8:16], [[16, 8]], 0)
    iota("idr", T.idr[:], [[1, C]], -144)
    fill("half", T.half[:], 0.5)
    fill("of", T.of[:], 0)
    fill("ke", T.ke[:], 0.0)
    op("v", ["half"], ["pw"], lambda: g.vector.tensor_tensor_scan(T.pw[:], T.half[:], T.half[:], 256.0, A.mult, A.max))
    fill("ones", T.ones[:, 0:256], 1.0)
    ts(["pf", "pw"], ["bi"], T.bi[:], T.pw[:], T.pf[:], A.mult)
    fill("ones2", T.ones[:, 256:516], 1.0)
    op("g", ["ones", "ones2"], ["e0"], lambda: g.affine_select(T.e0[:], T.ones[:], [[1, 516]], A.is_equal, 0.0, -3, -4))
    op("g", ["ones", "ones2"], ["four"], lambda: g.affine_select(T.four[:], T.ones[:, 0:384], [[0, 96], [1, 4]], A.is_gt, 0.0, 0, 0))
    b = lambda i: T.bit[:, i:i + 1]
    nb = lambda i: T.nb[:, i:i + 1]
    sg = lambda i: T.sg[:, i:i + 1]
    cc = lambda j: T.cst[:, j:j + 1]
    ts(["bi"], ["bj"], T.bj[:, 0:7], T.bi[:, 0:7], 7, A.logical_shift_right, 1, A.bitwise_and)
    ts(["bi"], ["bj7"], T.bj[:, 7:8], T.bi[:, 7:8], 15, A.bitwise_and)
    fill("sg5", T.sg[:, 5:6], 1.0)
    cp(["bj"], ["bit"], T.bit[:, 0:7], T.bj[:, 0:7])
    ts(["bj"], ["nb"], T.nb[:, 0:7], T.bj[:, 0:7], -1.0, A.mult, 1.0, A.add)
    ts(["bj"], ["sg"], T.sg[:, 0:4], T.bj[:, 0:4], 2.0, A.mult, -1.0, A.add)
    cp(["bj7"], ["c16"], cc(16), T.bj[:, 7:8])
    ts(["bit"], ["c1"], cc(1), b(1), 0.25, A.mult, b(0), A.max)
    ts(["bit", "nb"], ["c0"], cc(0), b(0), 4.0, A.mult, nb(1), A.max)
    ts(["sg"], ["sg4"], sg(4), sg(2), sg(3), A.mult)
    ts(["lor", "c1"], ["sel8"], T.sel[:, 8:12], T.lor[:, 0:4], cc(1), A.mult)
    ts(["lor", "c16"], ["sel4"], T.sel[:, 4:8], T.lor[:, 1:8:2], cc(16), A.is_equal)
    ts(["sg", "sg4", "sg5", "nb"], ["sel12"], T.sel[:, 12:16], T.sg[:, 2:6], nb(0), A.mult)
    for i in range(4):
        ts(["quart", "c0", "sel8"], ["base%d" % i], T.base[:, i:C:4], T.quart[:], cc(0), A.mult, T.sel[:, 8 + i:9 + i], A.add)
        if i == 1:
            tt(["sel4", "sel12"], ["sel"], T.sel[:, 0:4], T.sel[:, 4:8], T.sel[:, 12:16], A.add)
    whole = ["sel"] + ["base%d" % i for i in range(4)]
    fill("ex", T.ex[:], 0.0)
    fill("hs0", T.hs[:, 31:880:48], 0.0)
    ts(whole, ["dg3"], T.dg3[:], T.base[:], T.sel[:, 3:4], A.mult)
    ts(whole, ["dg2"], T.dg2[:], T.base[:], T.sel[:, 2:3], A.mult)
    cp(["pI"], ["pls0"], T.pls0[:], T.pI[:])

    def line(key, x, s, c=None, part=slice(0, 128)):
        col = lambda v: T[v[1]][part, v[2]:v[2] + 1] if isinstance(v, tuple) else v
        kw = {} if c is None else {"bias": col(c)}
        act([v[0] for v in (x, s, c) if isinstance(v, tuple)], ["c%d" % key], T.cst[part, key:key + 1], col(x), F.Copy if c is None else F.Identity, scale=col(s), **kw)

    K = lambda j: ("c%d" % j, "cst", j)
    B = lambda j: ("bit", "bit", j)
    NB = lambda j: ("nb", "nb", j)
    SG = lambda j: ("sg", "sg", j)
    ONE = ("ones", "ones", 0)
    late, early = slice(0, 128), slice(0, 32)
    plain("tra", T.tr[:, 16:32], 16, 0.0)
    plain("trb", T.tr[:, 352:368], 16, 0.0)
    plain("c17", cc(17), 1, -1e-29)
    plain("c23", cc(23), 1, 352.0)
    plain("c24", cc(24), 1, 0.5)
    plain("gt1v", T.gt1[:, 0:ROW], ROW, 1.0)
    for i in range(2):
        plain("gg%da" % i, T["gg%d" % i][:, 16:32], 16, 0.0)
        plain("gg%db" % i, T["gg%d" % i][:, 192:208], 16, 0.0)
    plain("gt1v", T.gt1[:, 0:ROW:8], 2 * ENT, 0.0)
    plain("gt1s", T.gt1[:, 4:ROW:16], ENT, -1.0)
    plain("ysa", T.ys[:, 3:64:4], 16, 0.0)
    line(2, B(5), 1.0)
    line(26, B(0), -672.0, K(23))
    line(25, B(0), 320.0)
    line(2, NB(4), 1.0, part=early)
    line(32, SG(0), SG(2))
    line(33, NB(2), NB(3))
    line(34, NB(0), NB(1))
    line(31, B(3), NB(2))
    line(27, K(16), 32.0, K(25))
    line(3, K(2), -1.0, ONE)
    line(42, K(32), -0.5, K(24))
    line(29, K(33), -1.0, ONE)
    line(35, K(34), -1.0, ONE)
    line(40, K(31), NB(0))
    line(28, K(26), B(4), K(27))
    line(36, SG(0), 0.25)
    line(39, SG(1), 0.25)
    line(41, K(40), -2.0, ONE)
    act(whole, ["dg1"], T.dg1[:], T.base[:], scale=T.sel[:, 1:2])
    line(30, K(29), -1e-29)
    line(37, K(39), K(41))

    def power(r, n):
        src, dst = ["dg3", "y1", "y2"][n], ["y1", "y2", "y3"][n]
        tt([src, "pls%d" % r, "dg%d" % (2 - n)], [dst], T[dst][:], T[src][:].indirect(T["pls%d" % r][:]), T["dg%d" % (2 - n)][:], A.add)

    def starts(cut):
        if cut:
            cp(["y3", "k20"], ["tr1"], T.tr[:, 32:32 + 16 * cut], T.y3[:].indirect(T.k20[:, 0:cut]))
        act(["y3", "k20"], ["tr2"] if cut else ["tr1", "tr2"], T.tr[:, 32 + 16 * cut:352], T.y3[:].indirect(T.k20[:, cut:20]))

    def table(part):
        if part == 0:
            turn(["tr1", "tr2"], ["tabA"], T.tab[:, 0:320], T.tr[:, 32:352])
        else:
            turn(["tr1", "tr2", "tra", "trb"], ["tabB"], T.tab[:, 320:672], T.tr[:, 16:368])

    cp(["kI"], ["kf"], T.kf[:], T.kI[:])
    cp(["ulf2"], ["ull2"], T.ull[:, 16:24], T.ulf[:, 8:16])
    power(0, 0)
    for h in range(2):
        for y in range(2):
            c0 = 10 * (1 - h) + y
            n = len(range(c0, 18 if h == 0 else 10, 2))
            m0 = 2 * h + y
            act(["kf", "c2", "ke"], ["ke%d" % m0], T.ke[:, m0:m0 + 4 * n - 3:4], T.kf[:, c0:c0 + 2 * n - 1:2], scale=cc(2))
    act(["kf", "c3", "ke"], ["ko1"], T.ke[:, 21:40:2], T.kf[:, 0:10], scale=cc(3))
    act(["kf", "c3", "ke"], ["ko0"], T.ke[:, 20:35:2], T.kf[:, 10:18], scale=cc(3))
    ts(["nb"], ["c5"], cc(5), nb(0), nb(1), A.mult, nb(2), A.mult)
    ts(["nb"], ["c6"], cc(6), nb(3), nb(5), A.mult, nb(6), A.mult)
    ts(["nb", "bit"], ["c7"], cc(7), nb(0), nb(1), A.mult, b(2), A.mult)
    power(0, 1)
    line(15, B(3), 16.0, K(7))
    act(whole, ["dg0"], T.dg0[:], T.base[:], scale=T.sel[:, 0:1])
    line(8, K(5), -1.0, NB(0))
    line(10, K(6), -1.0, ONE)
    line(38, K(37), SG(0))
    line(13, K(29), K(35), part=late)
    line(9, K(7), -2.0, K(8))
    line(43, K(8), K(10))
    line(14, K(13), -1e-29, part=late)
    line(11, K(9), K(6), B(0))
    line(13, K(43), 1.0, part=early)
    line(14, K(43), -1e-29, K(11), early)
    quant(["xt"], ["q0a", "q0b"], T.q0[:], T.qp0[:], T.xt[:])
    tt(["ke0", "ke1", "ke2", "ke3", "ko0", "ko1"], ["ke"], T.ke[:, 0:20], T.ke[:, 0:20], T.ke[:, 20:40], A.add)
    ts(["ulf", "c15"], ["ull0"], T.ull[:, 0:2], T.ulf[:, 0:2], cc(15), A.add, 0.0, A.max)
    ts(["ulf", "c42"], ["ull0b"], T.ull[:, 2:8], T.ulf[:, 2:8], cc(42), A.add)
    quant(["ut"], ["uq", "up"], T.uq[:], T.up[:], T.ut[:])
    power(0, 2)
    cp(["ke"], ["k20"], T.k20[:], T.ke[:, 0:20])
    ts(["ulf", "c31"], ["ull1"], T.ull[:, 8:16], T.ulf[:, 0:8], cc(31), A.add, 16.0, A.add)

    def codes_of_u(i):
        cp(["uq", "ull0b", "ull%d" % i], ["u%dq" % i], T["u%dq" % i][:].bitcast(dt.uint32), T.uq[:].bitcast(dt.uint32).indirect(T.ull[:, 8 * i:8 * i + 8]))

    def scales_of_u(i):
        act(["up", "ull0b", "ull%d" % i], ["u%dp" % i], T["u%dp" % i][:], T.up[:].indirect(T.ull[:, 8 * i:8 * i + 8]))

    scales_of_u(0)
    codes_of_u(0)
    starts(4)
    ts(["lor", "c28"], ["tlo"], T.tlo[:], T.lor[:, 1:8:2], cc(28), A.add, 671.0, A.min)
    scales_of_u(1)

    def unit(b):
        quant(["e0"], ["eq%d" % b], T.eq[:, 128 * b:128 * b + 128], T.ep[:, 128 * b:128 * b + 128], T.e0[:, 3 - b:515 - b])

    def shared(src, lst, dst):
        cp(src[1] + [lst], [dst + "a"], T[dst][:, 0:160], T[src[0]][:].indirect(T[lst][:, 0:10]))
        act(src[1] + [lst], [dst + "b"], T[dst][:, 160:C], T[src[0]][:].indirect(T[lst][:, 10:18]))

    def spread(key, src):
        tt([key, "avg"], ["hd"], T.hd[:, 0:18], src, T.ex[:, 2:54:3], A.subtract)
        return lambda: ts(["hd", "c20", "ex"], ["hdl"], T.ex[:, 0:54:3], T.hd[:, 0:18], cc(20), A.mult)

    part = lambda name, b, a0=0, b0=C: T[name][:, C * b + a0:C * b + b0]
    ph, mh = T.hd[:, 18:36], T.hd[:, 36:54]

    ROUND = 12582912.0
    every = lambda k, c0=0, c1=ENT: [k + "_%d" % c for c in range(c0, c1, 2)]
    rows = []
    left = [0]
    for r in range(3):
        partner = T.cores[rank ^ STEP[r]]
        data, lst = relays(core, partner, topo)
        q, qp = "q%d" % r, "qp%d" % r
        both = [q + "a", q + "b"]
        need("g", wr[q + "a"] + wr[q + "b"])
        fc, fs = [], []
        for k, c in enumerate(data):
            es = topo.engines(core, c)
            es = es[k * len(es) // 2:(k + 1) * len(es) // 2]
            rid, pid = topo.addr(c, core)
            a0, b0 = k * HALF, (k + 1) * HALF
            fc.append(RemoteDMATransfer(dst_ids=[DstId(rid=rid, pnc=pid)], dma_engine_mask=bits(es), remote_sem=T.sem["rc%d" % r],
                                        src=T[q][:, a0:b0].bitcast(dt.uint8), dst=T["aq%d" % r][:, a0:b0].bitcast(dt.uint8)))
            fs.append(RemoteDMATransfer(dst_ids=[DstId(rid=rid, pnc=pid)], dma_engine_mask=bits(es), remote_sem=T.sem["rs%d" % r],
                                        src=T[qp][:, a0:b0], dst=T["ap%d" % r][:, a0:b0]))
            left[0] += 2 * len(es)
        g.remote_dma_fused(fc, local_sem=T.sem.left)
        g.remote_dma_fused(fs, local_sem=T.sem.left)
        if r == 0:
            for a in range(4):
                p0, p1 = 32 * a, 32 * a + 32
                if a == 1:
                    need("g", [("sg", count["sg"])])
                for k in range(2):
                    for i0, n, pattern, first in pieces([place(a, y, 16 * k + i) for y in range(2) for i in range(16)]):
                        rows.append("fr%d" % len(rows))
                        iota(rows[-1], T.fr[p0:p1, 32 * k + i0:32 * k + i0 + n], pattern, first)

        def own_f(b):
            mm(both + ["eq%d" % b], 3 + b, T.eq[:, 128 * b:128 * b + 128], T.ep[:, 128 * b:128 * b + 128], q, qp)

        def scores(i):
            if i == 2:
                return mm(both + ["u2q", "u2p"], 0, T.u2q[:], T.u2p[:], q, qp)
            for h, (a0, b0) in enumerate(RUNS):
                mm([both[h], "u1q", "u1p"], (2, 7)[h], T.u1q[:], T.u1p[:], q, qp, a0, b0)

        def keep_f(b):
            act(["ps%d" % (3 + b)], ["fo%d" % b], part("fo", b), T["ps%d" % (3 + b)][:, 0:C])

        for h, (a0, b0) in enumerate(RUNS):
            mm([both[h], "u0q", "u0p"], h, T.u0q[:], T.u0p[:], q, qp, a0, b0)
        if r:
            scores(1)
        for h, (a0, b0) in enumerate(RUNS):
            act(["ps%d" % h, "c13", "c14"], ["w" + "xy"[h]], T.w[:, a0:b0], T["ps%d" % h][:, 0:b0 - a0], F.Sign, scale=cc(13), bias=cc(14))
        if r:
            scores(2)
            for b_ in range(4):
                own_f(b_)

        def lists():
            ts(["tabA", "tabB", "tlo"], ["tl"], T.tl[:], T.tab[:].indirect(T.tlo[:]), BIAS, A.add)

        def ahead(n, c0=0, c1=ENT):
            out, src = T.gi[:, 64 * c0 + n:64 * c1:4], T.wa[:].indirect(T.tl[:, 16 * n + c0:16 * n + c1])
            if n < 2 or (n, c1) == (2, ENT):
                act(["wa0", "wa1", "tl", "c%d" % (36 + n)], every("gi%d" % n, c0, c1), out, src, scale=cc(36 + n))
            else:
                ts(["wa0", "wa1", "tl", "c38"], every("gi%d" % n, c0, c1), out, src, cc(38) if n == 2 else 0.25, A.mult)

        def summed(c0, c1):
            scan(["four"] + [k for n in range(4) for k in every("gi%d" % n, c0, c1)], every("ys", c0, c1),
                 T.ys[:, 64 + 64 * c0:64 + 64 * c1], T.four[:, 0:64 * (c1 - c0)], T.gi[:, 64 * c0:64 * c1])

        def turned(part):
            if part == 0:
                turn(every("ys"), ["ytA"], T.yt[:, 0:ROW], T.ys[:, 67:704:4])
            else:
                turn(every("ys") + ["ysa"], ["ytB"], T.yt[:, ROW:2 * ROW], T.ys[:, 3:640:4])

        def pack(h, k):
            name = ("te", "to")[h]
            tt(["tabA", "tabB"], [name + str(k)], T[name][late, k:84:4], T.tab[late, 16 * h + 4 * k:672:32], T.tab[late, 16 * h + 4 * k + 2:672:32], A.add)

        te, to = ["te%d" % k for k in range(4)], ["to%d" % k for k in range(4)]
        pads = lambda k: every(k) + [k + "a", k + "b"]
        first = [
            lambda: cp(["mI"], ["mls"], T.mls[:], T.mI[:]),
            lambda: ts(["pI"], ["ph"], ph, T.pI[:], 0.5, A.mult),
            lambda: ts(["lor", "c16"], ["d16a"], T.d16[:, 0:16], T.lor[:, 0:16], cc(16), A.not_equal),
            lambda: ts(["lor", "c16"], ["d16b"], T.d16[:, 16:32], T.lor[:, 16:32], cc(16), A.is_equal, 65535.0, A.mult),
            lambda: ts(["ones", "c16"], ["lane"], T.lane[:], T.ones[:, 0:18], cc(16), A.mult),
            lambda: tt(["d16a", "d16b"], ["d16"], T.d16[:, 32:48], T.d16[:, 0:16], T.d16[:, 16:32], A.add),
            lambda: ts(["c16"], ["c19"], cc(19), cc(16), 15.0, A.is_equal, 2.0 ** -16, A.max),
            lambda: ts(["c16"], ["c20"], cc(20), cc(16), 15.0, A.is_equal, 2.0 ** -32, A.max),
            lambda: turn(rows, ["ft"], T.ft[:], T.fr[:]),
            lambda: ts(["ft"], ["fin"], T.fin[:], T.ft[:, 0:64:32], RES - 1.0, A.min),
        ]

        def both_f(b):
            unit(b)
            own_f(b)

        P = lambda h, k: (lambda: pack(h, k))
        waits = {
            (0, 0): [lambda: ahead(3, 0, 4)], (0, 1): [lambda: ahead(3, 4, ENT)], (0, 2): [lambda: ahead(2, 0, 4)], (0, 3): [P(1, 2), lambda: summed(0, 4)],
            (1, 0): [lambda: summed(4, ENT)], (1, 1): [lambda: turned(0), P(1, 3)],
            (1, 2): [lambda: turn(pads("gg1"), ["gt1b"], T.gt1[:, ROW:352], T.gg1[:, 16:208])], (1, 3): [lambda: turned(1), P(0, 1)],
            (1, 4): [lambda: turn(pads("gg0"), ["gt0b"], T.gt0[:, ROW:C], T.gg0[:, 16:144]), P(0, 0)],
            (2, 0): [lambda: scan(["gt0b", "tabB"], ["oddB"], T.res[:, ODDB:ODDB + 128], T.gt0[:, ROW:C], T.tab[:, 320:2 * C:2]), P(0, 2)],
            (2, 1): [lambda: scan(["gt1b", "tabB"], ["evenB"], T.res[:, EVENB:EVENB + 176], T.gt1[:, 176:352], T.tab[:, 320:672:2])],
            (2, 2): [P(0, 3)],
        }
        behind = {0: [lambda: ahead(0), lambda: ahead(1), lambda: ahead(2, 4, ENT)]}
        signs = lambda: act(["ps0", "c17"], ["wg"], T.wg[:], T.ps0[:, 0:C], F.Sign, bias=cc(17))
        if r:
            behind.update({1: [signs, lambda: keep_f(0), lambda: keep_f(1)], 2: [lambda: keep_f(2), lambda: keep_f(3)], 3: []})
        else:
            behind.update({1: [lambda: scales_of_u(2), lambda: act(["idr", "pls0"], ["prow"], T.prow[:], T.idr[:].indirect(T.pls0[:]))],
                           2: [lambda: act(["prow", "mls"], ["mrow"], T.mrow[:], T.prow[:].indirect(T.mls[:])), signs],
                           3: [lambda: act(["d16", "lane"], ["own"], T.own[:], T.d16[:, 32:48].indirect(T.lane[:]))]})
            waits[2, 3] = waits[1, 4] + [waits[2, 0][0]]
            waits[2, 0] = [P(0, 2)]
            waits[1, 4] = [lambda: codes_of_u(2), lambda: scores(2)]
            for t, k, n in ((1, 1, 1), (1, 2, 1), (1, 3, 1), (2, 0, 2), (2, 1, 1), (2, 2, 2), (2, 3, 1)):
                waits[t, k] = waits.get((t, k), []) + n * [lambda: first.pop(0)()]
            waits[2, 4] = [lambda: both_f(0), lambda: both_f(1)]

        def wait(t, k):
            for call in waits.get((t, k), []):
                call()

        def pick(i, runs):
            for e, c0, c1 in runs:
                (cp if e == "v" else act)(["wx", "wy", "of"] + every("of%d" % i, c0, c1), every("gg%d" % i, c0, c1), T["gg%d" % i][:, 32 + 16 * c0:32 + 16 * c1],
                                          T.w[:].indirect(T.of[:, ENT * i + c0:ENT * i + c1]))

        if r == 0:
            codes_of_u(1)
            scores(1)
        table(0)
        tabA = T.tab[:, 0:320:2]
        table(1)
        scan(every("gt1") + ["gt1v", "gt1s", "tabA"], every("even"), T.res[:, EVEN:EVEN + ROW], T.gt1[:, 0:ROW], tabA)
        lists()
        ts(every("even") + ["of"], every("of0"), T.of[0:32, 0:ENT], T.res[0:32, EVEN + 7:EVEN + ROW:16], BIAS, A.add)
        pack(1, 0)
        pack(1, 1)
        for h, (a0, b0) in enumerate(RUNS):
            act(["ps%d" % (2, 7)[h], "c29", "c30"], ["wa%d" % h], T.wa[:, a0:b0], T["ps%d" % (2, 7)[h]][:, 0:b0 - a0], F.Sign, scale=cc(29), bias=cc(30))
        pick(0, (("v", 0, ENT),))
        for call in behind[0]:
            call()
        wait(0, 0)
        turn(every("gg0"), every("gt0"), T.gt0[:, 0:ROW], T.gg0[:, 32:192])
        wait(0, 1)
        scan(every("gt0") + ["tabA"], every("odd"), T.res[:, ODD:ODD + ROW], T.gt0[:, 0:ROW], tabA)
        wait(0, 2)
        ts(every("odd"), every("of1"), T.of[32:64, ENT:2 * ENT], T.res[0:32, ODD + 15:ODD + ROW:16], BIAS, A.add)
        wait(0, 3)
        for a in (1, 2):
            pick(1, TWO if a == 2 else (("s", 4, ENT), ("v", 0, 4)))
            for call in behind[a]:
                call()
            wait(a, 0)
            turn(every("gg1"), every("gt1"), T.gt1[:, 0:ROW], T.gg1[:, 32:192])
            wait(a, 1)
            scan(every("gt1") + ["ytA"], ["s1A"], T.s1[late, 0:ROW], T.gt1[late, 0:ROW], T.yt[late, 0:ROW])
            wait(a, 2)
            scan(["s1A"] + to, ["od4"], T.res[late, OD4:OD4 + 40], T.s1[late, 3:ROW:4], T.to[late, 0:40])
            wait(a, 3)
            ts(["od4"], every("of1"), T.of[32 * a + 32:32 * a + 64, ENT:2 * ENT], T.res[32 * a:32 * a + 32, OD4 + 3:OD4 + 40:4], BIAS, A.add)
            wait(a, 4)
        pick(1, TWO)
        for call in behind[3]:
            call()
        if r == 0:
            both_f(2)
        turn(every("gg1"), every("gt1"), T.gt1[:, 0:ROW], T.gg1[:, 32:192])
        turn(pads("gg1"), ["gt1b"], T.gt1[:, ROW:352], T.gg1[:, 16:208])
        if r == 0:
            first.pop(0)()
        scan(every("gt1") + ["ytA"], ["s1A"], T.s1[late, 0:ROW], T.gt1[late, 0:ROW], T.yt[late, 0:ROW])
        scan(["gt1b", "ytB"], ["s1B"], T.s1[late, ROW:2 * ROW], T.gt1[late, ROW:2 * ROW], T.yt[late, ROW:2 * ROW])
        scan(every("gt1") + te, ["ev4"], T.res[late, EV4:EV4 + 40], T.gt1[late, 1:ROW:4], T.te[late, 0:40])
        scan(["gt1b"] + te, ["ev4B"], T.res[late, EV4B:EV4B + 44], T.gt1[late, 177:352:4], T.te[late, 40:84])
        scan(["s1A", "s1B"] + to, ["od4"], T.res[late, OD4:RES], T.s1[late, 3:2 * ROW:4], T.to[late, 0:80])
        ll = "ll%d" % r
        ts(every("even") + every("odd") + ["evenB", "oddB", "ev4", "ev4B", "od4", "fin"], [ll], T[ll][:], T.res[:].indirect(T.fin[:]), BIAS, A.add)
        need("g", wr[ll])
        rid, pid = topo.addr(lst, core)
        es = topo.engines(core, lst)
        g.remote_dma(T["al%d" % r][:], T[ll][:, 0:18], T.sem["rL%d" % r], T.sem.left, pid, rid, bits(es))
        left[0] += len(es)
        pn = "pls%d" % (r + 1)
        if r == 0:
            both_f(3)
            scan(["own", "mrow"], ["ms"], T.ms[:], T.own[:], T.mrow[:])
        shared(("wg", ["wg"]), ll, "be")
        if r == 0:
            keep_f(0)
            ts(["ms", "c19"], ["mh"], mh, T.ms[:, 15:C:16], cc(19), A.mult, ROUND, A.add)
            ts(["mh"], ["mh"], mh, mh, BIAS - ROUND, A.add, 0.5, A.mult)
        shared(("be", ["bea", "beb"]), "mls", "bm")
        if r == 0:
            keep_f(1)
            tt(["mh", "ph", "ex"], ["avg"], T.ex[:, 2:54:3], ph, mh, A.add)
        scan(["own", "bea", "beb"], ["hs1"], T.hs[:, 2:2 + 3 * C:3], T.own[:], T.be[:])
        if r == 0:
            scaled = spread("pI", T.pI[:])
        scan(["own", "bma", "bmb"], ["hs2"], T.hs[:, 18:880:3], T.own[:], T.bm[:])
        if r == 0:
            scaled()
        scan(["hs0", "hs1", "hs2", "ex", "avg", "hdl"], ["pn"], T.pn[:], T.hs[:, 31:880:16], T.ex[:])
        cp(["pn"], [pn], T[pn][:], T.pn[:, 2:54:3])
        if r < 2:
            scaled = spread("pn", T.pn[:, 2:54:3])
        wr["aq"] = [("aq_%d" % r, sum(2 * len(topo.engines(c, core)) for c in relays(partner, core, topo)[0]))]
        wr["al"] = [("aL_%d" % r, len(topo.engines(relays(partner, core, topo)[1], core)))]
        count["aq_%d" % r], count["aL_%d" % r] = wr["aq"][0][1], wr["al"][0][1]
        for b_ in range(4):
            mm(["aq", "eq%d" % b_], (0, 1, 2, 7)[b_], T.eq[:, 128 * b_:128 * b_ + 128], T.ep[:, 128 * b_:128 * b_ + 128], "aq%d" % r, "ap%d" % r)
        for b_ in range(4):
            act(["ps%d" % (0, 1, 2, 7)[b_]], ["fp%d" % b_], part("fp", b_), T["ps%d" % (0, 1, 2, 7)[b_]][:, 0:C])
        if r == 0:
            keep_f(2)
            keep_f(3)
        if r < 2:
            power(r + 1, 0)
            scaled()
            power(r + 1, 1)
        else:
            quant(["vt"], ["vq"], T.vq[:], T.vp[:], T.vt[:])
            ts(["idr", ll], ["lo0"], T.lo[:, 0:C], T.idr[:].indirect(T[ll][:, 0:18]), BIAS, A.add)
            ts(["idr", pn], ["lo1"], T.lo[:, C:2 * C], T.idr[:].indirect(T[pn][:]), BIAS, A.add)
            dma("s", "out", 9, ["lo0", "lo1"], ["pl"], T.pl[:], T.lo[0:128:16, :])
        al, zt = T["al%d" % r], T.zt
        for b_ in (0, 2):
            (cp if b_ < 2 else act)(["fp%d" % b_, "al"], ["zt%da" % b_, "zt%db" % b_], zt[:, b_:4 * C:4], part("fp", b_).indirect(al[:]))
        for h, (a0, b0) in enumerate(RUNS):
            for b_ in (1, 3):
                (cp if b_ < 2 else act)(["fp%d" % b_, "al"], ["zt%d%s" % (b_, "ab"[h])], zt[:, 4 * a0 + b_:4 * b0:4], part("fp", b_).indirect(al[:, a0 // 16:b0 // 16]))
        halves(["zt%d" % b_ for b_ in range(4)], "zq", "zp", "zt")
        if r < 2:
            power(r + 1, 2)
        for h, (a0, b0) in enumerate(RUNS):
            mm(["zq" + "ab"[h], "wq", "wp"], 3 + 4 * h, T.wq[:, 0:128], T.wp[:, 0:128], "zq", "zp", a0, b0)
        for b_ in range(1, 4):
            mm(["zqa", "zqb", "wq", "wp"], 3 + b_, T.wq[:, 128 * b_:128 * b_ + 128], T.wp[:, 128 * b_:128 * b_ + 128], "zq", "zp")
        xn = T["xn%d" % r]

        def state(b_, h):
            a0, b0 = RUNS[h] if h < 2 else (0, C)
            hb = "hb%d" % b_
            tt([hb + "a", hb + "b", "fo%d" % b_, ll], ["xn%d%s" % (b_, k) for k in ("a", "b", "ab")[h]], xn[:, 4 * a0 + b_:4 * b0:4],
               part("hb", b_).indirect(T[ll][:, a0 // 16:b0 // 16]), part("fo", b_, a0, b0), A.add)

        for b_ in range(4):
            hb = "hb%d" % b_
            if b_ == 0:
                for h, (a0, b0) in enumerate(RUNS):
                    act(["ps%d" % (3 + 4 * h)], [hb + "ab"[h]], part("hb", b_, a0, b0), T["ps%d" % (3 + 4 * h)][:, 0:b0 - a0], scale=0.03125)
            else:
                act(["ps%d" % (3 + b_)], [hb + "a", hb + "b"], part("hb", b_), T["ps%d" % (3 + b_)][:, 0:C], scale=0.03125)
        if r < 2:
            for b_, h in ((0, 2), (1, 2), (2, 2), (3, 0), (3, 1)):
                state(b_, h)
            starts(0)
            halves(["xn%d" % b_ for b_ in range(4)], "q%d" % (r + 1), "qp%d" % (r + 1), "xn%d" % r)

    def store(h):
        a0, b0 = RUNS[h]
        quant(["xn%d%s" % (b_, "ab"[h]) for b_ in range(4)], ["q3%d" % h], T.q3[:, a0:b0], T.qp3[:, a0:b0], xn[:, 4 * a0:4 * b0])
        mm(["q3%d" % h, "vq"], h, T.vq[:], T.vp[:], "q3", "qp3", a0, b0)
        dma("s", "out", 9, ["q3%d" % h], ["oc%d" % h], T.oc[:, 4 * a0:4 * b0], T.q3[:, a0:b0].bitcast(dt.uint8))
        if h:
            for k in range(4):
                dma("s", "out", 9, ["q30", "q31"], ["osc%d" % k], T.osc[4 * k:4 * k + 4, :], T.qp3[32 * k:32 * k + 4, :])
        act(["ps%d" % h], ["yo%d" % h], T.yo[:, a0:b0], T["ps%d" % h][:, 0:b0 - a0])
        dma("a", "out", 9, ["yo%d" % h], ["y%d" % h], T.y[:, a0:b0], T.yo[:, a0:b0])

    for b_, h in ((0, 0), (0, 1), (1, 0), (2, 0), (3, 0), (1, 1)):
        state(b_, h)
    store(0)
    state(2, 1)
    state(3, 1)
    store(1)
    g.wait_ge(T.sem.left, left[0])
    for s in sorted(count):
        g.wait_ge(T.sem[s], count[s])
